import numpy as np, ml_dtypes
CORES = [113,118,241,246]
N = 4
BF = ml_dtypes.bfloat16
NB, T0, P, Q, RO, CM = 2048, 1024, 240, 3, 3, 3840
H = 3 * P // 2
def tally(fork):
    far = np.arange(P) % Q < Q - 1
    return np.add.reduce(np.where(fork, np.where(far, 1, 1 - Q), 0), axis=(1, 2))
def lanes(lv):
    T = lv.shape[2]; o = (np.arange(T) + T - H) % T
    return o[np.argsort(1 - lv[:, :, o], axis=2, kind="stable")[:, :, :P]]
def at(a, ix):
    return np.take_along_axis(a, ix[:, :, None, :], 3)
def play(x, rg, lv, z, w, kap, th, cap, rounds):
    x, rg, lv, z, w, kap, th, cap = [np.asarray(a).astype(np.int32) for a in (x, rg, lv, z, w, kap, th, cap)]
    bal = np.zeros(N, np.int64); far = np.arange(P) % Q < Q - 1; best = None
    for t in range(rounds):
        T = T0 + P * t
        ring = at(rg, lanes(lv))
        xl = at(x, ring.transpose(0, 1, 3, 2).reshape(N, 8, P * 16)).reshape(N, 8, 16, P, 16)
        k = np.argmax(np.add.reduce(np.minimum(xl, z[..., None]), axis=2), axis=3)
        y0 = np.abs(np.take_along_axis(xl, k[:, :, None, :, None], 4)[..., 0] - z)
        y = np.array(y0)
        for c in range(Q - 1): y[..., c::Q] = np.roll(y0[..., c::Q], 1 + (t + c) % (N - 1), axis=0)
        u = np.add.reduce(w[..., None] * y, axis=2) & 4095
        h = ((u * u >> 5)[..., None] + kap[:, :, None, :] * u[..., None]) & 4095
        tau = h * T >> 12; age = h & 15
        b = np.take_along_axis(rg.reshape(N, 8, 16 * T), (age * T + tau).reshape(N, 8, P * 16), 2)
        xb = at(x, b).reshape(N, 8, 16, P, 16)
        far_off = np.add.reduce(np.abs(xb - y[..., None]), axis=2)
        m = np.argmin(far_off, axis=3)[..., None]
        best = np.take_along_axis(far_off, m, 3)[..., 0]; fork = best < th[:, :, None]
        tm = np.take_along_axis(tau, m, 3)[..., 0]; am = np.take_along_axis(age, m, 3)[..., 0]
        xm = np.take_along_axis(xb, m[:, :, None, :, :], 4)[..., 0]
        tail = np.take_along_axis(at(rg, tm), np.minimum(am[:, :, None, :] + np.arange(15)[:, None], 15), 2)
        tail = np.where(fork[:, :, None], tail, ring[:, :, :15])
        new = np.broadcast_to((NB + P * t + np.arange(P)).astype(np.int32), (N, 8, 1, P))
        xn = np.where(fork[:, :, None], (xm + y) >> 1, y)
        bal = bal + tally(fork)
        off = fork & np.where(far, bal[:, None, None] > cap[:, :, None], -bal[:, None, None] > cap[:, :, None])
        x = np.concatenate([x, xn.astype(np.int32)], axis=3); rg = np.concatenate([rg, np.concatenate([new, tail], axis=2).astype(np.int32)], axis=3)
        lv = np.concatenate([lv, np.where(off, 0, 1).astype(np.int32)], axis=2)
    return x, rg, lv, best, bal
def parts(rng):
    x = (rng.integers(24, 65, (N, 8, 1, NB)) * rng.random((N, 8, 16, NB))).astype(np.int64)
    rg = rng.integers(0, NB, (N, 8, 16, T0))
    lv = (np.argsort(rng.random((N, 8, T0)), axis=2) < rng.integers(T0 // 2, T0, (N, 8, 1))).astype(np.int64)
    z = (rng.permutation(np.linspace(16, 64, N))[:, None, None, None] * rng.random((N, 8, 16, P))).astype(np.int64)
    return x, rg, lv, z, rng.integers(0, 4096, (N, 8, 16)), rng.integers(0, 2048, (N, 8, 16))
def tune(rng, x, rg, lv, z, w, kap):
    one = np.ones((N, 8), np.int64); best = play(x, rg, lv, z, w, kap, one, one, 1)[3]
    th = np.take_along_axis(np.sort(best, axis=2), rng.integers(P // 4, 3 * P // 4, (N, 8, 1)), 2)[:, :, 0] + rng.integers(0, 2, (N, 8))
    return np.clip(th, 1, 1008), best
def caps(rng, th, best):
    return np.minimum((1.5 * (np.abs(tally(best < th[:, :, None]))[:, None] + 8) * rng.random((N, 8))).astype(np.int64), CM)
def close(th, best):
    b = np.abs(tally(best < th[:, :, None]))[:, None]; d = np.array([0, -1, 1, 0, -1, -CM, CM, -1])
    return np.clip(b + d[(np.arange(8)[None, :] + 3 * np.arange(N)[:, None]) % 8], 0, CM)
def pack(x, rg, lv, z, w, kap, th, cap):
    i = lambda a, s: np.ascontiguousarray(np.reshape(a, s)).astype(np.int32)
    return {"x0": np.reshape(x, (N, 128, NB)).astype(np.float32).astype(BF), "rings": i(rg, (N, 128, T0)), "live": i(lv, (N, 8, T0)), "z": np.reshape(z, (N, 128, P)).astype(np.float32).astype(BF),
            "w": i(w, (N, 128, 1)), "kap": i(kap, (N, 128, 1)), "th": i(th, (N, 8, 1)), "cap": i(cap, (N, 8, 1))}
def setup_inputs(rng):
    p = parts(rng); th, best = tune(rng, *p)
    return pack(*p, th, caps(rng, th, best))
def setup_inputs_spread(rng):
    x = (np.exp2(6 * rng.random((N, 8, 1, NB))) * rng.random((N, 8, 16, NB))).astype(np.int64)
    z = (np.exp2(6 * rng.random((N, 8, 1, P))) * rng.random((N, 8, 16, P))).astype(np.int64)
    rg = (NB * rng.random((N, 8, 16, T0)) ** rng.integers(1, 5, (N, 8, 1, 1))).astype(np.int64); rg = np.minimum(rg, NB - 1)
    lv = (np.argsort(rng.random((N, 8, T0)), axis=2) < (P * np.exp2(1.3 * rng.random((N, 8, 1)))).astype(np.int64)).astype(np.int64)
    w = np.exp2(12 * rng.random((N, 8, 16))).astype(np.int64); kap = np.exp2(11 * rng.random((N, 8, 16))).astype(np.int64)
    w = np.minimum(w, 4095); kap = np.minimum(kap, 2047); th, best = tune(rng, x, rg, lv, z, w, kap)
    return pack(x, rg, lv, z, w, kap, th, caps(rng, th, best))
def setup_inputs_ends(rng):
    hi = rng.integers(0, 2, (N, 8)); hi[:, 0] = 0; hi[:, 7] = 1; up = rng.permutation(N) % 2 == 0; o = rng.permutation(8); far = np.arange(P) % Q < Q - 1
    x = 63 * rng.integers(0, 2, (N, 8, 16, NB)); x[..., 0] = 63 * (1 - hi)[..., None]; x[..., NB - 1] = 63 * hi[..., None]
    one = (NB - 1) * hi; nil = NB - 1 - one
    rg = np.where(rng.random((N, 8, 16, T0)) < 0.5, one[:, :, None, None], nil[:, :, None, None]); rg[:, :, 0] = one[:, :, None]
    rg[:, :, 0, 0] = np.where(up[:, None], one, nil); rg[:, :, 1, 0] = one
    lv = rng.integers(0, 2, (N, 8, T0)); lv[:, :, T0 - H:] = 1
    z = np.array(np.broadcast_to(np.where(far, 0, 63), (N, 8, 16, P)))
    kap = 2047 * rng.integers(0, 2, (N, 8, 16)); w = 4095 * rng.integers(0, 2, (N, 8, 16)); cap = np.full((N, 8), CM)
    th = np.where(rng.integers(0, 2, (N, 8)) == 0, 1, 1008); th[:, o[0]] = 1; th[:, o[1]] = 1008
    for g in o[5:]:
        r = 63 * rng.integers(0, 2, (N, 16, P)); r[:, 1] = 63 - r[:, 0]
        z[:, g] = np.where(far, r, 63); th[:, g] = np.where(up, 1008, 1); cap[:, g] = 0
    good = []
    for n in range(1, 17):
        u = (4095 * 63 * n) & 4095; hs = [((u * u >> 5) + c * u) & 4095 for c in (0, 2047)]
        if all((h & 15) > 0 and (h * T0 >> 12) > 0 and (h * (T0 + P * (RO - 1)) >> 12) < T0 for h in hs): good.append((n, hs))
    for q in range(N):
        for g in o[:5]:
            n, hs = good[0] if g == o[0] else good[int(rng.integers(0, len(good)))]
            w[q, g] = 4095 * (rng.permutation(16) < n)
            for t in range(RO):
                for h in hs: rg[q, g, h & 15, h * (T0 + P * t) >> 12] = one[q, g] if up[q] else nil[q, g]
    return pack(x, rg, lv, z, w, kap, th, cap)
def setup_inputs_corners(rng):
    x, rg, lv, z, w, kap = parts(rng); v = np.arange(T0)
    for q in range(N):
        for g in range(8):
            lv[q, g] = (v < P, v >= T0 - P, v >= 0, (v < P - 1) | (v == T0 - 1), rng.permutation(T0) < P, (v >= T0 - H - P) & (v < T0 - H), rng.permutation(T0) < 2 * P, v != T0 - H)[(g + q) % 8]
    rg[:, 0] = np.where(rng.random((N, 16, T0)) < 0.5, 0, NB - 1); rg[:, 1] = rg[:, 1, :1]; rg[:, 2] = rng.integers(NB - 16, NB, (N, 16, T0))
    x[:, 3, :, 1::2] = x[:, 3, :, ::2]; x[:, 4, :, ::3] = 0; x[:, 4, :, 1::3] = 63
    w[:, 5:7] = 0; x[:, 5:7, 0] = 63
    w[:, 5, 0] = 65; z[:, 5, 0] = rng.choice(np.array([0, 62, 63]), (N, P)); kap[:, 5, 15] = 2047
    w[:, 6, 0] = 1; z[:, 6, 0] = rng.choice(np.array([60, 61, 63]), (N, P)); kap[:, 6] = np.where(rng.random((N, 16)) < 0.5, 1365, kap[:, 6])
    w[:, 7] = 4095; kap[:, 7] = 2047 * rng.integers(0, 2, (N, 16))
    th, best = tune(rng, x, rg, lv, z, w, kap); m = rng.integers(0, 5, (N, 8)); th = np.where(m == 0, 1, np.where(m == 1, 1008, th))
    return pack(x, rg, lv, z, w, kap, th, close(th, best))
def setup_inputs_crowd(rng):
    x, rg, lv, z, w, kap = parts(rng); lv[:, ::2] = 1
    for g in (0, 1, 4, 5): rg[:, g] = rg[:, g, :, :1]; z[:, g] = z[:, g, :, :1]
    z[:, 1, :, 0] = 63 - z[:, 1, :, 0]; z[:, 5, :, P - 1] = 63 - z[:, 5, :, P - 1]
    w[:, 2:4] = 0; w[:, 3, 7] = 3; x[:, 3, 7] = 63; z[:, 3, 7] = 63; z[:, 3, 7, 1] = 0
    kap[:, 6] = kap[:, 6, :1]; kap[:, 7] = 0; rg[:, 7] = np.where(rng.random((N, 16, T0)) < 0.5, 0, NB - 1)
    w[:, 7] = 4095; x[:, 7, :, 0] = 63; x[:, 7, :, NB - 1] = 63; z[:, 7, :, ::5] = 0
    th, best = tune(rng, x, rg, lv, z, w, kap); th[:, 0] = np.max(best[:, 0], axis=1) + 1; th[:, 4] = np.min(best[:, 4], axis=1); th[:, 1] = np.max(best[:, 1], axis=1)
    th = np.clip(th, 1, 1008)
    return pack(x, rg, lv, z, w, kap, th, close(th, best))
def setup_inputs_balance(rng):
    x, rg, lv, z, w, kap = parts(rng); far = np.arange(P) % Q < Q - 1; own = np.flatnonzero(~far); own = own[own >= P // 2]
    o = rng.permutation(N); m = int(o[2]); j = int(np.flatnonzero(o == (m - 3) % N)[0]); o[j] = o[1]; o[1] = (m - 3) % N
    tall = np.isin(np.arange(N), np.concatenate([o[:1], o[3::2]]))
    up = np.repeat(tall[:, None], 8, axis=1); up[m] = rng.permutation(8) < 4
    k = int(rng.choice(np.flatnonzero(up[m]))); dn = np.flatnonzero(~up[m]); dn = np.concatenate([dn[dn == (k - 1) % 8], dn[dn != (k - 1) % 8]])
    one = rng.integers(0, NB, (N, 8)); nil = (one + 1) % NB; near = (one + 2) % NB; dim = (one + 3) % NB
    n = rng.integers(1, 4, N); n[o[:3]] = 0; n[o[3]] = 1
    th = np.where(rng.integers(0, 2, (N, 8)) == 0, 1, 1008); th[:, k] = np.where(tall, 1008, 1); th[o[1], k - 1] = 1008; th[o[1], dn[2]] = 1; th[m, dn[2]] = 1008
    d = np.array([0, -1, 1, 0, -1, 0, -1, CM])
    cap = np.clip((CM - (Q - 1) * n)[:, None] + d[(np.arange(8)[None, :] + 3 * np.arange(N)[:, None]) % 8], 0, CM)
    cap[m] = rng.choice(np.array([0, 1, 2, CM]), 8); cap[m, dn[:2]] = 0; cap[m, dn[2]] = 1; cap[m, k] = 0
    lv[:, :, T0 - H:] = 1; lv[:, :, 0] = 0; lv[m, dn[:2]] = np.arange(T0) >= T0 - P
    z = np.array(np.broadcast_to(np.where(far, 0, 63), (N, 8, 16, P)))
    a = rng.integers(1, 4096, (N, 8, 8)); w[..., ::2] = a; w[..., 1::2] = 4096 - a; w[..., 14:] = 0
    for q in range(N):
        c = rng.permutation(own)
        for g in range(8):
            x[q, g, :, one[q, g]] = 63; x[q, g, :, nil[q, g]] = 0; x[q, g, :, near[q, g]] = 63; x[q, g, 15, near[q, g]] = 62
            x[q, g, :, dim[q, g]] = 0; x[q, g, 15, dim[q, g]] = 1
            rg[q, g, 0] = one[q, g]; rg[q, g, 1, 0] = one[q, g]; rg[q, g, 0, 0] = one[q, g] if up[q, g] else nil[q, g]
            if not up[q, g] and th[q, g] == 1008: z[q, g, :, c[0]] = 0; z[q, g, 15, c[0]] = 1
        for v in c[1:1 + int(n[q])]: z[q, int(rng.integers(0, 8)), :, v] = 0
    s = (m - 1) % N; i = P // 2 + Q * int(rng.integers(0, P // 2 // Q))
    rg[s, k, 0, T0 - H + i] = near[s, k]
    s = (m - 5) % N; i = Q * int(rng.integers(0, P // 2 // Q))
    rg[s, dn[2], 0, T0 - P // 2 + i] = dim[s, dn[2]]
    return pack(x, rg, lv, z, w, kap, th, cap)
def check_inputs(d):
    bad = []
    for k, lo, hi in (("x0", 0, 63), ("rings", 0, NB - 1), ("live", 0, 1), ("z", 0, 63), ("w", 0, 4095), ("kap", 0, 2047), ("th", 1, 1008), ("cap", 0, CM)):
        a = np.asarray(d[k]).astype(np.float64)
        if not (np.min(a) >= lo and np.max(a) <= hi): bad.append("range of " + k)
        elif np.any(a != np.floor(a)): bad.append("whole numbers of " + k)
    if np.min(np.add.reduce(np.asarray(d["live"]).astype(np.int64), axis=2)) < P: bad.append("live timelines")
    return bad
def reference(x0, rings, live, z, w, kap, th, cap):
    x, rg, lv, best, bal = play(x0.astype(np.float32).reshape(N, 8, 16, NB), rings.reshape(N, 8, 16, T0), live.reshape(N, 8, T0), z.astype(np.float32).reshape(N, 8, 16, P),
                                w.reshape(N, 8, 16), kap.reshape(N, 8, 16), th.reshape(N, 8), cap.reshape(N, 8), RO)
    return {"yx": x[..., NB:].reshape(N, 128, P * RO).astype(np.float32).astype(BF), "yt": rg[..., T0:].reshape(N, 128, P * RO).astype(np.float32), "ya": lv[..., T0:].reshape(N, 8, P * RO).astype(np.float32)}

@@ -1,0 +1,698 @@
+from concourse.bass import DstId, RemoteDMATransfer
+from concourse.mybir import AluOpType as OP, AxisListType, ActivationFunctionType as AF
+
+NB, T0, P, RO = 2048, 1024, 240, 3
+TM = T0 + P * (RO - 1)
+W0, W1, W2 = 1024, 1264, 1864
+WIN = (W0, W1, W2)
+KOFF = -63 * 2 ** 18
+F, H, I, U, B = "float32", "float16", "int32", "uint16", "bfloat16"
+
+
+def _plan(T):
+    per = 1
+    while (per * 16 * T) % 4096: per *= 2
+    out = []
+    for rho in range(per):
+        vs = [((16 * rho + a) * T) >> 12 for a in range(16)]
+        for v in sorted(set(vs)):
+            a = [i for i in range(16) if vs[i] == v]
+            out.append((rho, v, a[0], a[-1] + 1))
+    return per, per * 16 * T // 4096, out
+
+
+PLANS = [_plan(T0 + P * t) for t in range(RO)]
+SPANS = []
+for _p in PLANS:
+    for _x in _p[2]:
+        if _x[2:] not in SPANS: SPANS.append(_x[2:])
+
+_S = dict(
+    X=(2768, B), Ri=(1024, I), Z=(240, B), Lt=(64, I), Lb=(64, B), Lz=(72, B), rho=(64, F), A1=(64, F), A2=(64, F), e0=(64, F), p0u=(64, U),
+    BIG=(2464, F), Rh=(TM, H), R4=(4 * TM, F), ZR=(3840, B), D2=(3840, B), A2w=(3840, B), D5=(3856, B), A5=(3840, B),
+    XHa=(4096, B), XHb=(4096, B), BHa=(256, U), BHb=(256, U), RES=(240, U), WT=(1200, F), RC=(240, H), NEW=(240, F), YT=(720, F),
+    YS=(480, B), YB0=(1280, B), YB1=(1280, B), YB2=(1280, B), EE=(240, B), LN=(480, B), E0=(128, B), LV=(48, F),
+    ONE=(128, B), ONEf=(128, F), BLK=(128, B), BLKt=(128, B), BLKf=(128, F), EW=(144, B), TRI=(128, B), UP=(128, B), TRS=(128, B), LT8=(128, B),
+    S7=(128, F), S15=(128, F), S15b=(128, B), ID=(128, B), IDf=(128, F), G8=(128, F), G8t=(128, F), BK1=(128, B), BK1f=(128, F), SH=(512, B), SHf=(128, F),
+    RS=(384, B), RK=(384, B), MK=(128 * len(SPANS), B), WH=(128, B), WL=(128, B),
+    Ki0=(2, I), Kp=(10, F), ZLi=(240, I), ZL=(240, U), T17=(18, F), GE=(18, F), LTt=(18, F), C16=(240, F), BGM=(160, B), RST=(240, F),
+    PA=(240, B), PBb=(240, B), MT=(240, F), PBS=(240, F), RK2=(240, F), PAY=(240, F), KT=(16, F), WK=(4, I), WKi=(4, I), WKf=(4, F),
+    TC=(4, I), TCf=(4, F), TH=(8, F), CN=(16, F), SL=(16, F), LC=(16, F), DU=(16, F), NFL=(16, F), LOC=(16, F), STR=(16, F),
+    s0=(16, F), s1=(16, F), s2=(16, F), s3=(16, F), s4=(16, F), i0=(16, I), NBu=(16, U), L0=(16, U),
+    SC=(240, F), SU=(240, F), k2=(16, I), k2b=(16, I), LY=(16, U), ui0=(16, I), ui=(16, I), uf=(16, F), sq=(16, I), qi=(16, I), qf=(16, F),
+    Hi=(240, I), Hj=(240, I), Hu=(240, U), AC=(160, F), K=(16, F), Ki=(16, I), nf=(16, F), fw=(48, B), kp=(16, I), mi=(16, I),
+    t1=(16, I), t2=(16, I), hh=(16, I), a12=(16, I), a3=(16, I), x1=(16, F), x2=(16, F), ix=(16, I), L1=(16, U), L2=(16, U), L3=(16, U),
+    g2=(16, F), g3=(16, F), y2=(16, F), y3=(16, F), z2=(16, F), z3=(16, F), w2=(16, F), dB=(4, F), cum=(16, B), e1=(16, F), e2=(16, F), e3=(16, F),
+    LP=(16, U), fT=(16, F), msk=(16, F), bas=(16, F), pf1=(16, F), pf2=(16, F), LF=(16, U), ONEs=(64, F),
+)
+HOME = {}
+_W = {}
+for _k, _v in _S.items():
+    if _v[0] <= 18 and _k not in ("WK", "TC"):
+        HOME[_k] = ("pool_" + _v[1], _W.get(_v[1], 0)); _W[_v[1]] = _W.get(_v[1], 0) + (_v[0] + 15) // 16 * 16
+SCRATCH = {k: ("sbuf", [128, v[0]], v[1]) for k, v in _S.items() if k not in HOME}
+for _k, _v in _W.items(): SCRATCH["pool_" + _k] = ("sbuf", [128, _v], _k)
+for _i in range(8): SCRATCH["pb%d" % _i] = ("psum", [128, 512], F)
+DMAS = ["d%d" % i for i in range(24)]
+SEMAPHORES = ["qV", "qS", "qP", "qG", "sent", "arr0", "arr1", "arr2"] + DMAS
+
+
+ORDER = []
+PACE = [dict(cy=1.0, pe=0.5, ga=1.5, sc=3.8, lat=70, dma=2000, rem=2500), dict(cy=0.9, pe=0.45, ga=1.15, sc=2.2, lat=50, dma=1700, rem=2000),
+        dict(cy=1.15, pe=0.7, ga=1.95, sc=5.5, lat=110, dma=2500, rem=3500)]
+TRIES, PASSES, JIT, MOVES = 60, 2, 2000.0, 6000
+XC = 24
+SPLIT2, SPLIT5 = (3, 4, 5), (0, 1, 5)
+GMASK = 31
+WV = 4
+BASE = (10.6, 33.5, 55.5)
+G2AT = (0.0, 1.0, 2.0, 3.0, 4.0, 5.6)
+G5AT = (10.0, 11.5, 13.0, 14.0, 15.0, 16.0)
+XHAT = ((-2.2, 0.7), (-4.0, 0.8), (-12.0, 1.0))
+
+
+def _times(ops, p):
+    out = []
+    for o in ops:
+        kind, n, r = o["cost"]
+        if kind == "dma": out.append((60.0, p["dma"] + n / 200.0))
+        elif kind == "rem": out.append((300.0, 300.0))
+        elif kind == "arr": out.append((0.0, p["rem"] - 300.0))
+        else:
+            d = {"e": max(64, n * r) * p["cy"], "ga": r + n * p["ga"] * p["cy"], "sc": r + n * p["sc"] * p["cy"], "pe": n * p["pe"], "g": r + 2 * n * p["cy"]}[kind]
+            out.append((d, d))
+    return out
+
+
+def _replay(ops, order, p):
+    if "tm" not in p: p["tm"] = _times(ops, p)
+    tm = p["tm"]; lat = p["lat"]; free = {}; end = [0.0] * len(ops)
+    for n in order:
+        o = ops[n]; q = o["q"]; t = free.get(q, 0.0)
+        for m in o["deps"]:
+            if end[m] > t: t = end[m]
+        if o["kind"] == "arr": t = end[n - 1] - lat
+        free[q] = t + tm[n][0]; end[n] = t + tm[n][1] + lat
+    return max(end)
+
+
+def _place(ops, tm, edges, key, back):
+    start = [0.0] * len(ops); busy = {}
+    for i in sorted(range(len(ops)), key=key):
+        t = 0.0
+        for m, lag in edges[i]: t = max(t, start[m] + lag)
+        d = max(tm[i][0], 1.0); row = busy.setdefault(ops[i]["q"], []); k = len(row)
+        while k and row[k - 1][1] > t: k -= 1
+        while k < len(row) and row[k][0] < t + d:
+            t = max(t, row[k][1]); k += 1
+        row.insert(k, (t, t + d)); start[i] = t
+    return start
+
+
+def _schedule(ops):
+    n = len(ops); best = None; x = 12345; tm0 = _times(ops, PACE[0])
+    for k in range(TRIES):
+        p = PACE[0]; tm = _times(ops, p); fw = [[] for _ in ops]; bw = [[] for _ in ops]
+        for i, o in enumerate(ops):
+            for m, lat in [(m, p["lat"]) for m in o["deps"]] + [(m, tm[m][0] - tm[m][1]) for m in o["soft"]]:
+                fw[i].append((m, tm[m][1] + lat)); bw[m].append((i, max(tm[i][0], 1.0) + tm[m][1] - max(tm[m][0], 1.0) + lat))
+        late = [0.0] * n
+        for i in range(n - 1, -1, -1):
+            x = (x * 1103515245 + 12345) % 2 ** 31
+            want = -1e6 if ops[i]["tag"] is None else -ops[i]["tag"] + (x / 2 ** 31 - 0.5) * JIT * (k > 0)
+            late[i] = max([want] + [late[j] + tm0[i][1] + 70.0 for j, lag in bw[i]]) + 1e-3
+        for _ in range(PASSES):
+            s = _place(ops, tm, fw, lambda i: (-late[i], i), False)
+            order = sorted(range(n), key=lambda i: (s[i], i))
+            v = sum(_replay(ops, order, q) / w for q, w in zip(PACE, (1.0, 0.8, 1.3)))
+            if best is None or v < best[0]: best = (v, order, s)
+            e = [s[i] + max(tm[i][0], 1.0) for i in range(n)]
+            r = _place(ops, tm, bw, lambda i: (-e[i], -i), True)
+            late = [r[i] + max(tm[i][0], 1.0) for i in range(n)]
+    p = PACE[0]; tm = _times(ops, p)
+    fw = [[(m, tm[m][1] + p["lat"]) for m in o["deps"]] + [(m, tm[m][0]) for m in o["soft"]] for o in ops]
+    movable = [i for i, o in enumerate(ops) if o["q"] != "P" and o["w"]]
+    cur = best
+    for k in range(MOVES):
+        u = []
+        for _ in range(4):
+            x = (x * 1103515245 + 12345) % 2 ** 31; u.append(x / 2 ** 31)
+        i = movable[int(u[0] * len(movable))]; d = (u[1] - 0.6) * 12000 * u[2]; key = list(cur[2])
+        for j in movable:
+            if j == i or (0 < j - i < 40 * u[3] and ops[j]["w"][0][0] == ops[i]["w"][0][0]): key[j] += d
+        if d < 0:
+            for j in range(n - 1, -1, -1):
+                for m, _ in fw[j]: key[m] = min(key[m], key[j])
+        else:
+            for j in range(n):
+                for m, _ in fw[j]: key[j] = max(key[j], key[m])
+        s = _place(ops, tm, fw, lambda j: (key[j], j), False)
+        order = sorted(range(n), key=lambda j: (s[j], j))
+        v = sum(_replay(ops, order, q) / w for q, w in zip(PACE, (1.0, 0.8, 1.3)))
+        if v < cur[0] + 150.0 * (1.0 - k / MOVES): cur = (v, order, s)
+        if v < best[0]: best = (v, order, s)
+    return best[1]
+
+
+def rank_program(g, core, T, topo):
+    rank = T.rank_of(core)
+    if rank is None:
+        return
+    N = len(T.cores)
+    Q = {"V": g.vector, "S": g.scalar, "P": g.tensor, "G": g, "Y": g.sync}
+    ops = []; hint = []
+
+    def at(t, us):
+        hint.append(1000.0 * (BASE[t] + us))
+
+    def reg(name, lo, hi, st=1):
+        return (name, (1 << hi) - (1 << lo) if st == 1 else sum(1 << c for c in range(lo, hi, st)))
+
+    def A(name, lo=0, hi=None, st=1, p=None):
+        psum = name.startswith("pb")
+        if hi is None: hi = lo + 1 if (lo or psum) else _S[name][0]
+        rows = slice(0, 128) if p is None else slice(p[0], p[1])
+        buf, o = HOME.get(name, (name, 0))
+        ap = T[buf][rows, o + lo:o + hi] if st == 1 else T[buf][rows, o + lo:o + hi:st]
+        return ("AP", ap, [reg(name, lo, hi, st)])
+
+    def C(name, c):
+        return A(name, c, c + 1)
+
+    def IN(win, off):
+        return ("AP", win[1].indirect(off[1]), win[2], off[2])
+
+    def isap(x):
+        return isinstance(x, tuple) and len(x) > 2 and x[0] == "AP"
+
+    def emit(q, fn, args, kw=None, kind="c", extra=None):
+        w, r = [], []
+        for n, a in enumerate(list(args) + list((kw or {}).values())):
+            if isap(a):
+                (w if n == 0 else r).extend(a[2])
+                if len(a) > 3: r.extend(a[3])
+        if extra: w, r = extra
+        aps = [a for a in args if isap(a)]
+        size = lambda a: bin(a[2][0][1]).count("1")
+        wide = lambda a: 4 if a[2][0][0].startswith("pb") or _S[a[2][0][0]][1] in (F, I) else 2
+        if kind == "r": cost = ("rem", 0, 0)
+        elif kind == "d": cost = ("dma", 128 * size(aps[0]) * wide(aps[0]) if aps else 60000, 0)
+        elif q == "P": cost = ("pe", max(64, size(aps[0])) * (4 if wide(aps[1]) == 4 else 1), 0)
+        elif q == "G": cost = ("g", size(aps[0]), 130 if fn == "iota" else 170)
+        elif len(aps[0]) > 3: cost = ("sc", size(aps[1]), 50)
+        elif len(aps) > 1 and len(aps[1]) > 3: cost = ("ga", size(aps[0]), 50 if q == "V" else 65)
+        elif fn == "tensor_tensor": cost = ("e", size(aps[0]), 1 if any(a[2][0][0].startswith("pb") for a in aps[1:]) else 2)
+        else: cost = ("e", size(aps[min(1, len(aps) - 1)]), 0.5 if q == "V" and all(wide(a) == 2 for a in aps[:2]) else 1)
+        tag = hint.pop() if hint else None
+        ops.append(dict(tag=tag, cost=cost, q=q, fn=fn, a=[x[1] if isap(x) else x for x in args], k={n: (x[1] if isap(x) else x) for n, x in (kw or {}).items()}, w=w, r=r, kind=kind))
+
+    cp = lambda o, i: emit("V", "tensor_copy", [o, i])
+    tt = lambda o, a, b, op: emit("V", "tensor_tensor", [o, a, b, op])
+    ms = lambda o, c: emit("V", "memset", [o, c])
+
+    def ts(o, a, s1, op0, s2=None, op1=None):
+        emit("V", "tensor_scalar", [o, a, s1, s2, op0] + ([] if s2 is None else [op1]))
+
+    def act(o, i, f, **k):
+        emit("S", "activation", [o, i, f], k)
+
+    mm = lambda o, l, r, s, e: emit("P", "matmul", [o, l, r, s, e])
+    scan = lambda o, d0, d1, o0, o1: emit("V", "tensor_tensor_scan", [o, d0, d1, 0.0, o0, o1])
+
+    def iota(o, pat, base=0, cm=0):
+        emit("G", "iota", [o, pat, base, cm], None if _S[o[2][0][0]][1] == I else {"allow_small_or_imprecise_dtypes": True})
+
+    sel = lambda o, i, pat, op, base, cm, fill=0.0: emit("G", "affine_select", [o, i, pat, op, fill, base, cm])
+
+    def load(q, o, src):
+        emit(q, "dma_start", [o, src], kind="d")
+        ops[-1]["cost"] = ("dma", ops[-1]["cost"][1] + max([0] + [x["cost"][1] for x in ops[:-1]]), 0)
+
+    def store(q, dst, i):
+        emit(q, "dma_start", [dst, i[1]], kind="d", extra=([], i[2]))
+
+    Kp, P80, R0c, R1c, Rm, P15 = [C("Kp", j) for j in range(6)]
+    EQ, GEQ, GT, NE = OP.is_equal, OP.is_ge, OP.is_gt, OP.not_equal
+    ADD, SUB, MUL, MIN, AND, SHR = OP.add, OP.subtract, OP.mult, OP.min, OP.bitwise_and, OP.arith_shift_right
+    YB = lambda t: "YB%d" % t
+    XH = lambda t: "XHb" if t % 2 else "XHa"
+    BH = lambda t: "BHb" if t % 2 else "BHa"
+
+    for x in range(2):
+        for b in range(2):
+            load("Y" if b else "S", A("Lt", 32 * b + 16 * x, 32 * b + 16 * x + 16), T.live[x::2, 512 * b:512 * b + 512])
+    load("S", A("Z"), T.z[:])
+    load("Y", A("Ri"), T.rings[:])
+    load("Y", A("X", 0, NB), T.x0[:])
+    load("Y", C("WK", 0), T.w[:]); load("Y", C("WK", 1), T.kap[:])
+    load("Y", A("TC", 0, 1, p=(0, 8)), T.th[:]); load("Y", A("TC", 1, 2, p=(0, 8)), T.cap[:])
+
+    ms(A("ONE"), 1.0); ms(A("ONEf"), 1.0); ms(A("Lz", 0, 8), 0.0); ms(A("EW"), 0.0); ms(A("ONEs"), 1.0); ms(A("D5", 3840, 3856), 0.0)
+    iota(C("Ki0", 0), [[0, 1]], 0, 1)
+    iota(A("ZLi"), [[1, 3], [3, 80]])
+    iota(A("A1"), [[16, 64]])
+    sel(A("BLKt"), A("ONE"), [[-16, 8], [0, 16]], GEQ, 0, 1)
+    sel(A("BLK"), A("BLKt"), [[16, 8], [0, 16]], GEQ, 15, -1)
+    sel(A("TRI"), A("BLK"), [[1, 128]], GEQ, 0, -1)
+    sel(A("UP"), A("BLK"), [[-1, 128]], GT, 0, 1)
+    ts(C("Ki0", 1), C("Ki0", 0), 15, AND)
+    cp(Kp, C("Ki0", 1))
+    cp(A("ZL"), A("ZLi"))
+    ts(A("SL"), A("A1", 0, 16), Kp, ADD)
+    ts(A("A2"), A("A1"), Kp, ADD, -1.0, MUL)
+    ts(A("A1"), A("A1"), Kp, ADD, -1024.0, ADD)
+    ts(A("A2"), A("A2"), 1023.0, ADD)
+    ts(P80, Kp, 80.0, MUL); ts(R0c, Kp, 0.0, EQ); ts(Rm, Kp, 0.0, NE, -1024.0, MUL); ts(P15, Kp, 15.0, MUL)
+    sel(A("ID"), A("ONE"), [[-1, 128]], EQ, 0, 1)
+    iota(A("T17"), [[1, 18]])
+    sel(A("S7"), A("ONEf"), [[-16, 8], [0, 16]], EQ, -7, 1)
+    sel(A("S15"), A("ONEf"), [[-16, 8], [0, 16]], EQ, -15, 1)
+    ts(A("EW", 15, 143, 16), A("BLK", 0, 128, 16), 32768.0, MUL)
+
+    def zrep(c0, c1):
+        act(A("ZR", 16 * c0, 16 * c1), IN(A("Z"), A("ZL", c0, c1)), AF.Copy)
+
+    def mask(j):
+        lo, hi = SPANS[j]
+        m = A("MK", 128 * j, 128 * j + 128)
+        if j < GMASK:
+            ts(m, A("ID"), C("GE", lo), MUL, C("LTt", hi), MUL)
+        elif lo == 0 or hi == 16:
+            sel(m, A("ID"), [[0, 8], [1 if lo else -1, 16]], GEQ, -lo if lo else hi - 1, 0)
+        else:
+            sel(A("BLKt"), A("ID"), [[0, 8], [1, 16]], GEQ, -lo, 0)
+            sel(m, A("BLKt"), [[0, 8], [-1, 16]], GEQ, hi - 1, 0)
+
+    def bh(t, n0, n1):
+        per, stp, plan = PLANS[t]
+        for j, (rho, v, lo, hi) in enumerate(plan):
+            k = SPANS.index((lo, hi))
+            mm(A("pb5", rho + per * n0, rho + per * (n1 - 1) + 1, per), A("MK", 128 * k, 128 * k + 128),
+               A("Rh", v + stp * n0, v + stp * (n1 - 1) + 1, stp), lo == 0, hi == 16)
+
+    def bhc(t, c0, c1):
+        ts(A(BH(t), c0, c1), A("pb5", c0, c1), 1024.0, ADD)
+
+    def xh(t, c0, c1, nb):
+        for c in range(c0, c1, XC):
+            d = min(c + XC, c1)
+            at(t, XHAT[t][0] + XHAT[t][1] * c / 16)
+            act(A(XH(t), 16 * c, 16 * d), IN(A("X", 0, nb), A(BH(t), c, d)), AF.Copy)
+
+    def r4(j, v0, v1, bank):
+        if j == 0:
+            mm(A(bank, 0, v1 - v0), A("ID"), A("Rh", v0, v1), True, True)
+        else:
+            mm(A(bank, 0, v1 - v0), A("RS", 128 * j - 128, 128 * j), A("Rh", v0, v1), True, False)
+            mm(A(bank, 0, v1 - v0), A("RK", 128 * j - 128, 128 * j), A("Rh", v0, v1), False, True)
+        at((v1 - T0) // P, 10.0 + 2 * j + v0 % 1024 / 512)
+        act(A("R4", TM * j + v0, TM * j + v1), A(bank, 0, v1 - v0), AF.Copy)
+
+    zrep(0, 40); zrep(40, 80); zrep(80, 160)
+    cp(A("Lb"), A("Lt"))
+    emit("V", "transpose", [A("Lz", 8, 72), A("Lb")])
+    mm(A("pb2", 0, 64), A("TRI"), A("Lz", 8, 72), True, False)
+    mm(A("pb2", 0, 64), A("UP"), A("Lz", 7, 71), False, True)
+    tt(A("e0"), A("A1"), A("Lz", 8, 72), MUL)
+    tt(A("e0"), A("e0"), A("A2"), ADD)
+    scan(A("rho"), A("ONEs"), A("pb2", 0, 64), MUL, ADD)
+    tt(A("e0"), A("e0"), A("rho"), ADD)
+    cp(A("p0u"), A("e0"))
+    mm(A("pb2", 0, 2), A("S7"), A("rho", 41, 57, 15), True, True)
+    mm(A("pb2", 2, 3), A("S15"), C("rho", 63), True, True)
+    ts(A("GE"), A("T17"), Kp, OP.is_le); ts(A("LTt"), A("T17"), Kp, GT)
+    for j in range(4): mask(j)
+    cp(A("CN", 0, 3), A("pb2", 0, 3))
+    ts(A("s0", 0, 15), A("SL", 0, 15), C("CN", 0), ADD)
+    ts(A("s1", 0, 15), A("s0", 0, 15), C("CN", 2), GEQ, C("CN", 2), MUL)
+    tt(A("s0", 0, 15), A("s0", 0, 15), A("s1", 0, 15), SUB)
+    cp(A("L0", 0, 15), A("s0", 0, 15))
+    ts(A("Rh", 0, T0), A("Ri"), -1024.0, ADD)
+    cp(IN(A("BIG", 0, T0), A("p0u")), A("Ri"))
+    cp(A("BIG", W0, W0 + P), IN(A("BIG", 0, T0), A("L0", 0, 15)))
+    bh(0, 0, 256)
+    zrep(160, 240)
+    iota(A("C16"), [[0, 15], [1, 16]])
+    iota(A("PA"), [[0, 3], [1, 80]])
+    iota(A("PBb"), [[1280, 3], [0, 80]])
+    iota(A("MT", 0, 80), [[1, 16], [0, 5]]); iota(A("MT", 80, 240), [[1, 16], [0, 10]])
+    iota(A("PBS", 0, 80), [[2048, 16], [0, 5]], KOFF); iota(A("PBS", 80, 240), [[2048, 16], [0, 10]], KOFF)
+    sel(A("G8t", p=(0, 8)), A("ONEf", p=(0, 8)), [[1, 128]], GEQ, 0, -16)
+    sel(A("G8", p=(0, 8)), A("G8t", p=(0, 8)), [[-1, 128]], GEQ, 15, 16)
+    sel(A("IDf"), A("ONEf"), [[-1, 128]], EQ, 0, 1)
+    iota(A("LC", 0, 15), [[-1, 15]], 599); iota(A("NFL", 0, 15), [[1, 3], [3, 5]], 960)
+    sel(A("S15b"), A("ONE"), [[-16, 8], [0, 16]], EQ, -15, 1)
+    for j in (1, 2, 3):
+        sel(A("RS", 128 * j - 128, 128 * j), A("BLK"), [[-1, 128]], EQ, -4 * j, 1)
+        sel(A("RK", 128 * j - 128, 128 * j), A("S15b"), [[0, 8], [1, 16]], GEQ, 4 * j - 16, 0)
+
+    def late_consts():
+        sel(A("TRS"), A("BLK"), [[1, 128]], GT, 0, -1)
+        sel(A("LT8"), A("BLK"), [[16, 8], [0, 16]], GEQ, 7, -1)
+        sel(A("BK1"), A("BLK"), [[0, 8], [1, 16]], GT, 0, 0)
+        sel(A("BK1f"), A("BLKf"), [[0, 8], [1, 16]], GT, 0, 0)
+        sel(A("SHf"), A("BK1f"), [[-1, 128]], EQ, 1, 1)
+        for j in range(4):
+            sel(A("SH", 128 * j, 128 * j + 128), A("BK1"), [[-1, 128]], EQ, 1 - j, 1)
+            for k in range(17 - j, 16):
+                col = A("SH", 128 * j + k, 128 * j + 128, 16)
+                sel(col, col, [[-16, 8]], NE, -15, 1, 1.0)
+        for j in range(3): iota(A("R4", TM * j + T0, TM * j + TM), [[0, TM - T0]])
+        iota(A("LN", P, 2 * P), [[1, P]])
+        iota(A("LN", 0, P), [[1, 3], [3, 5], [15, 16]])
+        iota(A("BIG", W1 + P, W2), [[0, W2 - W1 - P]])
+        ts(A("E0"), A("ID"), R0c, MUL)
+
+    def tables_a():
+        iota(A("RK2"), [[0, P]], 2 ** 24 - 1)
+        sel(A("RST"), A("RK2"), [[0, 15], [1, 16]], EQ, 0, 0)
+        ts(A("BGM"), A("C16", 0, 160), Kp, NE, 2.0 ** 23, MUL)
+        ts(C("WKi", 0), C("WK", 0), 4032, AND); ts(C("WKi", 1), C("WK", 0), 63, AND)
+        cp(C("WKf", 2), C("WK", 1))
+        cp(A("WKf", 0, 2), A("WKi", 0, 2))
+        ts(A("WH"), A("BLK"), C("WKf", 0), MUL); ts(A("WL"), A("BLK"), C("WKf", 1), MUL)
+
+    def tables_b():
+        cp(A("BLKf"), A("BLK"))
+        ts(A("RK2"), A("MT"), Kp, EQ, C("WKf", 2), MUL)
+        cp(A("TCf", 0, 2, p=(0, 8)), A("TC", 0, 2, p=(0, 8)))
+        mm(A("pb6", 0, 240), A("BLKf"), A("RK2"), True, True)
+        mm(A("pb6", 240, 242), A("G8", p=(0, 8)), A("TCf", 0, 2, p=(0, 8)), True, True)
+
+    def tables_c():
+        cp(A("KT"), A("pb6", 0, 80, 5))
+        tt(A("PAY"), A("pb6", 0, 240), A("PBS"), ADD)
+        ts(C("TH", 0), A("pb6", 240, 241), 32768.0, MUL, float(KOFF), ADD)
+        ts(C("TH", 4), C("TH", 0), -1.0, MUL, 1.0, ADD); ts(C("TH", 3), C("TH", 4), 8192.0, MUL)
+        cp(C("TH", 1), A("pb6", 241, 242)); ts(C("TH", 2), A("pb6", 241, 242), -1.0, MUL)
+
+    def tables_d():
+        S15 = lambda n: A(n, 0, 15)
+        ts(A("LOC", 0, 10), A("SL", 0, 10), 1280.0, ADD); ts(A("LOC", 10, 15), A("SL", 10, 15), -160.0, ADD)
+        ms(A("STR", 0, 10), 160.0); ms(A("STR", 10, 15), 80.0)
+        ts(S15("i0"), S15("SL"), 1.0 / 15, MUL, -0.47, ADD)
+        ts(S15("DU"), S15("LC"), P15, SUB)
+        act(S15("NFL"), S15("NFL"), AF.Identity, bias=P15)
+        ts(S15("s1"), S15("i0"), -15.0, MUL); cp(S15("s4"), S15("i0"))
+        tt(S15("s1"), S15("s1"), S15("SL"), ADD)
+        ts(S15("i0"), S15("s1"), 1.0 / 3, MUL, -0.34, ADD)
+        ts(S15("s1"), S15("s1"), 80.0, MUL)
+        ts(S15("s2"), S15("i0"), -224.0, MUL)
+        tt(S15("s1"), S15("s1"), S15("s4"), ADD)
+        tt(S15("s1"), S15("s1"), S15("s2"), ADD)
+        cp(S15("NBu"), S15("s1"))
+
+    def prep(t):
+        S15 = lambda n: A(n, 0, 15)
+        n1, a0, q0 = C("CN", 3 + 3 * t), C("CN", 4 + 3 * t), C("CN", 5 + 3 * t)
+        if t == 0:
+            tt(n1, C("CN", 2), C("CN", 1), SUB); a0, q0 = C("CN", 1), C("CN", 2)
+        else:
+            tt(n1, C("CN", 10), C("CN", 11), SUB)
+            ts(a0, C("CN", 11), C("CN", 3), ADD, float(W1), ADD); ts(q0, C("CN", 10), C("CN", 3), ADD, float(W1), ADD)
+        act(S15("bas"), S15("SL"), AF.Identity, bias=a0)
+        ts(S15("msk"), S15("SL"), n1, GEQ)
+        act(S15("s3"), S15("msk"), AF.Identity, scale=q0)
+        act(C("fT", 0), n1, AF.Identity, bias=1023.0)
+        tt(S15("bas"), S15("bas"), S15("s3"), SUB)
+
+    def res(t):
+        for c in range(3): cp(A("RES", 80 * c, 80 * c + 80), A("BIG", WIN[t] + c, WIN[t] + P, 3))
+
+    def keep(t):
+        mm(A("pb6", 0, P), A("E0"), A("LN", P, 2 * P), True, False)
+        mm(A("pb6", 0, P), A("SHf"), A("BIG", WIN[t], WIN[t] + P), False, True)
+        act(A("WT", 960, 1200), A("pb6", 0, P), AF.Identity, bias=Rm)
+        ts(C("Kp", 6 + t), R0c, float(NB + P * t - 1024), MUL, 1024.0, ADD)
+
+    def g2(t, ch):
+        lo, hi = 640 * ch, 640 * ch + 640
+        step = 320 if ch in SPLIT2 else 640
+        for a in range(lo, hi, step):
+            at(t, G2AT[ch] + (a - lo) / 640)
+            tt(A("D2", a, a + step), IN(A("X", 0, NB + P * t), A("RES", a // 16, (a + step) // 16)), A("ZR", a, a + step), SUB)
+            act(A("A2w", a, a + step), A("D2", a, a + step), AF.Relu, scale=-0.125)
+        c = ch // 2; bank, o = ("pb0", 80 * c) if c < 2 else ("pb1", 0)
+        if ch % 2 == 0:
+            mm(A(bank, o, o + 80), A("ID"), A("PA", 0, 80), True, False)
+            if c: mm(A(bank, o, o + 80), A("ID"), A("PBb", 80 * c, 80 * c + 80), False, False)
+        for p in range(8 * (ch % 2), 8 * (ch % 2) + 8):
+            mm(A(bank, o, o + 80), A("EW", 15 - p, 143 - p), A("A2w", 1280 * c + 80 * p, 1280 * c + 80 * p + 80), False, p == 15)
+
+    def pick(t, own):
+        n, c0, bank = (80, 10, "pb1") if own else (160, 0, "pb0")
+        c1 = c0 + n // 16
+        scan(A("SC", 16 * c0, 16 * c1), A("RST", 0, n), A(bank, 0, n), ADD, MIN)
+        cp(A("k2", c0, c1), A("SC", 16 * c0 + 15, 16 * c1, 16))
+        ts(A("k2b", c0, c1), A("k2", c0, c1), 4095, AND)
+        ts(A("LY", c0, c1), A("k2b", c0, c1), P80, ADD)
+        act(A(YB(t), 640, 720) if own else A("YS", 160 * t, 160 * t + 160), IN(A("D2", 0, 3840 if own else 2560), A("LY", c0, c1)), AF.Abs)
+
+    def send(t):
+        tr = []
+        dst = [T.cores[(rank + 1 + (t + c) % (N - 1)) % N] for c in range(2)]
+        eng = [e for e in topo.engines(core, dst[0]) if e in topo.engines(core, dst[1])]
+        far = [e for e in eng if all(e in topo.engines(core, d) for d in T.cores if d != core)]
+        half = len(far) // 2
+        for c in range(2):
+            rid, pid = topo.addr(dst[c], core)
+            tr.append(RemoteDMATransfer(dst_ids=[DstId(rid=rid, pnc=pid)], dma_engine_mask=sum(1 << e for e in far[half * c:half * c + half]),
+                                        remote_sem=T.sem["arr%d" % t], src=T["YS"][:, 160 * t + 80 * c:160 * t + 80 * c + 80], dst=T[YB(t)][:, 80 * c:80 * c + 80]))
+        at(t, 5.9)
+        emit("G", "remote_dma_fused", [tr], {"local_sem": T.sem.sent}, kind="r", extra=([], [reg("YS", 160 * t, 160 * t + 160)]))
+        ops.append(dict(tag=None, cost=("arr", 0, 0), kind="arr", q="R%d" % t, w=[reg(YB(t), 0, 160)], r=[], n=2 * half))
+
+    def rep(t, own):
+        o, n = (640, 80) if own else (0, 160)
+        while n < 640:
+            act(A(YB(t), o + n, o + 2 * n), A(YB(t), o, o + n), AF.Copy); n *= 2
+
+    def upe(t, own):
+        o, n = (640, 80) if own else (0, 160)
+        mm(A("pb2", 0, n), A("ID"), A("BGM", 0, n), True, False)
+        mm(A("pb2", 0, n), A("WH"), A(YB(t), o, o + n), False, False)
+        mm(A("pb2", 0, n), A("WL"), A(YB(t), o, o + n), False, True)
+
+    def u1(own):
+        n, c0 = (80, 10) if own else (160, 0); c1 = c0 + n // 16
+        scan(A("SU", 16 * c0, 16 * c1), A("RST", 0, n), A("pb2", 0, n), ADD, MIN)
+        cp(A("ui0", c0, c1), A("SU", 16 * c0 + 15, 16 * c1, 16))
+        ts(A("ui", c0, c1), A("ui0", c0, c1), 4095, AND)
+
+    def u2(own):
+        n, c0, h0 = (80, 10, 0) if own else (160, 0, 80); k = n // 16; c1 = c0 + k
+        tt(A("sq", c0, c1), A("ui", c0, c1), A("ui", c0, c1), MUL)
+        cp(A("uf", c0, c1), A("ui", c0, c1))
+        ts(A("qi", c0, c1), A("sq", c0, c1), 5, SHR)
+        cp(A("qf", c0, c1), A("qi", c0, c1))
+        for c in range(k): ts(A("Hi", h0 + c, h0 + n, k), A("KT"), C("uf", c0 + c), MUL, C("qf", c0 + c), ADD)
+        ts(A("Hj", h0, h0 + n), A("Hi", h0, h0 + n), 4095, AND)
+        cp(A("Hu", h0, h0 + n), A("Hj", h0, h0 + n))
+
+    def g5(t, ch):
+        lo, hi = 640 * ch, 640 * ch + 640; y = 640 if ch < 2 else 0
+        step = 320 if ch in SPLIT5 else 640
+        for a in range(lo, hi, step):
+            at(t, G5AT[ch] + (a - lo) / 640)
+            tt(A("D5", a, a + step), IN(A(XH(t)), A("Hu", a // 16, (a + step) // 16)), A(YB(t), y, y + step), SUB)
+            act(A("A5", a, a + step), A("D5", a, a + step), AF.Abs)
+        for a, b, out in ([], [(0, 1280, A("pb3", 0, 80))], [], [(1280, 2560, A("pb0", 0, 80))], [(lo, hi, A("pb1", 0, 40))],
+                          [(lo, lo + 320, A("pb4", 0, 20)), (lo + 320, hi, A("pb2", 0, 20))])[ch]:
+            mm(out, A("IDf"), A("PAY", a // 16, b // 16), True, False)
+            for r in range(16): mm(out, A("EW", 15 - r, 143 - r), A("A5", a + r, b, 16), False, r == 15)
+
+    def kown():
+        for c in range(5): emit("V", "tensor_reduce", [C("K", 10 + c), A("pb3", c, 80, 5), AxisListType.X, MIN])
+
+    def kfar():
+        cp(A("AC", 0, 80), A("pb0", 0, 80))
+        tt(A("AC", 80, 120), A("AC", 0, 40), A("AC", 40, 80), MIN)
+        tt(A("AC", 0, 40), A("pb1", 0, 40), A("AC", 80, 120), MIN)
+        tt(A("AC", 40, 60), A("AC", 0, 20), A("AC", 20, 40), MIN)
+        tt(A("AC", 60, 80), A("pb4", 0, 20), A("AC", 40, 60), MIN)
+        tt(A("AC", 120, 140), A("pb2", 0, 20), A("AC", 60, 80), MIN)
+        tt(A("K", 0, 10), A("AC", 120, 130), A("AC", 130, 140), MIN)
+
+    def close(t):
+        S15 = lambda n: A(n, 0, 15)
+        last = t == RO - 1; TT = T0 + P * t; lv = 16 * t
+        cp(S15("Ki"), S15("K"))
+        ts(A("fw", lv, lv + 10), A("K", 0, 10), C("TH", 0), OP.is_lt)
+        ts(A("fw", lv + 10, lv + 15), A("K", 10, 15), C("TH", 0), OP.is_lt, -2.0, MUL)
+        for u in range(t + 1): mm(A("pb2", 0, 15), A("ONE"), A("fw", 16 * u, 16 * u + 15), u == 0, u == t)
+        ts(S15("kp"), S15("Ki"), 2047, AND)
+        act(S15("nf"), S15("K"), AF.Relu, bias=C("TH", 3), scale=8192.0)
+        tt(S15("t1"), S15("kp"), S15("ui"), MUL)
+        ts(S15("mi"), S15("Ki"), 11, SHR, 15, AND)
+        tt(S15("t2"), S15("t1"), S15("qi"), ADD)
+        emit("V", "tensor_reduce", [C("dB", 0), A("pb2", 0, 15), AxisListType.X, ADD])
+        ts(S15("hh"), S15("t2"), 4095, AND)
+        ts(S15("a12"), S15("t2"), 12, AND)
+        ts(C("dB", 1), C("dB", 0), C("TH", 1), GT, -1.0, MUL)
+        ts(C("dB", 2), C("dB", 0), C("TH", 2), OP.is_lt, 0.5, MUL)
+        ts(S15("x1"), S15("hh"), TT / 4096.0, MUL, -255.0 / 512, ADD)
+        ts(S15("x2"), S15("a12"), TM / 4.0, MUL)
+        for c in range(3): act(A("LV", lv + c, lv + 15, 3), A("fw", lv + 5 * c, lv + 5 * c + 5), AF.Identity, bias=1.0, scale=C("dB", 1 if c < 2 else 2))
+        tt(S15("ix"), S15("x1"), S15("x2"), ADD)
+        ts(S15("a3"), S15("t2"), 3, AND)
+        cp(S15("L1"), S15("ix"))
+        if not last:
+            scan(S15("cum"), A("ONEs", 0, 15), A("LV", lv, lv + 15), MUL, ADD)
+        cp(A("RC"), IN(A("R4", 0, 3 * TM + TT), S15("L1")))
+        if not last:
+            mm(A("pb2", 0, 1), A("TRS"), C("cum", 14), True, True)
+            mm(A("pb2", 1, 2), A("BLK"), C("cum", 14), True, True)
+            if t == 0: mm(A("pb2", 2, 3), A("LT8"), C("cum", 14), True, True)
+        for j in range(4):
+            out = A(("pb3", "pb4", "pb0", "pb7")[j], 0, P)
+            mm(out, A("E0"), A("LN", 0, P), True, False)
+            mm(out, A("SH", 128 * j, 128 * j + 128), A("RC"), False, True)
+            if j >= (2 if last else WV): cp(A("WT", P * j, P * j + P), out)
+            else: act(A("WT", P * j, P * j + P), out, AF.Copy)
+        tt(S15("y3"), S15("mi"), S15("STR"), MUL)
+        tt(S15("g3"), S15("nf"), S15("LOC"), ADD)
+        ts(S15("y2"), S15("a3"), 240.0, MUL)
+        tt(S15("g2"), S15("nf"), S15("SL"), ADD)
+        tt(S15("z3"), S15("y3"), S15("g3"), ADD)
+        tt(S15("z2"), S15("y2"), S15("g2"), ADD)
+        ts(S15("L3"), S15("z3"), 3840.0, MIN)
+        tt(S15("w2"), S15("z2"), S15("NFL"), MIN)
+        act(A("EE"), IN(A("D5"), S15("L3")), AF.Identity, bias=191.75, scale=0.5)
+        if not last:
+            act(S15("e1"), A("LV", lv, lv + 15), AF.Identity, bias=C("fT", 0), scale=-1024.0)
+            ts(S15("pf1"), S15("msk"), A("pb2", 1, 2), MUL)
+        cp(S15("L2"), S15("w2"))
+        if not last:
+            tt(S15("e2"), S15("e1"), S15("DU"), MIN)
+            tt(S15("pf2"), S15("bas"), S15("pf1"), SUB)
+            tt(S15("e3"), S15("e2"), S15("cum"), ADD)
+            cp(S15("LF"), S15("pf2"))
+            for c in range(3): ts(A("LP", 5 * c, 5 * c + 5), A("e3", c, 15, 3), A("pb2", 0, 1), ADD)
+            if t == 0: cp(A("CN", 10, 12), A("pb2", 1, 3))
+            w = WIN[t + 1]
+            act(A("BIG", w, w + P), IN(A("BIG", 0, T0 if t == 0 else w), S15("LF")), AF.Copy)
+        ts(A("NEW"), IN(A("WT"), S15("L2")), C("Kp", 6 + t), ADD)
+        if not last: cp(IN(A("BIG", w, w + 600), S15("LP")), A("NEW"))
+        act(A("YT", P * t, P * t + P), IN(A("NEW"), S15("NBu")), AF.Copy)
+        for c in range(15):
+            out = A("pb1", 3 * (c % 5) + c // 5, P, 15); y = 16 * c + (480 if c >= 10 else 0)
+            mm(out, A("ID"), A(YB(t), y, y + 16), True, False)
+            mm(out, A("ID"), A("EE", 16 * c, 16 * c + 16), False, True)
+        act(A("X", NB + P * t, NB + P * t + P), A("pb1", 0, P), AF.Identity, bias=-192.0)
+        at(t, 22.0); store("Y", T.ya[:, P * t:P * t + P], A("LV", lv, lv + 15))
+        at(t, 22.0); store("Y", T.yx[:, P * t:P * t + P], A("X", NB + P * t, NB + P * t + P))
+        at(t, 22.0); store("Y", T.yt[:, P * t:P * t + P], A("YT", P * t, P * t + P))
+
+    OLD = (None, 12, 26)
+    for t in range(RO):
+        TT = T0 + P * t; nx = t + 1 < RO
+        res(t)
+        if t == 0: bhc(0, 0, 256)
+        g2(t, 0)
+        if t:
+            ts(A("Rh", TT - P, TT), A("YT", P * t - P, P * t), -1024.0, ADD)
+            bh(t, OLD[t], 256 // PLANS[t][0])
+        else:
+            xh(0, 0, 64, NB); tables_a()
+        g2(t, 1)
+        if t == 0: xh(0, 64, 96, NB)
+        g2(t, 2)
+        if t: bhc(t, OLD[t] * PLANS[t][0], 256)
+        else: xh(0, 96, 128, NB); tables_b()
+        g2(t, 3); g2(t, 4)
+        pick(t, False); send(t)
+        if t: xh(t, OLD[t] * PLANS[t][0], 256, NB + P * t)
+        g2(t, 5)
+        if t == 0:
+            late_consts(); xh(0, 128, 192, NB); tables_c(); tables_d()
+            for j in range(4, 14): mask(j)
+        if nx: prep(t)
+        pick(t, True)
+        upe(t, True); rep(t, True)
+        if t == 0:
+            xh(0, 192, 256, NB)
+            for j in range(14, 22): mask(j)
+        u1(True); u2(True)
+        if t:
+            for j in range(4): r4(j, TT - P, TT, "pb6" if j % 2 else "pb7")
+        keep(t)
+        g5(t, 0)
+        upe(t, False); rep(t, False)
+        u1(False)
+        g5(t, 1)
+        u2(False)
+        if t == 0:
+            for j in range(22, 31): mask(j)
+        if nx: bh(t + 1, 0, OLD[t + 1])
+        for ch in range(2, 6):
+            g5(t, ch)
+            if t == 0:
+                r4(ch - 2, 0, 512, "pb6"); r4(ch - 2, 512, 1024, "pb7")
+            if ch == 3:
+                kown()
+                if nx: bhc(t + 1, 0, OLD[t + 1] * PLANS[t + 1][0])
+        if t == 0:
+            for j in range(31, len(SPANS)): mask(j)
+        kfar()
+        if nx: xh(t + 1, 0, 64, NB + P * t)
+        close(t)
+        if nx:
+            xh(t + 1, 64, OLD[t + 1] * PLANS[t + 1][0], NB + P * t)
+
+    seen = {}; bank = {}
+    for n, o in enumerate(ops):
+        deps = set(); soft = set()
+        for regs, wr in ((o["r"], False), (o["w"], True)):
+            for (name, cols) in regs:
+                if name.startswith("pb"):
+                    e, before, now = bank.get(name, (None, [], []))
+                    if e != o["q"]: e, before, now = o["q"], (now[-1:] if e == "P" else now), []
+                    deps.update(before)
+                    if e == "P": soft.update(now[-1:])
+                    if n not in now: now = now + [n]
+                    bank[name] = (e, before, now)
+                    continue
+                deps.update(m for (c2, w2, m) in seen.get(name, []) if m != n and (wr or w2) and cols & c2)
+        for regs, wr in ((o["r"], False), (o["w"], True)):
+            for (name, cols) in regs:
+                old = seen.get(name, [])
+                if wr: old = [x for x in old if x[0] & ~cols]
+                seen[name] = old + [(cols, wr, n)]
+        if o["kind"] == "arr": deps = set(); soft = {n - 1}
+        if o["kind"] == "d" and o["w"]:
+            soft.update(m for m in range(n) if ops[m]["kind"] == "d" and ops[m]["q"] == o["q"])
+        o["deps"] = sorted(deps); o["soft"] = sorted(soft)
+    if not ORDER: ORDER.extend(_schedule(ops))
+    pos = {m: n for n, m in enumerate(ORDER)}
+    got = {q: {} for q in Q}
+    for n in ORDER:
+        o = ops[n]
+        if o["kind"] == "arr": continue
+        best = {}
+        for m in o["deps"]:
+            key = ops[m]["q"] if ops[m]["kind"] == "c" else m
+            if key not in best or pos[best[key]] < pos[m]: best[key] = m
+        need = []
+        for key, m in best.items():
+            if got[o["q"]].get(key, -1) < pos[m]:
+                got[o["q"]][key] = pos[m]; need.append(m); ops[m]["sig"] = True
+        o["need"] = need
+    cnt = {q: 0 for q in Q}; nd = 0; sent = 0; tail = []
+    for n in ORDER:
+        o = ops[n]
+        if o["kind"] == "arr":
+            o["at"] = (T.sem["arr" + o["q"][1:]], o["n"]); sent += o["n"]; continue
+        q = Q[o["q"]]
+        for m in o["need"]: q.wait_ge(*ops[m]["at"])
+        call = {"tensor_copy": lambda: q.tensor_copy, "tensor_tensor": lambda: q.tensor_tensor, "tensor_scalar": lambda: q.tensor_scalar,
+                "memset": lambda: q.memset, "tensor_reduce": lambda: q.tensor_reduce, "tensor_tensor_scan": lambda: q.tensor_tensor_scan,
+                "transpose": lambda: q.transpose, "activation": lambda: q.activation, "matmul": lambda: q.matmul, "iota": lambda: q.iota,
+                "affine_select": lambda: q.affine_select, "dma_start": lambda: q.dma_start, "remote_dma_fused": lambda: q.remote_dma_fused}[o["fn"]]()
+        ins = call(*o["a"], **o["k"])
+        if o["kind"] == "d":
+            s = T.sem[DMAS[nd]]; nd += 1; ins.then_inc(s, 16); o["at"] = (s, 16)
+            if not o.get("sig"): tail.append(o["at"])
+        elif o["kind"] == "c" and o.get("sig"):
+            cnt[o["q"]] += 1; s = T.sem["q" + o["q"]]; ins.then_inc(s, 1); o["at"] = (s, cnt[o["q"]])
+    g.wait_ge(T.sem.sent, sent)
+    for at in tail: g.sync.wait_ge(*at)

@@ -3,9 +3,10 @@ from concourse.mybir import AluOpType as OP, AxisListType, ActivationFunctionTyp
 
 NB, T0, P, RO = 2048, 1024, 240, 3
 TM = T0 + P * (RO - 1)
-W0, W1, W2 = 1024, 1264, 1864
-WIN = (W0, W1, W2)
+CI, R1, CJ = 240, 1264, 1504
 KOFF = -63 * 2 ** 18
+TOP = 65536.0
+RND = 1.5 * 2 ** 23
 F, H, I, U, B = "float32", "float16", "int32", "uint16", "bfloat16"
 
 
@@ -28,22 +29,22 @@ for _p in PLANS:
         if _x[2:] not in SPANS: SPANS.append(_x[2:])
 
 _S = dict(
-    X=(2768, B), Ri=(1024, I), Z=(240, B), Lt=(64, I), Lb=(64, B), Lz=(72, B), rho=(64, F), A1=(64, F), A2=(64, F), e0=(64, F), p0u=(64, U),
-    BIG=(2464, F), Rh=(TM, H), R4=(4 * TM, F), ZR=(3840, B), D2=(3840, B), A2w=(3840, B), D5=(3856, B), A5=(3840, B),
-    XHa=(4096, B), XHb=(4096, B), BHa=(256, U), BHb=(256, U), RES=(240, U), WT=(1200, F), RC=(240, H), NEW=(240, F), YT=(720, F),
-    YS=(480, B), YB0=(1280, B), YB1=(1280, B), YB2=(1280, B), EE=(240, B), LN=(480, B), E0=(128, B), LV=(48, F),
-    ONE=(128, B), ONEf=(128, F), BLK=(128, B), BLKt=(128, B), BLKf=(128, F), EW=(144, B), TRI=(128, B), UP=(128, B), TRS=(128, B), LT8=(128, B),
+    X=(2768, B), Ri=(1024, I), Z=(240, B), Zp=(240, B), Lt=(64, I), Lb=(64, B), Lz=(72, B), rho=(64, F), A1=(64, F), A2=(64, F), e0=(64, F), p0u=(64, U),
+    BIG=(1744, F), Rh=(TM, H), R0=(1024, F), R4=(4 * TM, F), ZR=(3840, B), D2=(3840, B), A2w=(3840, B), D5=(3856, B), A5=(3840, B),
+    XHa=(4096, B), XHb=(4096, B), BHa=(256, U), BHb=(256, U), RES=(240, U), RESf=(240, F), WT=(1200, F), RC=(240, H), NEW=(240, F), YT=(720, F),
+    YS=(480, B), YB0=(1920, B), YB1=(1920, B), YB2=(1920, B), EE=(240, B), LN=(480, B), E0=(128, B), LV=(48, F),
+    ONE=(128, B), TWO=(128, B), ONEf=(128, F), BLK=(128, B), BLKt=(128, B), BLKf=(128, F), EW=(144, B), TRI=(128, B), UP=(128, B), UPI=(128, B), GE8=(128, B),
     S7=(128, F), S15=(128, F), S15b=(128, B), ID=(128, B), IDf=(128, F), G8=(128, F), G8t=(128, F), BK1=(128, B), BK1f=(128, F), SH=(512, B), SHf=(128, F),
-    RS=(384, B), RK=(384, B), MK=(128 * len(SPANS), B), WH=(128, B), WL=(128, B),
-    Ki0=(2, I), Kp=(10, F), ZLi=(240, I), ZL=(240, U), T17=(18, F), GE=(18, F), LTt=(18, F), C16=(240, F), BGM=(160, B), RST=(240, F),
-    PA=(240, B), PBb=(240, B), MT=(240, F), PBS=(240, F), RK2=(240, F), PAY=(240, F), KT=(16, F), WK=(4, I), WKi=(4, I), WKf=(4, F),
-    TC=(4, I), TCf=(4, F), TH=(8, F), CN=(16, F), SL=(16, F), LC=(16, F), DU=(16, F), NFL=(16, F), LOC=(16, F), STR=(16, F),
-    s0=(16, F), s1=(16, F), s2=(16, F), s3=(16, F), s4=(16, F), i0=(16, I), NBu=(16, U), L0=(16, U),
-    SC=(240, F), SU=(240, F), k2=(16, I), k2b=(16, I), LY=(16, U), ui0=(16, I), ui=(16, I), uf=(16, F), sq=(16, I), qi=(16, I), qf=(16, F),
-    Hi=(240, I), Hj=(240, I), Hu=(240, U), AC=(160, F), K=(16, F), Ki=(16, I), nf=(16, F), fw=(48, B), kp=(16, I), mi=(16, I),
-    t1=(16, I), t2=(16, I), hh=(16, I), a12=(16, I), a3=(16, I), x1=(16, F), x2=(16, F), ix=(16, I), L1=(16, U), L2=(16, U), L3=(16, U),
-    g2=(16, F), g3=(16, F), y2=(16, F), y3=(16, F), z2=(16, F), z3=(16, F), w2=(16, F), dB=(4, F), cum=(16, B), e1=(16, F), e2=(16, F), e3=(16, F),
-    LP=(16, U), fT=(16, F), msk=(16, F), bas=(16, F), pf1=(16, F), pf2=(16, F), LF=(16, U), ONEs=(64, F),
+    RS=(384, B), RK=(384, B), RT=(384, B), MK=(128 * len(SPANS), B), W16=(128, H),
+    Ki0=(2, I), Kp=(16, F), T17=(18, F), GE=(18, F), LTt=(18, F), C16=(80, F), BGM=(80, B), RST=(80, F), PK1=(80, F), PK2=(80, F),
+    MT=(80, F), PBS=(80, F), RK2=(80, F), PAY=(80, F), KT=(16, F), WK=(4, I), WKf=(4, F),
+    TC=(4, I), TCf=(4, F), TH=(8, F), CN=(16, F), SL=(16, F), IDX=(16, F), NFL=(16, F), LOC=(16, F), LAN=(18, F),
+    s0=(18, F), s1=(18, F), s2=(18, F), s3=(18, F), s4=(16, F), i0=(16, I), NBu=(16, U), LR=(18, U),
+    SC1=(240, F), SC2=(240, F), SU=(240, F), kf=(16, F), LY=(18, U), ri=(16, I), QD0=(60, F), QD1=(60, F), QS=(60, F), uf=(16, F),
+    Hi=(240, I), Hj=(240, I), Hu=(240, U), K=(16, F), Ki=(16, I), nf=(16, F), fw=(16, B), kp=(16, I), mi=(16, I),
+    t1=(16, F), t2=(16, I), hh=(16, I), a12=(16, I), a3=(16, I), x1=(16, F), x2=(16, F), ix=(16, F), L1=(16, U), L2=(16, U), L3=(16, U),
+    g2=(16, F), g3=(16, F), y2=(16, F), y3=(16, F), z2=(16, F), z3=(16, F), w2=(16, F), Bp=(2, F), cum=(16, B), dead=(16, F), e1=(16, F), e3=(16, F),
+    LP=(16, U), msk=(18, F), bas=(18, F), pf1=(18, F), pf2=(18, F), ONEs=(64, F),
 )
 HOME = {}
 _W = {}
@@ -54,53 +55,58 @@ SCRATCH = {k: ("sbuf", [128, v[0]], v[1]) for k, v in _S.items() if k not in HOM
 for _k, _v in _W.items(): SCRATCH["pool_" + _k] = ("sbuf", [128, _v], _k)
 for _i in range(8): SCRATCH["pb%d" % _i] = ("psum", [128, 512], F)
 DMAS = ["d%d" % i for i in range(24)]
-SEMAPHORES = ["qV", "qS", "qP", "qG", "sent", "arr0", "arr1", "arr2"] + DMAS
+SEMAPHORES = ["qV", "qS", "qP", "qG", "sent"] + ["arr%d%d" % (t, c) for t in range(RO) for c in range(2)] + DMAS
 
 
 ORDER = []
-PACE = [dict(cy=1.0, pe=0.5, ga=1.5, sc=3.8, lat=70, dma=2000, rem=2500), dict(cy=0.9, pe=0.45, ga=1.15, sc=2.2, lat=50, dma=1700, rem=2000),
-        dict(cy=1.15, pe=0.7, ga=1.95, sc=5.5, lat=110, dma=2500, rem=3500)]
-TRIES, PASSES, JIT, MOVES = 60, 2, 2000.0, 6000
-XC = 24
-SPLIT2, SPLIT5 = (3, 4, 5), (0, 1, 5)
-GMASK = 31
-WV = 4
-BASE = (10.6, 33.5, 55.5)
-G2AT = (0.0, 1.0, 2.0, 3.0, 4.0, 5.6)
-G5AT = (10.0, 11.5, 13.0, 14.0, 15.0, 16.0)
-XHAT = ((-2.2, 0.7), (-4.0, 0.8), (-12.0, 1.0))
+PACE = [dict(cy=0.83, pe=0.42, ga=1.56, sc=3.8, lat=170, dma=1500, bw=200.0, rem=2500),
+        dict(cy=1.15, pe=0.6, ga=1.8, sc=5.0, lat=200, dma=2200, bw=160.0, rem=3500)]
+WEIGHT = (1.0, 1.45)
+TRIES, PASSES, JIT, MOVES, HEAT, SIDE, SEED = 10, 3, 1500.0, 60000, 800.0, 0.3, 12345
+XC = 16
+CH2 = ((8, 4, 4), (8, 4, 4), (8, 4, 4))
+CH5 = ((8, 8), (8, 8), (8, 6, 2))
+GR5 = ((16,), (16,), (8, 8))
+ORD2 = (0, 1, 2)
+ORD5 = (0, 1, 2)
+XV = ((192, 256), (0, 0), (0, 0))
 
 
 def _times(ops, p):
     out = []
     for o in ops:
         kind, n, r = o["cost"]
-        if kind == "dma": out.append((60.0, p["dma"] + n / 200.0))
-        elif kind == "rem": out.append((300.0, 300.0))
+        if kind == "dma": out.append((60.0, p["dma"] + n / p["bw"]))
+        elif kind == "rem": out.append((300.0 + n, 300.0 + n))
         elif kind == "arr": out.append((0.0, p["rem"] - 300.0))
         else:
-            d = {"e": max(64, n * r) * p["cy"], "ga": r + n * p["ga"] * p["cy"], "sc": r + n * p["sc"] * p["cy"], "pe": n * p["pe"], "g": r + 2 * n * p["cy"]}[kind]
+            d = {"e": max(64, n * r), "ga": r * 1.2 + n * p["ga"], "sc": r * 1.2 + n * p["sc"], "pe": n * p["pe"] / p["cy"], "g": r * 1.2 + 2 * n}[kind] * p["cy"]
             out.append((d, d))
     return out
 
 
-def _replay(ops, order, p):
-    if "tm" not in p: p["tm"] = _times(ops, p)
-    tm = p["tm"]; lat = p["lat"]; free = {}; end = [0.0] * len(ops)
-    for n in order:
-        o = ops[n]; q = o["q"]; t = free.get(q, 0.0)
-        for m in o["deps"]:
-            if end[m] > t: t = end[m]
-        if o["kind"] == "arr": t = end[n - 1] - lat
-        free[q] = t + tm[n][0]; end[n] = t + tm[n][1] + lat
-    return max(end)
+def _replay(G, order, p, lo, old):
+    qs, deps = G; d0, d1 = p["d0"], p["d1"]
+    fin, end, by = (old[0][:], old[1][:], old[2][:]) if lo else ([0.0] * len(qs), [0.0] * len(qs), [-1] * len(qs))
+    last = [-1] * 12; free = [0.0] * 12; j = lo; left = 5
+    while j and left:
+        j -= 1; n = order[j]; q = qs[n]
+        if last[q] < 0:
+            last[q] = n; free[q] = fin[n]; left -= q < 5
+    for n in order[lo:]:
+        q = qs[n]; t = free[q]; w = last[q]
+        for m in deps[n]:
+            if end[m] > t: t = end[m]; w = m
+        free[q] = fin[n] = t + d0[n]; end[n] = t + d1[n]; by[n] = w; last[q] = n
+    return fin, end, by
 
 
-def _place(ops, tm, edges, key, back):
+def _place(ops, tm, edges, key):
     start = [0.0] * len(ops); busy = {}
     for i in sorted(range(len(ops)), key=key):
         t = 0.0
-        for m, lag in edges[i]: t = max(t, start[m] + lag)
+        for m, lag in edges[i]:
+            if start[m] + lag > t: t = start[m] + lag
         d = max(tm[i][0], 1.0); row = busy.setdefault(ops[i]["q"], []); k = len(row)
         while k and row[k - 1][1] > t: k -= 1
         while k < len(row) and row[k][0] < t + d:
@@ -110,47 +116,77 @@ def _place(ops, tm, edges, key, back):
 
 
 def _schedule(ops):
-    n = len(ops); best = None; x = 12345; tm0 = _times(ops, PACE[0])
+    n = len(ops); best = None; x = SEED; names = ["V", "S", "P", "G", "Y"]; anc = [0] * n; deps = []
+    for i, o in enumerate(ops):
+        if o["q"] not in names: names.append(o["q"])
+        d = o["deps"] + ([i - 1] if o["kind"] == "arr" else []); up = 0
+        for m in d: up |= anc[m]
+        deps.append([m for m in d if not up >> m & 1])
+        for m in d: up |= 1 << m
+        anc[i] = up
+    G = ([names.index(o["q"]) for o in ops], deps)
+    for q in PACE:
+        tm = _times(ops, q); q["d0"] = [a for a, b in tm]; q["d1"] = [b + q["lat"] * (o["kind"] != "r") for (a, b), o in zip(tm, ops)]
+    p = PACE[0]; tm = _times(ops, p); fw = [[] for _ in ops]; bw = [[] for _ in ops]; on = [[] for _ in ops]
+    for i, o in enumerate(ops):
+        for m, lat in [(m, p["lat"]) for m in deps[i]] + [(m, tm[m][0] - tm[m][1]) for m in o["soft"]]:
+            fw[i].append((m, tm[m][1] + lat)); bw[m].append((i, max(tm[i][0], 1.0) + tm[m][1] - max(tm[m][0], 1.0) + lat)); on[m].append((i, tm[m][1] + lat))
+    marks = [i for i, o in enumerate(ops) if "wide" in o]
+    value = lambda st: sum((max(s[1]) + SIDE * sum(s[1][i] for i in marks) / len(marks)) / w for s, w in zip(st, WEIGHT))
     for k in range(TRIES):
-        p = PACE[0]; tm = _times(ops, p); fw = [[] for _ in ops]; bw = [[] for _ in ops]
-        for i, o in enumerate(ops):
-            for m, lat in [(m, p["lat"]) for m in o["deps"]] + [(m, tm[m][0] - tm[m][1]) for m in o["soft"]]:
-                fw[i].append((m, tm[m][1] + lat)); bw[m].append((i, max(tm[i][0], 1.0) + tm[m][1] - max(tm[m][0], 1.0) + lat))
         late = [0.0] * n
         for i in range(n - 1, -1, -1):
             x = (x * 1103515245 + 12345) % 2 ** 31
-            want = -1e6 if ops[i]["tag"] is None else -ops[i]["tag"] + (x / 2 ** 31 - 0.5) * JIT * (k > 0)
-            late[i] = max([want] + [late[j] + tm0[i][1] + 70.0 for j, lag in bw[i]]) + 1e-3
+            late[i] = max([tm[i][1]] + [late[j] + lag for j, lag in on[i]]) + 1e-3 + (x / 2 ** 31) ** 8 * JIT * (k > 0)
         for _ in range(PASSES):
-            s = _place(ops, tm, fw, lambda i: (-late[i], i), False)
+            s = _place(ops, tm, fw, lambda i: (-late[i], i))
             order = sorted(range(n), key=lambda i: (s[i], i))
-            v = sum(_replay(ops, order, q) / w for q, w in zip(PACE, (1.0, 0.8, 1.3)))
-            if best is None or v < best[0]: best = (v, order, s)
+            st = [_replay(G, order, q, 0, None) for q in PACE]; v = value(st)
+            if best is None or v < best[0]: best = (v, order, st)
             e = [s[i] + max(tm[i][0], 1.0) for i in range(n)]
-            r = _place(ops, tm, bw, lambda i: (-e[i], -i), True)
+            r = _place(ops, tm, bw, lambda i: (-e[i], -i))
             late = [r[i] + max(tm[i][0], 1.0) for i in range(n)]
-    p = PACE[0]; tm = _times(ops, p)
-    fw = [[(m, tm[m][1] + p["lat"]) for m in o["deps"]] + [(m, tm[m][0]) for m in o["soft"]] for o in ops]
-    movable = [i for i, o in enumerate(ops) if o["q"] != "P" and o["w"]]
-    cur = best
+    pre = [set(m for m, _ in fw[i]) for i in range(n)]; qs = G[0]
+    cur = best; pos = None
     for k in range(MOVES):
         u = []
-        for _ in range(4):
+        for _ in range(6):
             x = (x * 1103515245 + 12345) % 2 ** 31; u.append(x / 2 ** 31)
-        i = movable[int(u[0] * len(movable))]; d = (u[1] - 0.6) * 12000 * u[2]; key = list(cur[2])
-        for j in movable:
-            if j == i or (0 < j - i < 40 * u[3] and ops[j]["w"][0][0] == ops[i]["w"][0][0]): key[j] += d
-        if d < 0:
-            for j in range(n - 1, -1, -1):
-                for m, _ in fw[j]: key[m] = min(key[m], key[j])
+        order = cur[1]
+        if pos is None:
+            pos = {m: j for j, m in enumerate(order)}; ways = {}
+        w = (int(u[4] * len(PACE)), marks[int(u[5] * 2 * len(marks))] if u[5] < 0.5 else -1)
+        if w not in ways:
+            fin, end, by = cur[2][w[0]]; j = w[1] if w[1] >= 0 else end.index(max(end)); ways[w] = []
+            while by[j] >= 0:
+                if by[j] not in pre[j]: ways[w].append((by[j], j))
+                j = by[j]
+        pairs = ways[w]
+        if not pairs: continue
+        a, b = pairs[int(u[0] * (len(pairs) if w[1] < 0 else min(len(pairs), 30)))]; lo, hi = pos[a], pos[b]; hop = int(1 + 12 * u[2] ** 3)
+        if u[1] < 0.5:
+            while hop > 1 and lo > 0:
+                lo -= 1; hop -= qs[order[lo]] == qs[b]
+            part = order[lo:hi + 1]; move = {b}
+            need = set(pre[b])
+            for j in reversed(part):
+                if j in need: move.add(j); need |= pre[j]
+            new = [j for j in part if j in move] + [j for j in part if j not in move]
         else:
-            for j in range(n):
-                for m, _ in fw[j]: key[j] = max(key[j], key[m])
-        s = _place(ops, tm, fw, lambda j: (key[j], j), False)
-        order = sorted(range(n), key=lambda j: (s[j], j))
-        v = sum(_replay(ops, order, q) / w for q, w in zip(PACE, (1.0, 0.8, 1.3)))
-        if v < cur[0] + 150.0 * (1.0 - k / MOVES): cur = (v, order, s)
-        if v < best[0]: best = (v, order, s)
+            while hop > 1 and hi < n - 1:
+                hi += 1; hop -= qs[order[hi]] == qs[a]
+            part = order[lo:hi + 1]; move = {a}
+            for j in part:
+                if pre[j] & move: move.add(j)
+            new = [j for j in part if j not in move] + [j for j in part if j in move]
+        if new == part: continue
+        order = order[:lo] + new + order[hi + 1:]
+        st = [_replay(G, order, q, lo, s) for q, s in zip(PACE, cur[2])]; v = value(st)
+        if v < cur[0] + HEAT * u[3] ** 2 * (1.0 - k / MOVES):
+            d0 = p["d0"]; fin = st[0][0]; at = {m: j for j, m in enumerate(order)}
+            order.sort(key=lambda j: (fin[j] - d0[j], at[j]))
+            cur = (v, order, st); pos = None
+            if v < best[0]: best = cur
     return best[1]
 
 
@@ -160,10 +196,7 @@ def rank_program(g, core, T, topo):
         return
     N = len(T.cores)
     Q = {"V": g.vector, "S": g.scalar, "P": g.tensor, "G": g, "Y": g.sync}
-    ops = []; hint = []
-
-    def at(t, us):
-        hint.append(1000.0 * (BASE[t] + us))
+    ops = []
 
     def reg(name, lo, hi, st=1):
         return (name, (1 << hi) - (1 << lo) if st == 1 else sum(1 << c for c in range(lo, hi, st)))
@@ -203,8 +236,7 @@ def rank_program(g, core, T, topo):
         elif len(aps) > 1 and len(aps[1]) > 3: cost = ("ga", size(aps[0]), 50 if q == "V" else 65)
         elif fn == "tensor_tensor": cost = ("e", size(aps[0]), 1 if any(a[2][0][0].startswith("pb") for a in aps[1:]) else 2)
         else: cost = ("e", size(aps[min(1, len(aps) - 1)]), 0.5 if q == "V" and all(wide(a) == 2 for a in aps[:2]) else 1)
-        tag = hint.pop() if hint else None
-        ops.append(dict(tag=tag, cost=cost, q=q, fn=fn, a=[x[1] if isap(x) else x for x in args], k={n: (x[1] if isap(x) else x) for n, x in (kw or {}).items()}, w=w, r=r, kind=kind))
+        ops.append(dict(cost=cost, q=q, fn=fn, a=[x[1] if isap(x) else x for x in args], k={n: (x[1] if isap(x) else x) for n, x in (kw or {}).items()}, w=w, r=r, kind=kind))
 
     cp = lambda o, i: emit("V", "tensor_copy", [o, i])
     tt = lambda o, a, b, op: emit("V", "tensor_tensor", [o, a, b, op])
@@ -216,40 +248,46 @@ def rank_program(g, core, T, topo):
     def act(o, i, f, **k):
         emit("S", "activation", [o, i, f], k)
 
-    mm = lambda o, l, r, s, e: emit("P", "matmul", [o, l, r, s, e])
-    scan = lambda o, d0, d1, o0, o1: emit("V", "tensor_tensor_scan", [o, d0, d1, 0.0, o0, o1])
+    def mm(o, l, r, s, e, join=False):
+        emit("P", "matmul", [o, l, r, s, e])
+        if join:
+            b = ops.pop(); a = ops[-1]
+            a["more"] = a.get("more", []) + [b["a"]]; a["w"] = a["w"] + b["w"]; a["r"] = a["r"] + b["r"]; a["cost"] = ("pe", a["cost"][1] + b["cost"][1], 0)
+
+    scan = lambda o, d0, d1, o0, o1, first=0.0: emit("V", "tensor_tensor_scan", [o, d0, d1, first, o0, o1])
 
     def iota(o, pat, base=0, cm=0):
         emit("G", "iota", [o, pat, base, cm], None if _S[o[2][0][0]][1] == I else {"allow_small_or_imprecise_dtypes": True})
 
     sel = lambda o, i, pat, op, base, cm, fill=0.0: emit("G", "affine_select", [o, i, pat, op, fill, base, cm])
+    loaded = [0]
 
     def load(q, o, src):
         emit(q, "dma_start", [o, src], kind="d")
-        ops[-1]["cost"] = ("dma", ops[-1]["cost"][1] + max([0] + [x["cost"][1] for x in ops[:-1]]), 0)
+        loaded[0] += ops[-1]["cost"][1] + 48000; ops[-1]["cost"] = ("dma", loaded[0], 0)
 
     def store(q, dst, i):
         emit(q, "dma_start", [dst, i[1]], kind="d", extra=([], i[2]))
 
-    Kp, P80, R0c, R1c, Rm, P15 = [C("Kp", j) for j in range(6)]
+    Kp, P5, R0c, P3, Rm, P15, PKc = [C("Kp", j) for j in range(7)]
     EQ, GEQ, GT, NE = OP.is_equal, OP.is_ge, OP.is_gt, OP.not_equal
     ADD, SUB, MUL, MIN, AND, SHR = OP.add, OP.subtract, OP.mult, OP.min, OP.bitwise_and, OP.arith_shift_right
     YB = lambda t: "YB%d" % t
     XH = lambda t: "XHb" if t % 2 else "XHa"
     BH = lambda t: "BHb" if t % 2 else "BHa"
+    S15 = lambda n: A(n, 0, 15)
 
     for x in range(2):
         for b in range(2):
             load("Y" if b else "S", A("Lt", 32 * b + 16 * x, 32 * b + 16 * x + 16), T.live[x::2, 512 * b:512 * b + 512])
+    for b in range(2): load("Y", A("Ri", 512 * b, 512 * b + 512), T.rings[:, 512 * b:512 * b + 512])
     load("S", A("Z"), T.z[:])
-    load("Y", A("Ri"), T.rings[:])
     load("Y", A("X", 0, NB), T.x0[:])
     load("Y", C("WK", 0), T.w[:]); load("Y", C("WK", 1), T.kap[:])
     load("Y", A("TC", 0, 1, p=(0, 8)), T.th[:]); load("Y", A("TC", 1, 2, p=(0, 8)), T.cap[:])
 
-    ms(A("ONE"), 1.0); ms(A("ONEf"), 1.0); ms(A("Lz", 0, 8), 0.0); ms(A("EW"), 0.0); ms(A("ONEs"), 1.0); ms(A("D5", 3840, 3856), 0.0)
+    ms(A("ONE"), 1.0); ms(A("TWO"), 2.0); ms(A("ONEf"), 1.0); ms(A("Lz", 0, 8), 0.0); ms(A("EW"), 0.0); ms(A("ONEs"), 1.0); ms(A("D5", 3840, 3856), 0.0)
     iota(C("Ki0", 0), [[0, 1]], 0, 1)
-    iota(A("ZLi"), [[1, 3], [3, 80]])
     iota(A("A1"), [[16, 64]])
     sel(A("BLKt"), A("ONE"), [[-16, 8], [0, 16]], GEQ, 0, 1)
     sel(A("BLK"), A("BLKt"), [[16, 8], [0, 16]], GEQ, 15, -1)
@@ -257,299 +295,258 @@ def rank_program(g, core, T, topo):
     sel(A("UP"), A("BLK"), [[-1, 128]], GT, 0, 1)
     ts(C("Ki0", 1), C("Ki0", 0), 15, AND)
     cp(Kp, C("Ki0", 1))
-    cp(A("ZL"), A("ZLi"))
     ts(A("SL"), A("A1", 0, 16), Kp, ADD)
     ts(A("A2"), A("A1"), Kp, ADD, -1.0, MUL)
     ts(A("A1"), A("A1"), Kp, ADD, -1024.0, ADD)
     ts(A("A2"), A("A2"), 1023.0, ADD)
-    ts(P80, Kp, 80.0, MUL); ts(R0c, Kp, 0.0, EQ); ts(Rm, Kp, 0.0, NE, -1024.0, MUL); ts(P15, Kp, 15.0, MUL)
+    ts(P5, Kp, 5.0, MUL); ts(R0c, Kp, 0.0, EQ); ts(P3, Kp, 3.0, MUL); ts(Rm, Kp, 0.0, NE, -1024.0, MUL); ts(P15, Kp, 15.0, MUL)
+    ts(PKc, Kp, -80.0, MUL, TOP - 15, ADD)
+    for t in range(RO): ts(C("Kp", 8 + t), R0c, float(NB + P * t - 1024), MUL, 1024.0, ADD)
     sel(A("ID"), A("ONE"), [[-1, 128]], EQ, 0, 1)
     iota(A("T17"), [[1, 18]])
     sel(A("S7"), A("ONEf"), [[-16, 8], [0, 16]], EQ, -7, 1)
     sel(A("S15"), A("ONEf"), [[-16, 8], [0, 16]], EQ, -15, 1)
     ts(A("EW", 15, 143, 16), A("BLK", 0, 128, 16), 32768.0, MUL)
-
-    def zrep(c0, c1):
-        act(A("ZR", 16 * c0, 16 * c1), IN(A("Z"), A("ZL", c0, c1)), AF.Copy)
+    iota(A("LAN"), [[1, 3], [48, 6]])
+    ts(A("LAN"), A("LAN"), P3, ADD)
+    ms(A("RST"), 0.0); ms(A("RST", 0, 80, 16), TOP)
+    ms(A("PK2"), -1.0); ms(A("PK2", 15, 80, 16), TOP)
+    ms(A("PK1"), 0.0); ts(A("PK1", 15, 80, 16), A("T17", 0, 5), -16.0, MUL, PKc, ADD)
+    ms(A("QD0"), 1.0); ms(A("QD0", 0, 60, 4), 0.0); ms(A("QD0", 2, 60, 4), 2.0 ** 19)
+    ms(A("QD1", 1, 60, 4), -12.0 / 2 ** 24); ms(A("QD1", 2, 60, 4), RND); ms(A("QD1", 3, 60, 4), -RND)
+    for c in range(3): act(A("Zp", 80 * c, 80 * c + 80), A("Z", c, P, 3), AF.Copy)
+    for k in range(16): act(A("ZR", k, 3840, 16), A("Zp"), AF.Copy)
 
     def mask(j):
         lo, hi = SPANS[j]
-        m = A("MK", 128 * j, 128 * j + 128)
-        if j < GMASK:
-            ts(m, A("ID"), C("GE", lo), MUL, C("LTt", hi), MUL)
-        elif lo == 0 or hi == 16:
-            sel(m, A("ID"), [[0, 8], [1 if lo else -1, 16]], GEQ, -lo if lo else hi - 1, 0)
-        else:
-            sel(A("BLKt"), A("ID"), [[0, 8], [1, 16]], GEQ, -lo, 0)
-            sel(m, A("BLKt"), [[0, 8], [-1, 16]], GEQ, hi - 1, 0)
+        ts(A("MK", 128 * j, 128 * j + 128), A("ID"), C("GE", lo), MUL, C("LTt", hi), MUL)
 
     def bh(t, n0, n1):
         per, stp, plan = PLANS[t]
         for j, (rho, v, lo, hi) in enumerate(plan):
             k = SPANS.index((lo, hi))
-            mm(A("pb5", rho + per * n0, rho + per * (n1 - 1) + 1, per), A("MK", 128 * k, 128 * k + 128),
-               A("Rh", v + stp * n0, v + stp * (n1 - 1) + 1, stp), lo == 0, hi == 16)
-
-    def bhc(t, c0, c1):
-        ts(A(BH(t), c0, c1), A("pb5", c0, c1), 1024.0, ADD)
+            mm(A("pb6", rho + per * n0, rho + per * (n1 - 1) + 1, per), A("MK", 128 * k, 128 * k + 128),
+               A("Rh", v + stp * n0, v + stp * (n1 - 1) + 1, stp), lo == 0, hi == 16, lo > 0)
+        ts(A(BH(t), n0 * per, n1 * per), A("pb6", n0 * per, n1 * per), 1024.0, ADD)
 
     def xh(t, c0, c1, nb):
         for c in range(c0, c1, XC):
             d = min(c + XC, c1)
-            at(t, XHAT[t][0] + XHAT[t][1] * c / 16)
-            act(A(XH(t), 16 * c, 16 * d), IN(A("X", 0, nb), A(BH(t), c, d)), AF.Copy)
+            o, i = A(XH(t), 16 * c, 16 * d), IN(A("X", 0, nb), A(BH(t), c, d))
+            if XV[t][0] <= c < XV[t][1]: cp(o, i)
+            else: act(o, i, AF.Copy)
 
-    def r4(j, v0, v1, bank):
-        if j == 0:
-            mm(A(bank, 0, v1 - v0), A("ID"), A("Rh", v0, v1), True, True)
-        else:
-            mm(A(bank, 0, v1 - v0), A("RS", 128 * j - 128, 128 * j), A("Rh", v0, v1), True, False)
-            mm(A(bank, 0, v1 - v0), A("RK", 128 * j - 128, 128 * j), A("Rh", v0, v1), False, True)
-        at((v1 - T0) // P, 10.0 + 2 * j + v0 % 1024 / 512)
-        act(A("R4", TM * j + v0, TM * j + v1), A(bank, 0, v1 - v0), AF.Copy)
+    def r4(j, out, v0, v1, st, bank):
+        n = len(range(v0, v1, st))
+        mm(A(bank, 0, n), A("RT", 128 * j - 128, 128 * j) if j else A("ID"), A("Rh", v0, v1, st), True, True)
+        act(out, A(bank, 0, n), AF.Copy)
 
-    zrep(0, 40); zrep(40, 80); zrep(80, 160)
     cp(A("Lb"), A("Lt"))
     emit("V", "transpose", [A("Lz", 8, 72), A("Lb")])
-    mm(A("pb2", 0, 64), A("TRI"), A("Lz", 8, 72), True, False)
-    mm(A("pb2", 0, 64), A("UP"), A("Lz", 7, 71), False, True)
+    mm(A("pb4", 0, 64), A("TRI"), A("Lz", 8, 72), True, False)
+    mm(A("pb4", 0, 64), A("UP"), A("Lz", 7, 71), False, True)
     tt(A("e0"), A("A1"), A("Lz", 8, 72), MUL)
     tt(A("e0"), A("e0"), A("A2"), ADD)
-    scan(A("rho"), A("ONEs"), A("pb2", 0, 64), MUL, ADD)
+    scan(A("rho"), A("ONEs"), A("pb4", 0, 64), MUL, ADD)
     tt(A("e0"), A("e0"), A("rho"), ADD)
     cp(A("p0u"), A("e0"))
-    mm(A("pb2", 0, 2), A("S7"), A("rho", 41, 57, 15), True, True)
-    mm(A("pb2", 2, 3), A("S15"), C("rho", 63), True, True)
+    mm(A("pb4", 0, 2), A("S7"), A("rho", 41, 57, 15), True, True)
+    mm(A("pb4", 2, 3), A("S15"), C("rho", 63), True, True)
     ts(A("GE"), A("T17"), Kp, OP.is_le); ts(A("LTt"), A("T17"), Kp, GT)
-    for j in range(4): mask(j)
-    cp(A("CN", 0, 3), A("pb2", 0, 3))
-    ts(A("s0", 0, 15), A("SL", 0, 15), C("CN", 0), ADD)
-    ts(A("s1", 0, 15), A("s0", 0, 15), C("CN", 2), GEQ, C("CN", 2), MUL)
-    tt(A("s0", 0, 15), A("s0", 0, 15), A("s1", 0, 15), SUB)
-    cp(A("L0", 0, 15), A("s0", 0, 15))
-    ts(A("Rh", 0, T0), A("Ri"), -1024.0, ADD)
-    cp(IN(A("BIG", 0, T0), A("p0u")), A("Ri"))
-    cp(A("BIG", W0, W0 + P), IN(A("BIG", 0, T0), A("L0", 0, 15)))
+    for j in range(len(SPANS)): mask(j)
+    cp(A("CN", 0, 3), A("pb4", 0, 3))
+    ts(A("s0"), A("LAN"), C("CN", 0), ADD)
+    ts(A("s1"), A("s0"), C("CN", 2), GEQ, C("CN", 2), MUL)
+    tt(A("s2"), A("s0"), A("s1"), SUB)
+    cp(A("LR"), A("s2"))
+    for b in range(2):
+        ts(A("Rh", 512 * b, 512 * b + 512), A("Ri", 512 * b, 512 * b + 512), -1024.0, ADD)
+        cp(IN(A("BIG", CI, R1), A("p0u", 32 * b, 32 * b + 32)), A("Ri", 512 * b, 512 * b + 512))
+    act(A("BIG", CJ, CJ + P), A("BIG", CI, CI + P), AF.Copy)
     bh(0, 0, 256)
-    zrep(160, 240)
-    iota(A("C16"), [[0, 15], [1, 16]])
-    iota(A("PA"), [[0, 3], [1, 80]])
-    iota(A("PBb"), [[1280, 3], [0, 80]])
-    iota(A("MT", 0, 80), [[1, 16], [0, 5]]); iota(A("MT", 80, 240), [[1, 16], [0, 10]])
-    iota(A("PBS", 0, 80), [[2048, 16], [0, 5]], KOFF); iota(A("PBS", 80, 240), [[2048, 16], [0, 10]], KOFF)
+    xh(0, 0, 256, NB)
+    iota(A("C16"), [[0, 5], [1, 16]])
+    iota(A("MT"), [[1, 16], [0, 5]])
+    iota(A("PBS"), [[2048, 16], [0, 5]], KOFF)
     sel(A("G8t", p=(0, 8)), A("ONEf", p=(0, 8)), [[1, 128]], GEQ, 0, -16)
     sel(A("G8", p=(0, 8)), A("G8t", p=(0, 8)), [[-1, 128]], GEQ, 15, 16)
     sel(A("IDf"), A("ONEf"), [[-1, 128]], EQ, 0, 1)
-    iota(A("LC", 0, 15), [[-1, 15]], 599); iota(A("NFL", 0, 15), [[1, 3], [3, 5]], 960)
+    iota(S15("NFL"), [[80, 3], [1, 5]], 960); iota(S15("LOC"), [[1280, 3], [16, 5]])
     sel(A("S15b"), A("ONE"), [[-16, 8], [0, 16]], EQ, -15, 1)
     for j in (1, 2, 3):
         sel(A("RS", 128 * j - 128, 128 * j), A("BLK"), [[-1, 128]], EQ, -4 * j, 1)
         sel(A("RK", 128 * j - 128, 128 * j), A("S15b"), [[0, 8], [1, 16]], GEQ, 4 * j - 16, 0)
-
-    def late_consts():
-        sel(A("TRS"), A("BLK"), [[1, 128]], GT, 0, -1)
-        sel(A("LT8"), A("BLK"), [[16, 8], [0, 16]], GEQ, 7, -1)
-        sel(A("BK1"), A("BLK"), [[0, 8], [1, 16]], GT, 0, 0)
-        sel(A("BK1f"), A("BLKf"), [[0, 8], [1, 16]], GT, 0, 0)
-        sel(A("SHf"), A("BK1f"), [[-1, 128]], EQ, 1, 1)
-        for j in range(4):
-            sel(A("SH", 128 * j, 128 * j + 128), A("BK1"), [[-1, 128]], EQ, 1 - j, 1)
-            for k in range(17 - j, 16):
-                col = A("SH", 128 * j + k, 128 * j + 128, 16)
-                sel(col, col, [[-16, 8]], NE, -15, 1, 1.0)
-        for j in range(3): iota(A("R4", TM * j + T0, TM * j + TM), [[0, TM - T0]])
-        iota(A("LN", P, 2 * P), [[1, P]])
-        iota(A("LN", 0, P), [[1, 3], [3, 5], [15, 16]])
-        iota(A("BIG", W1 + P, W2), [[0, W2 - W1 - P]])
-        ts(A("E0"), A("ID"), R0c, MUL)
-
-    def tables_a():
-        iota(A("RK2"), [[0, P]], 2 ** 24 - 1)
-        sel(A("RST"), A("RK2"), [[0, 15], [1, 16]], EQ, 0, 0)
-        ts(A("BGM"), A("C16", 0, 160), Kp, NE, 2.0 ** 23, MUL)
-        ts(C("WKi", 0), C("WK", 0), 4032, AND); ts(C("WKi", 1), C("WK", 0), 63, AND)
-        cp(C("WKf", 2), C("WK", 1))
-        cp(A("WKf", 0, 2), A("WKi", 0, 2))
-        ts(A("WH"), A("BLK"), C("WKf", 0), MUL); ts(A("WL"), A("BLK"), C("WKf", 1), MUL)
-
-    def tables_b():
-        cp(A("BLKf"), A("BLK"))
-        ts(A("RK2"), A("MT"), Kp, EQ, C("WKf", 2), MUL)
-        cp(A("TCf", 0, 2, p=(0, 8)), A("TC", 0, 2, p=(0, 8)))
-        mm(A("pb6", 0, 240), A("BLKf"), A("RK2"), True, True)
-        mm(A("pb6", 240, 242), A("G8", p=(0, 8)), A("TCf", 0, 2, p=(0, 8)), True, True)
-
-    def tables_c():
-        cp(A("KT"), A("pb6", 0, 80, 5))
-        tt(A("PAY"), A("pb6", 0, 240), A("PBS"), ADD)
-        ts(C("TH", 0), A("pb6", 240, 241), 32768.0, MUL, float(KOFF), ADD)
-        ts(C("TH", 4), C("TH", 0), -1.0, MUL, 1.0, ADD); ts(C("TH", 3), C("TH", 4), 8192.0, MUL)
-        cp(C("TH", 1), A("pb6", 241, 242)); ts(C("TH", 2), A("pb6", 241, 242), -1.0, MUL)
-
-    def tables_d():
-        S15 = lambda n: A(n, 0, 15)
-        ts(A("LOC", 0, 10), A("SL", 0, 10), 1280.0, ADD); ts(A("LOC", 10, 15), A("SL", 10, 15), -160.0, ADD)
-        ms(A("STR", 0, 10), 160.0); ms(A("STR", 10, 15), 80.0)
-        ts(S15("i0"), S15("SL"), 1.0 / 15, MUL, -0.47, ADD)
-        ts(S15("DU"), S15("LC"), P15, SUB)
-        act(S15("NFL"), S15("NFL"), AF.Identity, bias=P15)
-        ts(S15("s1"), S15("i0"), -15.0, MUL); cp(S15("s4"), S15("i0"))
-        tt(S15("s1"), S15("s1"), S15("SL"), ADD)
-        ts(S15("i0"), S15("s1"), 1.0 / 3, MUL, -0.34, ADD)
-        ts(S15("s1"), S15("s1"), 80.0, MUL)
-        ts(S15("s2"), S15("i0"), -224.0, MUL)
-        tt(S15("s1"), S15("s1"), S15("s4"), ADD)
-        tt(S15("s1"), S15("s1"), S15("s2"), ADD)
-        cp(S15("NBu"), S15("s1"))
+        mm(A("pb7", 0, 128), A("ID"), A("RS", 128 * j - 128, 128 * j), True, False)
+        mm(A("pb7", 0, 128), A("ID"), A("RK", 128 * j - 128, 128 * j), False, True)
+        act(A("RT", 128 * j - 128, 128 * j), A("pb7", 0, 128), AF.Copy)
+    act(A("BLKf"), A("BLK"), AF.Copy)
+    sel(A("UPI"), A("BLK"), [[-1, 128]], GEQ, 0, 1)
+    sel(A("GE8"), A("BLK"), [[-16, 8], [0, 16]], GEQ, -8, 1)
+    sel(A("BK1"), A("BLK"), [[0, 8], [1, 16]], GT, 0, 0)
+    sel(A("BK1f"), A("BLKf"), [[0, 8], [1, 16]], GT, 0, 0)
+    sel(A("SHf"), A("BK1f"), [[-1, 128]], EQ, 1, 1)
+    for j in range(4):
+        sel(A("SH", 128 * j, 128 * j + 128), A("BK1"), [[-1, 128]], EQ, 1 - j, 1)
+        for k in range(17 - j, 16):
+            col = A("SH", 128 * j + k, 128 * j + 128, 16)
+            sel(col, col, [[-16, 8]], NE, -15, 1, 1.0)
+    for j in range(3): iota(A("R4", TM * j + T0 + P, TM * j + TM), [[0, P]])
+    iota(A("LN", P, 2 * P), [[1, 3], [3, 80]])
+    iota(A("LN", 0, P), [[1, 3], [3, 5], [15, 16]])
+    ts(A("E0"), A("ID"), R0c, MUL)
+    ts(A("BGM"), A("C16"), Kp, NE, 2048.0, MUL)
+    ts(C("WKf", 0), C("WK", 0), 2048.0, GEQ); ts(C("WKf", 1), C("WK", 0), 2.0 ** -12, MUL)
+    cp(C("WKf", 2), C("WK", 1))
+    ts(C("WKf", 3), C("WKf", 1), C("WKf", 0), SUB)
+    ts(A("W16"), A("BLK"), C("WKf", 3), MUL)
+    ts(A("RK2"), A("MT"), Kp, EQ, C("WKf", 2), MUL)
+    cp(A("TCf", 0, 2, p=(0, 8)), A("TC", 0, 2, p=(0, 8)))
+    mm(A("pb5", 0, 80), A("BLKf"), A("RK2"), True, True)
+    mm(A("pb5", 80, 82), A("G8", p=(0, 8)), A("TCf", 0, 2, p=(0, 8)), True, True)
+    ts(A("KT"), A("pb5", 0, 80, 5), 4096.0, MUL)
+    tt(A("PAY"), A("pb5", 0, 80), A("PBS"), ADD)
+    ts(C("TH", 0), A("pb5", 80, 81), 32768.0, MUL, float(KOFF), ADD)
+    cp(C("TH", 1), A("pb5", 81, 82))
+    ts(C("TH", 4), C("TH", 0), -1.0, MUL, 1.0, ADD); ts(C("TH", 3), C("TH", 4), 8192.0, MUL)
+    act(S15("NFL"), S15("NFL"), AF.Identity, bias=P5)
+    act(S15("LOC"), S15("LOC"), AF.Identity, bias=Kp)
+    act(S15("IDX"), S15("T17"), AF.Identity, bias=P15)
+    ts(S15("i0"), S15("SL"), 1.0 / 15, MUL, -0.47, ADD)
+    ts(S15("y2"), S15("i0"), -15.0, MUL); cp(S15("s4"), S15("i0"))
+    tt(S15("y2"), S15("y2"), S15("SL"), ADD)
+    ts(S15("i0"), S15("y2"), 1.0 / 3, MUL, -0.34, ADD)
+    ts(S15("y2"), S15("y2"), 80.0, MUL)
+    ts(S15("y3"), S15("i0"), -224.0, MUL)
+    tt(S15("y2"), S15("y2"), S15("s4"), ADD)
+    tt(S15("y2"), S15("y2"), S15("y3"), ADD)
+    cp(S15("NBu"), S15("y2"))
+    for j in range(4): r4(j, A("R0", j, T0, 4), j, T0, 4, "pb7" if j % 2 else "pb3")
 
     def prep(t):
-        S15 = lambda n: A(n, 0, 15)
-        n1, a0, q0 = C("CN", 3 + 3 * t), C("CN", 4 + 3 * t), C("CN", 5 + 3 * t)
         if t == 0:
-            tt(n1, C("CN", 2), C("CN", 1), SUB); a0, q0 = C("CN", 1), C("CN", 2)
+            tt(C("CN", 3), C("CN", 2), C("CN", 1), SUB)
+            ts(A("msk"), A("LAN"), C("CN", 3), GEQ)
+            ts(A("s3"), A("LAN"), C("CN", 3), GEQ, C("CN", 2), MUL)
+            ts(A("s0"), A("LAN"), C("CN", 1), ADD, float(CI), ADD)
+            tt(A("bas"), A("s0"), A("s3"), SUB)
         else:
-            tt(n1, C("CN", 10), C("CN", 11), SUB)
-            ts(a0, C("CN", 11), C("CN", 3), ADD, float(W1), ADD); ts(q0, C("CN", 10), C("CN", 3), ADD, float(W1), ADD)
-        act(S15("bas"), S15("SL"), AF.Identity, bias=a0)
-        ts(S15("msk"), S15("SL"), n1, GEQ)
-        act(S15("s3"), S15("msk"), AF.Identity, scale=q0)
-        act(C("fT", 0), n1, AF.Identity, bias=1023.0)
-        tt(S15("bas"), S15("bas"), S15("s3"), SUB)
-
-    def res(t):
-        for c in range(3): cp(A("RES", 80 * c, 80 * c + 80), A("BIG", WIN[t] + c, WIN[t] + P, 3))
+            ts(A("msk"), A("LAN"), C("CN", 10), GEQ)
+            ts(A("s3"), A("LAN"), C("CN", 10), GEQ, float(CJ - CI), MUL)
+            ts(A("s0"), A("LAN"), C("CN", 10), SUB, float(CI), ADD)
+            tt(A("bas"), A("s0"), A("s3"), ADD)
 
     def keep(t):
-        mm(A("pb6", 0, P), A("E0"), A("LN", P, 2 * P), True, False)
-        mm(A("pb6", 0, P), A("SHf"), A("BIG", WIN[t], WIN[t] + P), False, True)
-        act(A("WT", 960, 1200), A("pb6", 0, P), AF.Identity, bias=Rm)
-        ts(C("Kp", 6 + t), R0c, float(NB + P * t - 1024), MUL, 1024.0, ADD)
+        cp(A("RESf"), A("RES"))
+        mm(A("pb7", 0, P), A("E0"), A("LN", P, 2 * P), True, False)
+        mm(A("pb7", 0, P), A("SHf"), A("RESf"), False, True)
+        act(A("WT", 960, 1200), A("pb7", 0, P), AF.Identity, bias=Rm)
 
-    def g2(t, ch):
-        lo, hi = 640 * ch, 640 * ch + 640
-        step = 320 if ch in SPLIT2 else 640
-        for a in range(lo, hi, step):
-            at(t, G2AT[ch] + (a - lo) / 640)
-            tt(A("D2", a, a + step), IN(A("X", 0, NB + P * t), A("RES", a // 16, (a + step) // 16)), A("ZR", a, a + step), SUB)
-            act(A("A2w", a, a + step), A("D2", a, a + step), AF.Relu, scale=-0.125)
-        c = ch // 2; bank, o = ("pb0", 80 * c) if c < 2 else ("pb1", 0)
-        if ch % 2 == 0:
-            mm(A(bank, o, o + 80), A("ID"), A("PA", 0, 80), True, False)
-            if c: mm(A(bank, o, o + 80), A("ID"), A("PBb", 80 * c, 80 * c + 80), False, False)
-        for p in range(8 * (ch % 2), 8 * (ch % 2) + 8):
-            mm(A(bank, o, o + 80), A("EW", 15 - p, 143 - p), A("A2w", 1280 * c + 80 * p, 1280 * c + 80 * p + 80), False, p == 15)
+    def step2(t, c):
+        bank = "pb%d" % c; o = 1280 * c; p = 0; n0 = 80 * c
+        cp(A("RES", n0, n0 + 80), IN(A("BIG", CI if t == 0 else 0, (R1, R1, CJ + P)[t]), A("LR", 6 * c, 6 * c + 5)))
+        for n in CH2[c]:
+            a, b = o + 80 * p, o + 80 * (p + n)
+            tt(A("D2", a, b), IN(A("X", 0, NB + P * t), A("RES", a // 16, b // 16)), A("ZR", a, b), SUB)
+            ops[-1]["wide"] = True
+            act(A("A2w", a, b), A("D2", a, b), AF.Relu, scale=-1.0 / 1024)
+            for r in range(p, p + n):
+                mm(A(bank, 0, 80), A("EW", 15 - r, 143 - r), A("A2w", o + 80 * r, o + 80 * r + 80), r == 0, r == 15, r > p)
+            p += n
+        scan(A("SC1", n0, n0 + 80), A(bank, 0, 80), A("PK1"), MIN, ADD, TOP)
+        scan(A("SC2", n0, n0 + 80), A(bank, 0, 80), A("PK2"), MIN, ADD, TOP)
+        tt(A("kf", 5 * c, 5 * c + 5), A("SC2", n0 + 15, n0 + 80, 16), A("SC1", n0 + 15, n0 + 80, 16), SUB)
+        cp(A("LY", 6 * c, 6 * c + 5), A("kf", 5 * c, 5 * c + 5))
+        y = A(YB(t), 1280, 1360) if c == 2 else A("YS", 160 * t + n0, 160 * t + n0 + 80)
+        act(y, IN(A("D2", o, o + 1280), A("LY", 6 * c, 6 * c + 5)), AF.Abs)
+        if c < 2: send(t, c)
 
-    def pick(t, own):
-        n, c0, bank = (80, 10, "pb1") if own else (160, 0, "pb0")
-        c1 = c0 + n // 16
-        scan(A("SC", 16 * c0, 16 * c1), A("RST", 0, n), A(bank, 0, n), ADD, MIN)
-        cp(A("k2", c0, c1), A("SC", 16 * c0 + 15, 16 * c1, 16))
-        ts(A("k2b", c0, c1), A("k2", c0, c1), 4095, AND)
-        ts(A("LY", c0, c1), A("k2b", c0, c1), P80, ADD)
-        act(A(YB(t), 640, 720) if own else A("YS", 160 * t, 160 * t + 160), IN(A("D2", 0, 3840 if own else 2560), A("LY", c0, c1)), AF.Abs)
+    def send(t, c):
+        dst = T.cores[(rank + 1 + (t + c) % (N - 1)) % N]
+        far = [e for e in topo.engines(core, dst) if all(e in topo.engines(core, d) for d in T.cores if d != core)]
+        rid, pid = topo.addr(dst, core); y = 160 * t + 80 * c
+        tr = RemoteDMATransfer(dst_ids=[DstId(rid=rid, pnc=pid)], dma_engine_mask=sum(1 << e for e in far), remote_sem=T.sem["arr%d%d" % (t, c)],
+                               src=T["YS"][:, y:y + 80], dst=T[YB(t)][:, 640 * c:640 * c + 80])
+        emit("G", "remote_dma_fused", [[tr]], {"local_sem": T.sem.sent}, kind="r", extra=([], [reg("YS", y, y + 80)]))
+        if t + c == 0: ops[-1]["cost"] = ("rem", 1800.0, 0)
+        ops.append(dict(cost=("arr", 0, 0), kind="arr", q="R%d%d" % (t, c), w=[reg(YB(t), 640 * c, 640 * c + 80)], r=[], n=len(far)))
 
-    def send(t):
-        tr = []
-        dst = [T.cores[(rank + 1 + (t + c) % (N - 1)) % N] for c in range(2)]
-        eng = [e for e in topo.engines(core, dst[0]) if e in topo.engines(core, dst[1])]
-        far = [e for e in eng if all(e in topo.engines(core, d) for d in T.cores if d != core)]
-        half = len(far) // 2
-        for c in range(2):
-            rid, pid = topo.addr(dst[c], core)
-            tr.append(RemoteDMATransfer(dst_ids=[DstId(rid=rid, pnc=pid)], dma_engine_mask=sum(1 << e for e in far[half * c:half * c + half]),
-                                        remote_sem=T.sem["arr%d" % t], src=T["YS"][:, 160 * t + 80 * c:160 * t + 80 * c + 80], dst=T[YB(t)][:, 80 * c:80 * c + 80]))
-        at(t, 5.9)
-        emit("G", "remote_dma_fused", [tr], {"local_sem": T.sem.sent}, kind="r", extra=([], [reg("YS", 160 * t, 160 * t + 160)]))
-        ops.append(dict(tag=None, cost=("arr", 0, 0), kind="arr", q="R%d" % t, w=[reg(YB(t), 0, 160)], r=[], n=2 * half))
-
-    def rep(t, own):
-        o, n = (640, 80) if own else (0, 160)
-        while n < 640:
+    def step4(t, c):
+        bank = "pb%d" % c; o = 640 * c; n0 = 80 * c; n = 80; s = 20 * c
+        while n < 80 * max(CH5[c]):
             act(A(YB(t), o + n, o + 2 * n), A(YB(t), o, o + n), AF.Copy); n *= 2
+        mm(A(bank, 0, 80), A("ID"), A("BGM"), True, False)
+        mm(A(bank, 0, 80), A("W16"), A(YB(t), o, o + 80), False, True)
+        scan(A("SU", n0, n0 + 80), A("RST"), A(bank, 0, 80), ADD, MIN)
+        raw = A("SU", n0 + 15, n0 + 80, 16); ri = A("ri", 5 * c, 5 * c + 5)
+        ts(ri, raw, -0.5, ADD)
+        tt(A("QD1", s, s + 20, 4), raw, ri, SUB); tt(A("QD0", s + 1, s + 20, 4), raw, ri, SUB)
+        scan(A("QS", s, s + 20), A("QD0", s, s + 20), A("QD1", s, s + 20), MUL, ADD)
+        for k in range(5): ts(A("Hi", n0 + k, n0 + 80, 5), A("KT"), C("QD1", s + 4 * k), MUL, C("QS", s + 4 * k + 3), ADD)
+        ts(A("Hj", n0, n0 + 80), A("Hi", n0, n0 + 80), 4095, AND)
+        cp(A("Hu", n0, n0 + 80), A("Hj", n0, n0 + 80))
 
-    def upe(t, own):
-        o, n = (640, 80) if own else (0, 160)
-        mm(A("pb2", 0, n), A("ID"), A("BGM", 0, n), True, False)
-        mm(A("pb2", 0, n), A("WH"), A(YB(t), o, o + n), False, False)
-        mm(A("pb2", 0, n), A("WL"), A(YB(t), o, o + n), False, True)
-
-    def u1(own):
-        n, c0 = (80, 10) if own else (160, 0); c1 = c0 + n // 16
-        scan(A("SU", 16 * c0, 16 * c1), A("RST", 0, n), A("pb2", 0, n), ADD, MIN)
-        cp(A("ui0", c0, c1), A("SU", 16 * c0 + 15, 16 * c1, 16))
-        ts(A("ui", c0, c1), A("ui0", c0, c1), 4095, AND)
-
-    def u2(own):
-        n, c0, h0 = (80, 10, 0) if own else (160, 0, 80); k = n // 16; c1 = c0 + k
-        tt(A("sq", c0, c1), A("ui", c0, c1), A("ui", c0, c1), MUL)
-        cp(A("uf", c0, c1), A("ui", c0, c1))
-        ts(A("qi", c0, c1), A("sq", c0, c1), 5, SHR)
-        cp(A("qf", c0, c1), A("qi", c0, c1))
-        for c in range(k): ts(A("Hi", h0 + c, h0 + n, k), A("KT"), C("uf", c0 + c), MUL, C("qf", c0 + c), ADD)
-        ts(A("Hj", h0, h0 + n), A("Hi", h0, h0 + n), 4095, AND)
-        cp(A("Hu", h0, h0 + n), A("Hj", h0, h0 + n))
-
-    def g5(t, ch):
-        lo, hi = 640 * ch, 640 * ch + 640; y = 640 if ch < 2 else 0
-        step = 320 if ch in SPLIT5 else 640
-        for a in range(lo, hi, step):
-            at(t, G5AT[ch] + (a - lo) / 640)
-            tt(A("D5", a, a + step), IN(A(XH(t)), A("Hu", a // 16, (a + step) // 16)), A(YB(t), y, y + step), SUB)
-            act(A("A5", a, a + step), A("D5", a, a + step), AF.Abs)
-        for a, b, out in ([], [(0, 1280, A("pb3", 0, 80))], [], [(1280, 2560, A("pb0", 0, 80))], [(lo, hi, A("pb1", 0, 40))],
-                          [(lo, lo + 320, A("pb4", 0, 20)), (lo + 320, hi, A("pb2", 0, 20))])[ch]:
-            mm(out, A("IDf"), A("PAY", a // 16, b // 16), True, False)
-            for r in range(16): mm(out, A("EW", 15 - r, 143 - r), A("A5", a + r, b, 16), False, r == 15)
-
-    def kown():
-        for c in range(5): emit("V", "tensor_reduce", [C("K", 10 + c), A("pb3", c, 80, 5), AxisListType.X, MIN])
-
-    def kfar():
-        cp(A("AC", 0, 80), A("pb0", 0, 80))
-        tt(A("AC", 80, 120), A("AC", 0, 40), A("AC", 40, 80), MIN)
-        tt(A("AC", 0, 40), A("pb1", 0, 40), A("AC", 80, 120), MIN)
-        tt(A("AC", 40, 60), A("AC", 0, 20), A("AC", 20, 40), MIN)
-        tt(A("AC", 60, 80), A("pb4", 0, 20), A("AC", 40, 60), MIN)
-        tt(A("AC", 120, 140), A("pb2", 0, 20), A("AC", 60, 80), MIN)
-        tt(A("K", 0, 10), A("AC", 120, 130), A("AC", 130, 140), MIN)
+    def step5(t, c, first, last):
+        bank = "pb%d" % c; o = 1280 * c; m = 0
+        for n in CH5[c]:
+            a, b = o + 80 * m, o + 80 * (m + n)
+            tt(A("D5", a, b), IN(A(XH(t)), A("Hu", a // 16, b // 16)), A(YB(t), 640 * c, 640 * c + 80 * n), SUB)
+            ops[-1]["wide"] = True
+            act(A("A5", a, b), A("D5", a, b), AF.Abs)
+            m += n
+        m = 0
+        for n in GR5[c]:
+            out = A(bank, 5 * m, 5 * (m + n))
+            mm(out, A("IDf"), A("PAY", 5 * m, 5 * (m + n)), True, False)
+            for r in range(16): mm(out, A("EW", 15 - r, 143 - r), A("A5", o + 80 * m + r, o + 80 * (m + n), 16), False, r == 15, r > 0)
+            m += n
+        for k in range(5): emit("V", "tensor_reduce", [C("K", 5 * c + k), A(bank, k, 80, 5), AxisListType.X, MIN])
+        ts(A("fw", c, 15, 3), A("K", 5 * c, 5 * c + 5), C("TH", 0), OP.is_lt, -1.0 if c == 2 else 1.0, MUL)
+        if first and t: mm(A("pb4", 0, 1), A("IDf"), C("Bp", 0), True, False)
+        for k in range(5): mm(A("pb4", 0, 1), A("TWO" if c == 2 else "ONE"), C("fw", 3 * k + c), first and k == 0 and t == 0, last and k == 4, k > 0)
 
     def close(t):
-        S15 = lambda n: A(n, 0, 15)
-        last = t == RO - 1; TT = T0 + P * t; lv = 16 * t
+        last = t == RO - 1; TT = T0 + P * t; lv = A("LV", 16 * t, 16 * t + 15)
+        act(S15("uf"), A("QD1", 0, 60, 4), AF.Copy, scale=4096.0)
         cp(S15("Ki"), S15("K"))
-        ts(A("fw", lv, lv + 10), A("K", 0, 10), C("TH", 0), OP.is_lt)
-        ts(A("fw", lv + 10, lv + 15), A("K", 10, 15), C("TH", 0), OP.is_lt, -2.0, MUL)
-        for u in range(t + 1): mm(A("pb2", 0, 15), A("ONE"), A("fw", 16 * u, 16 * u + 15), u == 0, u == t)
         ts(S15("kp"), S15("Ki"), 2047, AND)
         act(S15("nf"), S15("K"), AF.Relu, bias=C("TH", 3), scale=8192.0)
-        tt(S15("t1"), S15("kp"), S15("ui"), MUL)
+        tt(S15("t1"), S15("kp"), S15("uf"), MUL)
         ts(S15("mi"), S15("Ki"), 11, SHR, 15, AND)
-        tt(S15("t2"), S15("t1"), S15("qi"), ADD)
-        emit("V", "tensor_reduce", [C("dB", 0), A("pb2", 0, 15), AxisListType.X, ADD])
-        ts(S15("hh"), S15("t2"), 4095, AND)
-        ts(S15("a12"), S15("t2"), 12, AND)
-        ts(C("dB", 1), C("dB", 0), C("TH", 1), GT, -1.0, MUL)
-        ts(C("dB", 2), C("dB", 0), C("TH", 2), OP.is_lt, 0.5, MUL)
-        ts(S15("x1"), S15("hh"), TT / 4096.0, MUL, -255.0 / 512, ADD)
-        ts(S15("x2"), S15("a12"), TM / 4.0, MUL)
-        for c in range(3): act(A("LV", lv + c, lv + 15, 3), A("fw", lv + 5 * c, lv + 5 * c + 5), AF.Identity, bias=1.0, scale=C("dB", 1 if c < 2 else 2))
-        tt(S15("ix"), S15("x1"), S15("x2"), ADD)
+        tt(S15("t2"), S15("t1"), A("QS", 3, 60, 4), ADD)
+        ts(lv, S15("fw"), A("pb4", 0, 1), MUL, C("TH", 1), OP.is_le)
+        if t == 0:
+            ts(S15("hh"), S15("t2"), 2, SHR, 1023, AND)
+            cp(S15("L1"), S15("hh"))
+        else:
+            ts(S15("hh"), S15("t2"), 4095, AND)
+            ts(S15("a12"), S15("t2"), 12, AND)
+            ts(S15("x1"), S15("hh"), TT / 4096.0, MUL, -255.0 / 512, ADD)
+            ts(S15("x2"), S15("a12"), TM / 4.0, MUL)
+            tt(S15("ix"), S15("x1"), S15("x2"), ADD)
+            cp(S15("L1"), S15("ix"))
         ts(S15("a3"), S15("t2"), 3, AND)
-        cp(S15("L1"), S15("ix"))
         if not last:
-            scan(S15("cum"), A("ONEs", 0, 15), A("LV", lv, lv + 15), MUL, ADD)
-        cp(A("RC"), IN(A("R4", 0, 3 * TM + TT), S15("L1")))
-        if not last:
-            mm(A("pb2", 0, 1), A("TRS"), C("cum", 14), True, True)
-            mm(A("pb2", 1, 2), A("BLK"), C("cum", 14), True, True)
-            if t == 0: mm(A("pb2", 2, 3), A("LT8"), C("cum", 14), True, True)
+            ts(S15("dead"), S15("fw"), A("pb4", 0, 1), MUL, C("TH", 1), GT)
+            cp(C("Bp", 0), A("pb4", 0, 1))
+            scan(S15("cum"), A("ONEs", 0, 15), lv, MUL, ADD)
+            tt(S15("e1"), S15("dead"), S15("IDX"), MUL)
+            mm(A("pb4", 0, 1), A("UPI"), C("cum", 14), True, True)
+            mm(A("pb4", 1, 2), A("BLK"), C("cum", 14), True, True)
+            if t == 0: mm(A("pb4", 2, 3), A("GE8"), C("cum", 14), True, True)
+            tt(S15("e3"), S15("cum"), S15("e1"), SUB)
+            for c in range(3): ts(A("LP", 5 * c, 5 * c + 5), A("e3", c, 15, 3), A("pb4", 0, 1), SUB, P - 1.0, ADD)
+            ts(A("pf1"), A("msk"), A("pb4", 1, 2), MUL)
+            if t == 0: cp(C("CN", 10), A("pb4", 2, 3))
+            tt(A("pf2"), A("bas"), A("pf1"), SUB)
+            cp(A("LR"), A("pf2"))
+        cp(A("RC"), IN(A("R4", 0, 3 * TM + TT) if t else A("R0"), S15("L1")))
         for j in range(4):
-            out = A(("pb3", "pb4", "pb0", "pb7")[j], 0, P)
+            out = A("pb%d" % j, 0, P)
             mm(out, A("E0"), A("LN", 0, P), True, False)
             mm(out, A("SH", 128 * j, 128 * j + 128), A("RC"), False, True)
-            if j >= (2 if last else WV): cp(A("WT", P * j, P * j + P), out)
+            if j % 2: cp(A("WT", P * j, P * j + P), out)
             else: act(A("WT", P * j, P * j + P), out, AF.Copy)
-        tt(S15("y3"), S15("mi"), S15("STR"), MUL)
+        ts(S15("y3"), S15("mi"), 80.0, MUL)
         tt(S15("g3"), S15("nf"), S15("LOC"), ADD)
         ts(S15("y2"), S15("a3"), 240.0, MUL)
         tt(S15("g2"), S15("nf"), S15("SL"), ADD)
@@ -558,86 +555,39 @@ def rank_program(g, core, T, topo):
         ts(S15("L3"), S15("z3"), 3840.0, MIN)
         tt(S15("w2"), S15("z2"), S15("NFL"), MIN)
         act(A("EE"), IN(A("D5"), S15("L3")), AF.Identity, bias=191.75, scale=0.5)
-        if not last:
-            act(S15("e1"), A("LV", lv, lv + 15), AF.Identity, bias=C("fT", 0), scale=-1024.0)
-            ts(S15("pf1"), S15("msk"), A("pb2", 1, 2), MUL)
         cp(S15("L2"), S15("w2"))
-        if not last:
-            tt(S15("e2"), S15("e1"), S15("DU"), MIN)
-            tt(S15("pf2"), S15("bas"), S15("pf1"), SUB)
-            tt(S15("e3"), S15("e2"), S15("cum"), ADD)
-            cp(S15("LF"), S15("pf2"))
-            for c in range(3): ts(A("LP", 5 * c, 5 * c + 5), A("e3", c, 15, 3), A("pb2", 0, 1), ADD)
-            if t == 0: cp(A("CN", 10, 12), A("pb2", 1, 3))
-            w = WIN[t + 1]
-            act(A("BIG", w, w + P), IN(A("BIG", 0, T0 if t == 0 else w), S15("LF")), AF.Copy)
-        ts(A("NEW"), IN(A("WT"), S15("L2")), C("Kp", 6 + t), ADD)
-        if not last: cp(IN(A("BIG", w, w + 600), S15("LP")), A("NEW"))
+        ts(A("NEW"), IN(A("WT"), S15("L2")), C("Kp", 8 + t), ADD)
+        if not last: cp(IN(A("BIG", R1 * t, R1 * t + P), S15("LP")), A("NEW"))
         act(A("YT", P * t, P * t + P), IN(A("NEW"), S15("NBu")), AF.Copy)
         for c in range(15):
-            out = A("pb1", 3 * (c % 5) + c // 5, P, 15); y = 16 * c + (480 if c >= 10 else 0)
-            mm(out, A("ID"), A(YB(t), y, y + 16), True, False)
-            mm(out, A("ID"), A("EE", 16 * c, 16 * c + 16), False, True)
-        act(A("X", NB + P * t, NB + P * t + P), A("pb1", 0, P), AF.Identity, bias=-192.0)
-        at(t, 22.0); store("Y", T.ya[:, P * t:P * t + P], A("LV", lv, lv + 15))
-        at(t, 22.0); store("Y", T.yx[:, P * t:P * t + P], A("X", NB + P * t, NB + P * t + P))
-        at(t, 22.0); store("Y", T.yt[:, P * t:P * t + P], A("YT", P * t, P * t + P))
+            out = A("pb5", 3 * (c % 5) + c // 5, P, 15); y = 640 * (c // 5) + 16 * (c % 5)
+            mm(out, A("ID"), A(YB(t), y, y + 16), True, False, c % 3 > 0)
+            mm(out, A("ID"), A("EE", 16 * c, 16 * c + 16), False, True, True)
+        act(A("X", NB + P * t, NB + P * t + P), A("pb5", 0, P), AF.Identity, bias=-192.0)
+        store("Y", T.ya[:, P * t:P * t + P], lv)
+        store("Y", T.yx[:, P * t:P * t + P], A("X", NB + P * t, NB + P * t + P))
+        store("Y", T.yt[:, P * t:P * t + P], A("YT", P * t, P * t + P))
 
     OLD = (None, 12, 26)
     for t in range(RO):
         TT = T0 + P * t; nx = t + 1 < RO
-        res(t)
-        if t == 0: bhc(0, 0, 256)
-        g2(t, 0)
         if t:
             ts(A("Rh", TT - P, TT), A("YT", P * t - P, P * t), -1024.0, ADD)
             bh(t, OLD[t], 256 // PLANS[t][0])
-        else:
-            xh(0, 0, 64, NB); tables_a()
-        g2(t, 1)
-        if t == 0: xh(0, 64, 96, NB)
-        g2(t, 2)
-        if t: bhc(t, OLD[t] * PLANS[t][0], 256)
-        else: xh(0, 96, 128, NB); tables_b()
-        g2(t, 3); g2(t, 4)
-        pick(t, False); send(t)
-        if t: xh(t, OLD[t] * PLANS[t][0], 256, NB + P * t)
-        g2(t, 5)
-        if t == 0:
-            late_consts(); xh(0, 128, 192, NB); tables_c(); tables_d()
-            for j in range(4, 14): mask(j)
-        if nx: prep(t)
-        pick(t, True)
-        upe(t, True); rep(t, True)
-        if t == 0:
-            xh(0, 192, 256, NB)
-            for j in range(14, 22): mask(j)
-        u1(True); u2(True)
-        if t:
-            for j in range(4): r4(j, TT - P, TT, "pb6" if j % 2 else "pb7")
-        keep(t)
-        g5(t, 0)
-        upe(t, False); rep(t, False)
-        u1(False)
-        g5(t, 1)
-        u2(False)
-        if t == 0:
-            for j in range(22, 31): mask(j)
-        if nx: bh(t + 1, 0, OLD[t + 1])
-        for ch in range(2, 6):
-            g5(t, ch)
-            if t == 0:
-                r4(ch - 2, 0, 512, "pb6"); r4(ch - 2, 512, 1024, "pb7")
-            if ch == 3:
-                kown()
-                if nx: bhc(t + 1, 0, OLD[t + 1] * PLANS[t + 1][0])
-        if t == 0:
-            for j in range(31, len(SPANS)): mask(j)
-        kfar()
-        if nx: xh(t + 1, 0, 64, NB + P * t)
-        close(t)
+            xh(t, OLD[t] * PLANS[t][0], 256, NB + P * t)
+        for c in ORD2: step2(t, c)
         if nx:
-            xh(t + 1, 64, OLD[t + 1] * PLANS[t + 1][0], NB + P * t)
+            prep(t)
+            bh(t + 1, 0, OLD[t + 1])
+            xh(t + 1, 0, OLD[t + 1] * PLANS[t + 1][0], NB + P * t)
+        if t == 1:
+            for j in range(8): r4(j // 2, A("R4", TM * (j // 2) + 512 * (j % 2), TM * (j // 2) + 512 * (j % 2) + 512), 512 * (j % 2), 512 * (j % 2) + 512, 1, "pb7" if j % 2 else "pb3")
+        if t:
+            for j in range(4): r4(j, A("R4", TM * j + TT - P, TM * j + TT), TT - P, TT, 1, "pb7" if j % 2 else "pb3")
+        keep(t)
+        for c in ORD5: step4(t, c)
+        for c in ORD5: step5(t, c, c == ORD5[0], c == ORD5[2])
+        close(t)
 
     seen = {}; bank = {}
     for n, o in enumerate(ops):
@@ -661,6 +611,7 @@ def rank_program(g, core, T, topo):
         if o["kind"] == "arr": deps = set(); soft = {n - 1}
         if o["kind"] == "d" and o["w"]:
             soft.update(m for m in range(n) if ops[m]["kind"] == "d" and ops[m]["q"] == o["q"])
+        if "wide" in o: soft.update([m for m in range(n) if "wide" in ops[m]][-1:])
         o["deps"] = sorted(deps); o["soft"] = sorted(soft)
     if not ORDER: ORDER.extend(_schedule(ops))
     pos = {m: n for n, m in enumerate(ORDER)}
@@ -689,6 +640,7 @@ def rank_program(g, core, T, topo):
                 "transpose": lambda: q.transpose, "activation": lambda: q.activation, "matmul": lambda: q.matmul, "iota": lambda: q.iota,
                 "affine_select": lambda: q.affine_select, "dma_start": lambda: q.dma_start, "remote_dma_fused": lambda: q.remote_dma_fused}[o["fn"]]()
         ins = call(*o["a"], **o["k"])
+        for a in o.get("more", []): ins = call(*a)
         if o["kind"] == "d":
             s = T.sem[DMAS[nd]]; nd += 1; ins.then_inc(s, 16); o["at"] = (s, 16)
             if not o.get("sig"): tail.append(o["at"])

@@ -29,19 +29,19 @@ for _p in PLANS:
         if _x[2:] not in SPANS: SPANS.append(_x[2:])
 
 _S = dict(
-    X=(2768, B), Ri=(1024, I), Z=(240, B), Zp=(240, B), Lt=(64, I), Lb=(64, B), Lz=(72, B), rho=(64, F), A1=(64, F), A2=(64, F), e0=(64, F), p0u=(64, U),
-    BIG=(1744, F), Rh=(TM, H), R0=(1024, F), R4=(4 * TM, F), ZR=(3840, B), D2=(3840, B), A2w=(3840, B), D5=(3856, B), A5=(3840, B),
-    XHa=(4096, B), XHb=(4096, B), BHa=(256, U), BHb=(256, U), RES=(240, U), RESf=(240, F), WT=(1200, F), RC=(240, H), NEW=(240, F), YT=(720, F),
-    YS=(480, B), YB0=(1920, B), YB1=(1920, B), YB2=(1920, B), EE=(240, B), LN=(480, B), E0=(128, B), LV=(48, F),
+    X=(2768, B), Ri=(1024, I), Z=(240, B), Zp=(240, B), Lt=(64, I), Lb=(64, B), Lz=(72, B), rho=(64, F), A1=(64, F), A2=(64, F), e0=(64, F), p0u=(64, U), IDu=(32, U),
+    BIG=(1744, F), Rh=(TM, H), R0=(1024, F), R4=(4 * TM, F), ZR=(3840, B), D2=(3840, B), A2w=(3840, B), D5=(3840, B), A5=(3840, B),
+    XHa=(4336, B), XHb=(4336, B), BHa=(256, U), BHb=(256, U), RES=(240, U), RESh=(240, H), WT=(1200, F), RC=(240, H), NEW=(240, F), YT=(720, F),
+    YS=(480, B), YB0=(1920, B), YB1=(1920, B), YB2=(1920, B), EE=(240, B), EF=(240, B), LN=(480, B), E0=(128, B), LV=(48, F),
     ONE=(128, B), TWO=(128, B), ONEf=(128, F), BLK=(128, B), BLKt=(128, B), BLKf=(128, F), EW=(144, B), TRI=(128, B), UP=(128, B), UPI=(128, B), GE8=(128, B),
-    S7=(128, F), S15=(128, F), S15b=(128, B), ID=(128, B), IDf=(128, F), G8=(128, F), G8t=(128, F), BK1=(128, B), BK1f=(128, F), SH=(512, B), SHf=(128, F),
+    S7=(128, F), S15=(128, F), S15b=(128, B), ID=(128, B), NID=(128, B), IDf=(128, F), G8=(128, F), G8t=(128, F), BK1=(128, B), SH=(512, B),
     RS=(384, B), RK=(384, B), RT=(384, B), MK=(128 * len(SPANS), B), W16=(128, H),
-    Ki0=(2, I), Kp=(16, F), T17=(18, F), GE=(18, F), LTt=(18, F), C16=(80, F), BGM=(80, B), RST=(80, F), PK1=(80, F), PK2=(80, F),
+    Ki0=(2, I), Kp=(16, F), T17=(18, F), GE=(18, F), LTt=(18, F), C16=(80, F), BGM=(80, B), RST=(160, F), PK1=(80, F), PK2=(80, F),
     MT=(80, F), PBS=(80, F), RK2=(80, F), PAY=(80, F), KT=(16, F), WK=(4, I), WKf=(4, F),
     TC=(4, I), TCf=(4, F), TH=(8, F), CN=(16, F), SL=(16, F), IDX=(16, F), NFL=(16, F), LOC=(16, F), LAN=(18, F),
     s0=(18, F), s1=(18, F), s2=(18, F), s3=(18, F), s4=(16, F), i0=(16, I), NBu=(16, U), LR=(18, U),
     SC1=(240, F), SC2=(240, F), SU=(240, F), kf=(16, F), LY=(18, U), ri=(16, I), QD0=(60, F), QD1=(60, F), QS=(60, F), uf=(16, F),
-    Hi=(240, I), Hj=(240, I), Hu=(240, U), K=(16, F), Ki=(16, I), nf=(16, F), fw=(16, B), kp=(16, I), mi=(16, I),
+    Hi=(240, I), Hj=(240, I), Hu=(240, U), K=(16, F), Ki=(16, I), nf=(16, F), fw=(16, B), kp=(16, I),
     t1=(16, F), t2=(16, I), hh=(16, I), a12=(16, I), a3=(16, I), x1=(16, F), x2=(16, F), ix=(16, F), L1=(16, U), L2=(16, U), L3=(16, U),
     g2=(16, F), g3=(16, F), y2=(16, F), y3=(16, F), z2=(16, F), z3=(16, F), w2=(16, F), Bp=(2, F), cum=(16, B), dead=(16, F), e1=(16, F), e3=(16, F),
     LP=(16, U), msk=(18, F), bas=(18, F), pf1=(18, F), pf2=(18, F), ONEs=(64, F),
@@ -62,14 +62,18 @@ ORDER = []
 PACE = [dict(cy=0.83, pe=0.42, ga=1.56, sc=3.8, lat=170, dma=1500, bw=200.0, rem=2500),
         dict(cy=1.15, pe=0.6, ga=1.8, sc=5.0, lat=200, dma=2200, bw=160.0, rem=3500)]
 WEIGHT = (1.0, 1.45)
-TRIES, PASSES, JIT, MOVES, HEAT, SIDE, SEED = 10, 3, 1500.0, 60000, 800.0, 0.3, 12345
-XC = 16
-CH2 = ((8, 4, 4), (8, 4, 4), (8, 4, 4))
-CH5 = ((8, 8), (8, 8), (8, 6, 2))
+SHIFTS, MOVES, MIX, HEAT, SIDE, SEED = 200, (22000, 22000, 22000, 8000), 0.0, 300.0, 0.3, 12345
+TT16, AND16, GCAST = True, False, True
+XC = 24
+CH2 = (((8, 4, 4), (8, 4, 4), (8, 4, 4)),) * 3
+CH5 = (((4, 4, 4, 4), (8, 8), (8, 6, 2)),) * 3
 GR5 = ((16,), (16,), (8, 8))
-ORD2 = (0, 1, 2)
-ORD5 = (0, 1, 2)
+GR4 = ((0,), (1,), (2,))
+SP5 = (((1, 1),), ((1, 1),), ((1, 0), (1, 1)))
+REPG = 320
 XV = ((192, 256), (0, 0), (0, 0))
+DONE = (0, 0, 0)
+RCV, WTV = 8, (1, 3)
 
 
 def _times(ops, p):
@@ -85,7 +89,7 @@ def _times(ops, p):
     return out
 
 
-def _replay(G, order, p, lo, old):
+def _replay(G, order, p, lo, hi, old):
     qs, deps = G; d0, d1 = p["d0"], p["d1"]
     fin, end, by = (old[0][:], old[1][:], old[2][:]) if lo else ([0.0] * len(qs), [0.0] * len(qs), [-1] * len(qs))
     last = [-1] * 12; free = [0.0] * 12; j = lo; left = 5
@@ -93,7 +97,7 @@ def _replay(G, order, p, lo, old):
         j -= 1; n = order[j]; q = qs[n]
         if last[q] < 0:
             last[q] = n; free[q] = fin[n]; left -= q < 5
-    for n in order[lo:]:
+    for n in order[lo:hi]:
         q = qs[n]; t = free[q]; w = last[q]
         for m in deps[n]:
             if end[m] > t: t = end[m]; w = m
@@ -116,7 +120,7 @@ def _place(ops, tm, edges, key):
 
 
 def _schedule(ops):
-    n = len(ops); best = None; x = SEED; names = ["V", "S", "P", "G", "Y"]; anc = [0] * n; deps = []
+    n = len(ops); x = [SEED]; names = ["V", "S", "P", "G", "Y"]; anc = [0] * n; deps = []
     for i, o in enumerate(ops):
         if o["q"] not in names: names.append(o["q"])
         d = o["deps"] + ([i - 1] if o["kind"] == "arr" else []); up = 0
@@ -124,69 +128,94 @@ def _schedule(ops):
         deps.append([m for m in d if not up >> m & 1])
         for m in d: up |= 1 << m
         anc[i] = up
-    G = ([names.index(o["q"]) for o in ops], deps)
+    qs = [names.index(o["q"]) for o in ops]; G = (qs, deps)
     for q in PACE:
         tm = _times(ops, q); q["d0"] = [a for a, b in tm]; q["d1"] = [b + q["lat"] * (o["kind"] != "r") for (a, b), o in zip(tm, ops)]
-    p = PACE[0]; tm = _times(ops, p); fw = [[] for _ in ops]; bw = [[] for _ in ops]; on = [[] for _ in ops]
+    p = PACE[0]; tm = _times(ops, p); d0 = p["d0"]; fw = [[] for _ in ops]; on = [[] for _ in ops]
     for i, o in enumerate(ops):
         for m, lat in [(m, p["lat"]) for m in deps[i]] + [(m, tm[m][0] - tm[m][1]) for m in o["soft"]]:
-            fw[i].append((m, tm[m][1] + lat)); bw[m].append((i, max(tm[i][0], 1.0) + tm[m][1] - max(tm[m][0], 1.0) + lat)); on[m].append((i, tm[m][1] + lat))
-    marks = [i for i, o in enumerate(ops) if "wide" in o]
-    value = lambda st: sum((max(s[1]) + SIDE * sum(s[1][i] for i in marks) / len(marks)) / w for s, w in zip(st, WEIGHT))
-    for k in range(TRIES):
-        late = [0.0] * n
-        for i in range(n - 1, -1, -1):
-            x = (x * 1103515245 + 12345) % 2 ** 31
-            late[i] = max([tm[i][1]] + [late[j] + lag for j, lag in on[i]]) + 1e-3 + (x / 2 ** 31) ** 8 * JIT * (k > 0)
-        for _ in range(PASSES):
-            s = _place(ops, tm, fw, lambda i: (-late[i], i))
-            order = sorted(range(n), key=lambda i: (s[i], i))
-            st = [_replay(G, order, q, 0, None) for q in PACE]; v = value(st)
-            if best is None or v < best[0]: best = (v, order, st)
-            e = [s[i] + max(tm[i][0], 1.0) for i in range(n)]
-            r = _place(ops, tm, bw, lambda i: (-e[i], -i))
-            late = [r[i] + max(tm[i][0], 1.0) for i in range(n)]
-    pre = [set(m for m, _ in fw[i]) for i in range(n)]; qs = G[0]
-    cur = best; pos = None
-    for k in range(MOVES):
+            fw[i].append((m, tm[m][1] + lat)); on[m].append((i, tm[m][1] + lat))
+    pre = [set(m for m, _ in fw[i]) for i in range(n)]
+    wide = [i for i, o in enumerate(ops) if "wide" in o]; gates = [i for i, o in enumerate(ops) if o.get("gate")]
+    names = sorted(set(o["tag"] for o in ops)); tag = [names.index(o["tag"]) for o in ops]
+
+    def draw(k):
         u = []
-        for _ in range(6):
-            x = (x * 1103515245 + 12345) % 2 ** 31; u.append(x / 2 ** 31)
-        order = cur[1]
-        if pos is None:
-            pos = {m: j for j, m in enumerate(order)}; ways = {}
-        w = (int(u[4] * len(PACE)), marks[int(u[5] * 2 * len(marks))] if u[5] < 0.5 else -1)
-        if w not in ways:
-            fin, end, by = cur[2][w[0]]; j = w[1] if w[1] >= 0 else end.index(max(end)); ways[w] = []
-            while by[j] >= 0:
-                if by[j] not in pre[j]: ways[w].append((by[j], j))
-                j = by[j]
-        pairs = ways[w]
-        if not pairs: continue
-        a, b = pairs[int(u[0] * (len(pairs) if w[1] < 0 else min(len(pairs), 30)))]; lo, hi = pos[a], pos[b]; hop = int(1 + 12 * u[2] ** 3)
-        if u[1] < 0.5:
-            while hop > 1 and lo > 0:
-                lo -= 1; hop -= qs[order[lo]] == qs[b]
-            part = order[lo:hi + 1]; move = {b}
-            need = set(pre[b])
-            for j in reversed(part):
-                if j in need: move.add(j); need |= pre[j]
-            new = [j for j in part if j in move] + [j for j in part if j not in move]
+        for _ in range(k):
+            x[0] = (x[0] * 1103515245 + 12345) % 2 ** 31; u.append(x[0] / 2 ** 31)
+        return u
+
+    def value(st, goal, marks):
+        return sum(((max(s[1]) if goal < 0 else s[1][goal]) + SIDE * sum(s[1][i] for i in marks) / len(marks)) / w for s, w in zip(st, WEIGHT))
+
+    def fill(key, up):
+        if up:
+            for i in range(n - 1, -1, -1):
+                for m, _ in fw[i]:
+                    if key[m] >= key[i]: key[m] = key[i] - 1e-3
         else:
-            while hop > 1 and hi < n - 1:
-                hi += 1; hop -= qs[order[hi]] == qs[a]
-            part = order[lo:hi + 1]; move = {a}
-            for j in part:
-                if pre[j] & move: move.add(j)
-            new = [j for j in part if j not in move] + [j for j in part if j in move]
-        if new == part: continue
-        order = order[:lo] + new + order[hi + 1:]
-        st = [_replay(G, order, q, lo, s) for q, s in zip(PACE, cur[2])]; v = value(st)
-        if v < cur[0] + HEAT * u[3] ** 2 * (1.0 - k / MOVES):
-            d0 = p["d0"]; fin = st[0][0]; at = {m: j for j, m in enumerate(order)}
-            order.sort(key=lambda j: (fin[j] - d0[j], at[j]))
-            cur = (v, order, st); pos = None
-            if v < best[0]: best = cur
+            for i in range(n):
+                for m, _ in fw[i]:
+                    if key[m] >= key[i]: key[i] = key[m] + 1e-3
+        s = _place(ops, tm, fw, lambda i: (key[i], i))
+        order = sorted(range(n), key=lambda i: (s[i], key[i], i))
+        return order, [_replay(G, order, q, 0, n, None) for q in PACE]
+
+    late = [0.0] * n; best = cur = None
+    for i in range(n - 1, -1, -1): late[i] = max([tm[i][1]] + [late[j] + lag for j, lag in on[i]]) + 1e-3
+    for k in range(SHIFTS):
+        u = draw(4); off = list(cur[1]) if cur else [0.0] * len(names)
+        if cur: off[int(u[0] * len(names))] += (u[1] - 0.5) * 8000 * u[2] ** 2
+        order, st = fill([-late[i] - off[tag[i]] for i in range(n)], True); v = value(st, -1, wide)
+        if cur is None or v < cur[0] + HEAT * u[3] ** 2 * (1.0 - k / SHIFTS): cur = (v, off)
+        if best is None or v < best[0]: best = (v, order, st)
+    for stage, moves in enumerate(MOVES):
+        goal = gates[stage] if stage < len(gates) else -1; first = gates[stage - 1] if 0 < stage <= len(gates) else 0
+        marks = [i for i in wide if first <= i and (goal < 0 or i < goal)]
+        st = [_replay(G, best[1], q, 0, n, None) for q in PACE]
+        cur = best = (value(st, goal, marks), best[1], st); pos = None
+        for k in range(moves):
+            u = draw(6); order = cur[1]; heat = HEAT * u[3] ** 2 * (1.0 - k / moves)
+            if pos is None:
+                pos = {m: j for j, m in enumerate(order)}; ways = {}; cut = pos[goal] + 1 if goal >= 0 else n
+            if u[3] < MIX and first == 0 and goal < 0:
+                g = int(u[0] * len(names)); d = (u[1] - 0.5) * 8000 * u[2] ** 2; fin = cur[2][0][0]
+                order, st = fill([fin[i] - d0[i] + d * (tag[i] == g) for i in range(n)], d < 0); v = value(st, goal, marks)
+                if v < cur[0] + heat:
+                    cur = (v, order, st); pos = None
+                    if v < best[0]: best = cur
+                continue
+            w = (int(u[4] * len(PACE)), marks[int(u[5] * 2 * len(marks))] if u[5] < 0.5 else goal)
+            if w not in ways:
+                fin, end, by = cur[2][w[0]]; j = w[1] if w[1] >= 0 else end.index(max(end)); ways[w] = []
+                while by[j] >= 0 and pos[j] > pos[first] - 40:
+                    if by[j] not in pre[j]: ways[w].append((by[j], j))
+                    j = by[j]
+            pairs = ways[w]
+            if not pairs: continue
+            a, b = pairs[int(u[0] * (len(pairs) if w[1] == goal else min(len(pairs), 30)))]; lo, hi = pos[a], pos[b]; hop = int(1 + 12 * u[2] ** 3)
+            if u[1] < 0.5:
+                while hop > 1 and lo > 0:
+                    lo -= 1; hop -= qs[order[lo]] == qs[b]
+                part = order[lo:hi + 1]; move = {b}; need = set(pre[b])
+                for j in reversed(part):
+                    if j in need: move.add(j); need |= pre[j]
+                new = [j for j in part if j in move] + [j for j in part if j not in move]
+            else:
+                while hop > 1 and hi < n - 1:
+                    hi += 1; hop -= qs[order[hi]] == qs[a]
+                part = order[lo:hi + 1]; move = {a}
+                for j in part:
+                    if pre[j] & move: move.add(j)
+                new = [j for j in part if j not in move] + [j for j in part if j in move]
+            if new == part: continue
+            order = order[:lo] + new + order[hi + 1:]; stop = max(cut, hi + 1)
+            st = [_replay(G, order, q, lo, stop, s) for q, s in zip(PACE, cur[2])]; v = value(st, goal, marks)
+            if v < cur[0] + heat:
+                fin = st[0][0]; at = {m: j for j, m in enumerate(order)}
+                order[:stop] = sorted(order[:stop], key=lambda j: (fin[j] - d0[j], at[j]))
+                cur = (v, order, st); pos = None
+                if v < best[0]: best = cur
     return best[1]
 
 
@@ -196,7 +225,7 @@ def rank_program(g, core, T, topo):
         return
     N = len(T.cores)
     Q = {"V": g.vector, "S": g.scalar, "P": g.tensor, "G": g, "Y": g.sync}
-    ops = []
+    ops = []; piece = ["set"]; loaded = [0]; flip = [0]
 
     def reg(name, lo, hi, st=1):
         return (name, (1 << hi) - (1 << lo) if st == 1 else sum(1 << c for c in range(lo, hi, st)))
@@ -236,11 +265,23 @@ def rank_program(g, core, T, topo):
         elif len(aps) > 1 and len(aps[1]) > 3: cost = ("ga", size(aps[0]), 50 if q == "V" else 65)
         elif fn == "tensor_tensor": cost = ("e", size(aps[0]), 1 if any(a[2][0][0].startswith("pb") for a in aps[1:]) else 2)
         else: cost = ("e", size(aps[min(1, len(aps) - 1)]), 0.5 if q == "V" and all(wide(a) == 2 for a in aps[:2]) else 1)
-        ops.append(dict(cost=cost, q=q, fn=fn, a=[x[1] if isap(x) else x for x in args], k={n: (x[1] if isap(x) else x) for n, x in (kw or {}).items()}, w=w, r=r, kind=kind))
+        ops.append(dict(tag=piece[0] + (fn[:3] + q) * (piece[0] == "set"), cost=cost, q=q, fn=fn, a=[x[1] if isap(x) else x for x in args],
+                        k={n: (x[1] if isap(x) else x) for n, x in (kw or {}).items()}, w=w, r=r, kind=kind))
+
+    def part(name, *k):
+        piece[0] = name + repr(k)
 
     cp = lambda o, i: emit("V", "tensor_copy", [o, i])
     tt = lambda o, a, b, op: emit("V", "tensor_tensor", [o, a, b, op])
     ms = lambda o, c: emit("V", "memset", [o, c])
+
+    def tu(o, mid, a, b, op):
+        if TT16: tt(o, a, b, op)
+        else: tt(mid, a, b, op); cp(o, mid)
+
+    def au(o, mid, a, *k):
+        if AND16: ts(o, a, *k)
+        else: ts(mid, a, *k); cp(o, mid)
 
     def ts(o, a, s1, op0, s2=None, op1=None):
         emit("V", "tensor_scalar", [o, a, s1, s2, op0] + ([] if s2 is None else [op1]))
@@ -260,7 +301,7 @@ def rank_program(g, core, T, topo):
         emit("G", "iota", [o, pat, base, cm], None if _S[o[2][0][0]][1] == I else {"allow_small_or_imprecise_dtypes": True})
 
     sel = lambda o, i, pat, op, base, cm, fill=0.0: emit("G", "affine_select", [o, i, pat, op, fill, base, cm])
-    loaded = [0]
+    gcp = lambda o, i, n: sel(o, i, [[0, n]], OP.is_ge, 0, 0)
 
     def load(q, o, src):
         emit(q, "dma_start", [o, src], kind="d")
@@ -269,7 +310,7 @@ def rank_program(g, core, T, topo):
     def store(q, dst, i):
         emit(q, "dma_start", [dst, i[1]], kind="d", extra=([], i[2]))
 
-    Kp, P5, R0c, P3, Rm, P15, PKc = [C("Kp", j) for j in range(7)]
+    Kp, P5, R0c, P3, P15, PKc = [C("Kp", j) for j in range(6)]
     EQ, GEQ, GT, NE = OP.is_equal, OP.is_ge, OP.is_gt, OP.not_equal
     ADD, SUB, MUL, MIN, AND, SHR = OP.add, OP.subtract, OP.mult, OP.min, OP.bitwise_and, OP.arith_shift_right
     YB = lambda t: "YB%d" % t
@@ -280,14 +321,16 @@ def rank_program(g, core, T, topo):
     for x in range(2):
         for b in range(2):
             load("Y" if b else "S", A("Lt", 32 * b + 16 * x, 32 * b + 16 * x + 16), T.live[x::2, 512 * b:512 * b + 512])
-    for b in range(2): load("Y", A("Ri", 512 * b, 512 * b + 512), T.rings[:, 512 * b:512 * b + 512])
     load("S", A("Z"), T.z[:])
+    for b in range(2): load("Y", A("Ri", 512 * b, 512 * b + 512), T.rings[:, 512 * b:512 * b + 512])
     load("Y", A("X", 0, NB), T.x0[:])
     load("Y", C("WK", 0), T.w[:]); load("Y", C("WK", 1), T.kap[:])
     load("Y", A("TC", 0, 1, p=(0, 8)), T.th[:]); load("Y", A("TC", 1, 2, p=(0, 8)), T.cap[:])
 
-    ms(A("ONE"), 1.0); ms(A("TWO"), 2.0); ms(A("ONEf"), 1.0); ms(A("Lz", 0, 8), 0.0); ms(A("EW"), 0.0); ms(A("ONEs"), 1.0); ms(A("D5", 3840, 3856), 0.0)
+    ms(A("ONE"), 1.0); ms(A("TWO"), 2.0); ms(A("ONEf"), 1.0); ms(A("Lz", 0, 8), 0.0); ms(A("EW"), 0.0); ms(A("ONEs"), 1.0)
     iota(C("Ki0", 0), [[0, 1]], 0, 1)
+    sel(A("ID"), A("ONE"), [[-1, 128]], EQ, 0, 1)
+    iota(A("T17"), [[1, 18]])
     iota(A("A1"), [[16, 64]])
     sel(A("BLKt"), A("ONE"), [[-16, 8], [0, 16]], GEQ, 0, 1)
     sel(A("BLK"), A("BLKt"), [[16, 8], [0, 16]], GEQ, 15, -1)
@@ -295,34 +338,33 @@ def rank_program(g, core, T, topo):
     sel(A("UP"), A("BLK"), [[-1, 128]], GT, 0, 1)
     ts(C("Ki0", 1), C("Ki0", 0), 15, AND)
     cp(Kp, C("Ki0", 1))
-    ts(A("SL"), A("A1", 0, 16), Kp, ADD)
+    ts(A("SL"), A("A1", 0, 16), Kp, ADD); ts(A("IDu"), A("A1", 0, 32), Kp, ADD)
     ts(A("A2"), A("A1"), Kp, ADD, -1.0, MUL)
     ts(A("A1"), A("A1"), Kp, ADD, -1024.0, ADD)
     ts(A("A2"), A("A2"), 1023.0, ADD)
-    ts(P5, Kp, 5.0, MUL); ts(R0c, Kp, 0.0, EQ); ts(P3, Kp, 3.0, MUL); ts(Rm, Kp, 0.0, NE, -1024.0, MUL); ts(P15, Kp, 15.0, MUL)
+    ts(P5, Kp, 5.0, MUL); ts(R0c, Kp, 0.0, EQ); ts(P3, Kp, 3.0, MUL); ts(P15, Kp, 15.0, MUL)
     ts(PKc, Kp, -80.0, MUL, TOP - 15, ADD)
     for t in range(RO): ts(C("Kp", 8 + t), R0c, float(NB + P * t - 1024), MUL, 1024.0, ADD)
-    sel(A("ID"), A("ONE"), [[-1, 128]], EQ, 0, 1)
-    iota(A("T17"), [[1, 18]])
     sel(A("S7"), A("ONEf"), [[-16, 8], [0, 16]], EQ, -7, 1)
     sel(A("S15"), A("ONEf"), [[-16, 8], [0, 16]], EQ, -15, 1)
     ts(A("EW", 15, 143, 16), A("BLK", 0, 128, 16), 32768.0, MUL)
     iota(A("LAN"), [[1, 3], [48, 6]])
     ts(A("LAN"), A("LAN"), P3, ADD)
-    ms(A("RST"), 0.0); ms(A("RST", 0, 80, 16), TOP)
+    ms(A("RST"), 0.0); ms(A("RST", 0, 160, 16), TOP)
     ms(A("PK2"), -1.0); ms(A("PK2", 15, 80, 16), TOP)
     ms(A("PK1"), 0.0); ts(A("PK1", 15, 80, 16), A("T17", 0, 5), -16.0, MUL, PKc, ADD)
     ms(A("QD0"), 1.0); ms(A("QD0", 0, 60, 4), 0.0); ms(A("QD0", 2, 60, 4), 2.0 ** 19)
     ms(A("QD1", 1, 60, 4), -12.0 / 2 ** 24); ms(A("QD1", 2, 60, 4), RND); ms(A("QD1", 3, 60, 4), -RND)
+    part("zr")
     for c in range(3): act(A("Zp", 80 * c, 80 * c + 80), A("Z", c, P, 3), AF.Copy)
     for k in range(16): act(A("ZR", k, 3840, 16), A("Zp"), AF.Copy)
 
     def mask(j):
-        lo, hi = SPANS[j]
+        lo, hi = SPANS[j]; part("mask", j < 4)
         ts(A("MK", 128 * j, 128 * j + 128), A("ID"), C("GE", lo), MUL, C("LTt", hi), MUL)
 
     def bh(t, n0, n1):
-        per, stp, plan = PLANS[t]
+        per, stp, plan = PLANS[t]; part("bh", t, n0)
         for j, (rho, v, lo, hi) in enumerate(plan):
             k = SPANS.index((lo, hi))
             mm(A("pb6", rho + per * n0, rho + per * (n1 - 1) + 1, per), A("MK", 128 * k, 128 * k + 128),
@@ -331,16 +373,20 @@ def rank_program(g, core, T, topo):
 
     def xh(t, c0, c1, nb):
         for c in range(c0, c1, XC):
-            d = min(c + XC, c1)
+            d = min(c + XC, c1); part("xh", t, c0, c // 64)
             o, i = A(XH(t), 16 * c, 16 * d), IN(A("X", 0, nb), A(BH(t), c, d))
             if XV[t][0] <= c < XV[t][1]: cp(o, i)
-            else: act(o, i, AF.Copy)
+            else:
+                act(o, i, AF.Copy)
+                if t and c0 == 0 and d <= DONE[t]: ops[-1]["ahead"] = t
 
-    def r4(j, out, v0, v1, st, bank):
-        n = len(range(v0, v1, st))
-        mm(A(bank, 0, n), A("RT", 128 * j - 128, 128 * j) if j else A("ID"), A("Rh", v0, v1, st), True, True)
-        act(out, A(bank, 0, n), AF.Copy)
+    def r4(j, out, v0, v1, st):
+        n = len(range(v0, v1, st)); part("r4", v0 // 512, st, j // 2)
+        if GCAST and j == 0: return gcp(out, A("Rh", v0, v1, st), n)
+        mm(A("pb7", 0, n), A("RT", 128 * j - 128, 128 * j) if j else A("ID"), A("Rh", v0, v1, st), True, True)
+        act(out, A("pb7", 0, n), AF.Copy)
 
+    part("live")
     cp(A("Lb"), A("Lt"))
     emit("V", "transpose", [A("Lz", 8, 72), A("Lb")])
     mm(A("pb4", 0, 64), A("TRI"), A("Lz", 8, 72), True, False)
@@ -348,30 +394,25 @@ def rank_program(g, core, T, topo):
     tt(A("e0"), A("A1"), A("Lz", 8, 72), MUL)
     tt(A("e0"), A("e0"), A("A2"), ADD)
     scan(A("rho"), A("ONEs"), A("pb4", 0, 64), MUL, ADD)
-    tt(A("e0"), A("e0"), A("rho"), ADD)
-    cp(A("p0u"), A("e0"))
+    tu(A("p0u"), A("A2"), A("e0"), A("rho"), ADD)
     mm(A("pb4", 0, 2), A("S7"), A("rho", 41, 57, 15), True, True)
     mm(A("pb4", 2, 3), A("S15"), C("rho", 63), True, True)
     ts(A("GE"), A("T17"), Kp, OP.is_le); ts(A("LTt"), A("T17"), Kp, GT)
     for j in range(len(SPANS)): mask(j)
+    part("lr")
     cp(A("CN", 0, 3), A("pb4", 0, 3))
     ts(A("s0"), A("LAN"), C("CN", 0), ADD)
     ts(A("s1"), A("s0"), C("CN", 2), GEQ, C("CN", 2), MUL)
-    tt(A("s2"), A("s0"), A("s1"), SUB)
-    cp(A("LR"), A("s2"))
+    tu(A("LR"), A("s2"), A("s0"), A("s1"), SUB)
     for b in range(2):
-        ts(A("Rh", 512 * b, 512 * b + 512), A("Ri", 512 * b, 512 * b + 512), -1024.0, ADD)
+        part("rh", b)
+        act(A("Rh", 512 * b, 512 * b + 512), IN(A("Ri", 512 * b, 512 * b + 512), A("IDu")), AF.Identity, bias=-1024.0)
+        part("sc", b)
         cp(IN(A("BIG", CI, R1), A("p0u", 32 * b, 32 * b + 32)), A("Ri", 512 * b, 512 * b + 512))
-    act(A("BIG", CJ, CJ + P), A("BIG", CI, CI + P), AF.Copy)
     bh(0, 0, 256)
     xh(0, 0, 256, NB)
+    piece[0] = "set"
     iota(A("C16"), [[0, 5], [1, 16]])
-    iota(A("MT"), [[1, 16], [0, 5]])
-    iota(A("PBS"), [[2048, 16], [0, 5]], KOFF)
-    sel(A("G8t", p=(0, 8)), A("ONEf", p=(0, 8)), [[1, 128]], GEQ, 0, -16)
-    sel(A("G8", p=(0, 8)), A("G8t", p=(0, 8)), [[-1, 128]], GEQ, 15, 16)
-    sel(A("IDf"), A("ONEf"), [[-1, 128]], EQ, 0, 1)
-    iota(S15("NFL"), [[80, 3], [1, 5]], 960); iota(S15("LOC"), [[1280, 3], [16, 5]])
     sel(A("S15b"), A("ONE"), [[-16, 8], [0, 16]], EQ, -15, 1)
     for j in (1, 2, 3):
         sel(A("RS", 128 * j - 128, 128 * j), A("BLK"), [[-1, 128]], EQ, -4 * j, 1)
@@ -379,20 +420,28 @@ def rank_program(g, core, T, topo):
         mm(A("pb7", 0, 128), A("ID"), A("RS", 128 * j - 128, 128 * j), True, False)
         mm(A("pb7", 0, 128), A("ID"), A("RK", 128 * j - 128, 128 * j), False, True)
         act(A("RT", 128 * j - 128, 128 * j), A("pb7", 0, 128), AF.Copy)
+    iota(A("MT"), [[1, 16], [0, 5]])
+    iota(A("PBS"), [[2048, 16], [0, 5]], KOFF)
+    sel(A("G8t", p=(0, 8)), A("ONEf", p=(0, 8)), [[1, 128]], GEQ, 0, -16)
+    sel(A("G8", p=(0, 8)), A("G8t", p=(0, 8)), [[-1, 128]], GEQ, 15, 16)
+    sel(A("IDf"), A("ONEf"), [[-1, 128]], EQ, 0, 1)
+    iota(S15("NFL"), [[80, 3], [1, 5]], 960)
     act(A("BLKf"), A("BLK"), AF.Copy)
-    sel(A("UPI"), A("BLK"), [[-1, 128]], GEQ, 0, 1)
-    sel(A("GE8"), A("BLK"), [[-16, 8], [0, 16]], GEQ, -8, 1)
     sel(A("BK1"), A("BLK"), [[0, 8], [1, 16]], GT, 0, 0)
-    sel(A("BK1f"), A("BLKf"), [[0, 8], [1, 16]], GT, 0, 0)
-    sel(A("SHf"), A("BK1f"), [[-1, 128]], EQ, 1, 1)
+    iota(A("LN", P, 2 * P), [[1, 3], [3, 80]])
+    for j in range(4): sel(A("SH", 128 * j, 128 * j + 128), A("BK1"), [[-1, 128]], EQ, 1 - j, 1)
+    part("late")
     for j in range(4):
-        sel(A("SH", 128 * j, 128 * j + 128), A("BK1"), [[-1, 128]], EQ, 1 - j, 1)
         for k in range(17 - j, 16):
             col = A("SH", 128 * j + k, 128 * j + 128, 16)
             sel(col, col, [[-16, 8]], NE, -15, 1, 1.0)
-    for j in range(3): iota(A("R4", TM * j + T0 + P, TM * j + TM), [[0, P]])
-    iota(A("LN", P, 2 * P), [[1, 3], [3, 80]])
     iota(A("LN", 0, P), [[1, 3], [3, 5], [15, 16]])
+    sel(A("UPI"), A("BLK"), [[-1, 128]], GEQ, 0, 1)
+    sel(A("GE8"), A("BLK"), [[-16, 8], [0, 16]], GEQ, -8, 1)
+    part("later")
+    for j in range(3): iota(A("R4", TM * j + T0 + P, TM * j + TM), [[0, P]])
+    gcp(A("BIG", CJ, CJ + P), A("BIG", CI, CI + P), P)
+    part("tables")
     ts(A("E0"), A("ID"), R0c, MUL)
     ts(A("BGM"), A("C16"), Kp, NE, 2048.0, MUL)
     ts(C("WKf", 0), C("WK", 0), 2048.0, GEQ); ts(C("WKf", 1), C("WK", 0), 2.0 ** -12, MUL)
@@ -409,8 +458,10 @@ def rank_program(g, core, T, topo):
     cp(C("TH", 1), A("pb5", 81, 82))
     ts(C("TH", 4), C("TH", 0), -1.0, MUL, 1.0, ADD); ts(C("TH", 3), C("TH", 4), 8192.0, MUL)
     act(S15("NFL"), S15("NFL"), AF.Identity, bias=P5)
-    act(S15("LOC"), S15("LOC"), AF.Identity, bias=Kp)
+    act(S15("LOC"), S15("SL"), AF.Identity, bias=4096.0)
+    act(A("NID"), A("ID"), AF.Copy, scale=-1.0)
     act(S15("IDX"), S15("T17"), AF.Identity, bias=P15)
+    part("nbu")
     ts(S15("i0"), S15("SL"), 1.0 / 15, MUL, -0.47, ADD)
     ts(S15("y2"), S15("i0"), -15.0, MUL); cp(S15("s4"), S15("i0"))
     tt(S15("y2"), S15("y2"), S15("SL"), ADD)
@@ -420,9 +471,10 @@ def rank_program(g, core, T, topo):
     tt(S15("y2"), S15("y2"), S15("s4"), ADD)
     tt(S15("y2"), S15("y2"), S15("y3"), ADD)
     cp(S15("NBu"), S15("y2"))
-    for j in range(4): r4(j, A("R0", j, T0, 4), j, T0, 4, "pb7" if j % 2 else "pb3")
+    for j in range(4): r4(j, A("R0", j, T0, 4), j, T0, 4)
 
     def prep(t):
+        part("prep", t)
         if t == 0:
             tt(C("CN", 3), C("CN", 2), C("CN", 1), SUB)
             ts(A("msk"), A("LAN"), C("CN", 3), GEQ)
@@ -436,26 +488,28 @@ def rank_program(g, core, T, topo):
             tt(A("bas"), A("s0"), A("s3"), ADD)
 
     def keep(t):
-        cp(A("RESf"), A("RES"))
-        mm(A("pb7", 0, P), A("E0"), A("LN", P, 2 * P), True, False)
-        mm(A("pb7", 0, P), A("SHf"), A("RESf"), False, True)
-        act(A("WT", 960, 1200), A("pb7", 0, P), AF.Identity, bias=Rm)
+        part("keep", t)
+        ts(A("RESh"), A("RES"), -1024.0, ADD)
+        mm(A("pb3", 0, P), A("E0"), A("LN", P, 2 * P), True, False)
+        mm(A("pb3", 0, P), A("SH", 0, 128), A("RESh"), False, True)
+        act(A("WT", 960, 1200), A("pb3", 0, P), AF.Copy)
 
     def step2(t, c):
-        bank = "pb%d" % c; o = 1280 * c; p = 0; n0 = 80 * c
+        bank = "pb%d" % c; o = 1280 * c; p = 0; n0 = 80 * c; part("s2", t, c)
         cp(A("RES", n0, n0 + 80), IN(A("BIG", CI if t == 0 else 0, (R1, R1, CJ + P)[t]), A("LR", 6 * c, 6 * c + 5)))
-        for n in CH2[c]:
+        for n in CH2[t][c]:
             a, b = o + 80 * p, o + 80 * (p + n)
             tt(A("D2", a, b), IN(A("X", 0, NB + P * t), A("RES", a // 16, b // 16)), A("ZR", a, b), SUB)
-            ops[-1]["wide"] = True
+            ops[-1]["wide"] = "V"; ops[-1]["gate"] = t and a == 0
             act(A("A2w", a, b), A("D2", a, b), AF.Relu, scale=-1.0 / 1024)
+            if a == 0: ops[-1]["opens"] = t
             for r in range(p, p + n):
                 mm(A(bank, 0, 80), A("EW", 15 - r, 143 - r), A("A2w", o + 80 * r, o + 80 * r + 80), r == 0, r == 15, r > p)
             p += n
+        part("pick", t, c)
         scan(A("SC1", n0, n0 + 80), A(bank, 0, 80), A("PK1"), MIN, ADD, TOP)
         scan(A("SC2", n0, n0 + 80), A(bank, 0, 80), A("PK2"), MIN, ADD, TOP)
-        tt(A("kf", 5 * c, 5 * c + 5), A("SC2", n0 + 15, n0 + 80, 16), A("SC1", n0 + 15, n0 + 80, 16), SUB)
-        cp(A("LY", 6 * c, 6 * c + 5), A("kf", 5 * c, 5 * c + 5))
+        tu(A("LY", 6 * c, 6 * c + 5), A("kf", 5 * c, 5 * c + 5), A("SC2", n0 + 15, n0 + 80, 16), A("SC1", n0 + 15, n0 + 80, 16), SUB)
         y = A(YB(t), 1280, 1360) if c == 2 else A("YS", 160 * t + n0, 160 * t + n0 + 80)
         act(y, IN(A("D2", o, o + 1280), A("LY", 6 * c, 6 * c + 5)), AF.Abs)
         if c < 2: send(t, c)
@@ -468,30 +522,48 @@ def rank_program(g, core, T, topo):
                                src=T["YS"][:, y:y + 80], dst=T[YB(t)][:, 640 * c:640 * c + 80])
         emit("G", "remote_dma_fused", [[tr]], {"local_sem": T.sem.sent}, kind="r", extra=([], [reg("YS", y, y + 80)]))
         if t + c == 0: ops[-1]["cost"] = ("rem", 1800.0, 0)
-        ops.append(dict(cost=("arr", 0, 0), kind="arr", q="R%d%d" % (t, c), w=[reg(YB(t), 640 * c, 640 * c + 80)], r=[], n=len(far)))
+        ops.append(dict(tag=piece[0], cost=("arr", 0, 0), kind="arr", q="R%d%d" % (t, c), w=[reg(YB(t), 640 * c, 640 * c + 80)], r=[], n=len(far)))
 
-    def step4(t, c):
-        bank = "pb%d" % c; o = 640 * c; n0 = 80 * c; n = 80; s = 20 * c
-        while n < 80 * max(CH5[c]):
-            act(A(YB(t), o + n, o + 2 * n), A(YB(t), o, o + n), AF.Copy); n *= 2
-        mm(A(bank, 0, 80), A("ID"), A("BGM"), True, False)
-        mm(A(bank, 0, 80), A("W16"), A(YB(t), o, o + 80), False, True)
-        scan(A("SU", n0, n0 + 80), A("RST"), A(bank, 0, 80), ADD, MIN)
-        raw = A("SU", n0 + 15, n0 + 80, 16); ri = A("ri", 5 * c, 5 * c + 5)
+    def spread(t, c):
+        o = 640 * c; n = 80; part("spread", t, c)
+        while n < 80 * max([4] + [w for j, w in enumerate(CH5[t][c]) if (c, j) not in SP5[t]]):
+            a, b = A(YB(t), o + n, o + 2 * n), A(YB(t), o, o + n)
+            if n >= REPG: gcp(a, b, n)
+            else: act(a, b, AF.Copy)
+            n *= 2
+        part("beside", t)
+        gcp(A(XH(t), 4096 + 80 * c, 4176 + 80 * c), A(YB(t), o, o + 80), 80)
+
+    def step4(t, cs):
+        c = cs[0]; w = len(cs); bank = "pb%d" % c; n0, n1 = 80 * c, 80 * (c + w); s0, s1 = 20 * c, 20 * (c + w); part("s4", t, c)
+        for j in range(w):
+            mm(A(bank, 80 * j, 80 * j + 80), A("ID"), A("BGM"), True, False)
+            mm(A(bank, 80 * j, 80 * j + 80), A("W16"), A(YB(t), 640 * (c + j), 640 * (c + j) + 80), False, True)
+        scan(A("SU", n0, n1), A("RST", 0, 80 * w), A(bank, 0, 80 * w), ADD, MIN)
+        raw = A("SU", n0 + 15, n1, 16); ri = A("ri", 5 * c, 5 * (c + w))
         ts(ri, raw, -0.5, ADD)
-        tt(A("QD1", s, s + 20, 4), raw, ri, SUB); tt(A("QD0", s + 1, s + 20, 4), raw, ri, SUB)
-        scan(A("QS", s, s + 20), A("QD0", s, s + 20), A("QD1", s, s + 20), MUL, ADD)
-        for k in range(5): ts(A("Hi", n0 + k, n0 + 80, 5), A("KT"), C("QD1", s + 4 * k), MUL, C("QS", s + 4 * k + 3), ADD)
-        ts(A("Hj", n0, n0 + 80), A("Hi", n0, n0 + 80), 4095, AND)
-        cp(A("Hu", n0, n0 + 80), A("Hj", n0, n0 + 80))
+        tt(A("QD1", s0, s1, 4), raw, ri, SUB); tt(A("QD0", s0 + 1, s1, 4), raw, ri, SUB)
+        scan(A("QS", s0, s1), A("QD0", s0, s1), A("QD1", s0, s1), MUL, ADD)
+        for c in cs:
+            for k in range(5): ts(A("Hi", 80 * c + k, 80 * c + 80, 5), A("KT"), C("QD1", 20 * c + 4 * k), MUL, C("QS", 20 * c + 4 * k + 3), ADD)
+        au(A("Hu", n0, n1), A("Hj", n0, n1), A("Hi", n0, n1), 4095, AND)
 
-    def step5(t, c, first, last):
-        bank = "pb%d" % c; o = 1280 * c; m = 0
-        for n in CH5[c]:
-            a, b = o + 80 * m, o + 80 * (m + n)
-            tt(A("D5", a, b), IN(A(XH(t)), A("Hu", a // 16, b // 16)), A(YB(t), 640 * c, 640 * c + 80 * n), SUB)
-            ops[-1]["wide"] = True
-            act(A("A5", a, b), A("D5", a, b), AF.Abs)
+    def step5(t, c):
+        bank = "pb%d" % c; o = 1280 * c; m = 0; part("s5", t, c)
+        for j, n in enumerate(CH5[t][c]):
+            a, b = o + 80 * m, o + 80 * (m + n); x = IN(A(XH(t), 0, 4096), A("Hu", a // 16, b // 16))
+            if (c, j) in SP5[t]:
+                act(A("D5", a, b), x, AF.Copy)
+                ops[-1]["wide"] = "S"
+                for e in range(a, b, 320):
+                    f = min(e + 320, b); flip[0] ^= 1; out = A("pb5" if flip[0] else "pb3", 0, f - e)
+                    mm(out, A("NID"), A(YB(t), 640 * c, 640 * c + f - e), True, False)
+                    mm(out, A("ID"), A("D5", e, f), False, True)
+                    act(A("A5", e, f), out, AF.Abs)
+            else:
+                tt(A("D5", a, b), x, A(YB(t), 640 * c, 640 * c + 80 * n), SUB)
+                ops[-1]["wide"] = "V"
+                act(A("A5", a, b), A("D5", a, b), AF.Abs)
             m += n
         m = 0
         for n in GR5[c]:
@@ -499,71 +571,74 @@ def rank_program(g, core, T, topo):
             mm(out, A("IDf"), A("PAY", 5 * m, 5 * (m + n)), True, False)
             for r in range(16): mm(out, A("EW", 15 - r, 143 - r), A("A5", o + 80 * m + r, o + 80 * (m + n), 16), False, r == 15, r > 0)
             m += n
+        part("least", t, c)
         for k in range(5): emit("V", "tensor_reduce", [C("K", 5 * c + k), A(bank, k, 80, 5), AxisListType.X, MIN])
         ts(A("fw", c, 15, 3), A("K", 5 * c, 5 * c + 5), C("TH", 0), OP.is_lt, -1.0 if c == 2 else 1.0, MUL)
-        if first and t: mm(A("pb4", 0, 1), A("IDf"), C("Bp", 0), True, False)
-        for k in range(5): mm(A("pb4", 0, 1), A("TWO" if c == 2 else "ONE"), C("fw", 3 * k + c), first and k == 0 and t == 0, last and k == 4, k > 0)
+        if c == 0 and t: mm(A("pb4", 0, 1), A("IDf"), C("Bp", 0), True, False)
+        for k in range(5): mm(A("pb4", 0, 1), A("TWO" if c == 2 else "ONE"), C("fw", 3 * k + c), c + k + t == 0, c == 2 and k == 4, k > 0)
 
     def close(t):
-        last = t == RO - 1; TT = T0 + P * t; lv = A("LV", 16 * t, 16 * t + 15)
+        last = t == RO - 1; TT = T0 + P * t; lv = A("LV", 16 * t, 16 * t + 15); part("ring", t)
         act(S15("uf"), A("QD1", 0, 60, 4), AF.Copy, scale=4096.0)
         cp(S15("Ki"), S15("K"))
         ts(S15("kp"), S15("Ki"), 2047, AND)
         act(S15("nf"), S15("K"), AF.Relu, bias=C("TH", 3), scale=8192.0)
         tt(S15("t1"), S15("kp"), S15("uf"), MUL)
-        ts(S15("mi"), S15("Ki"), 11, SHR, 15, AND)
         tt(S15("t2"), S15("t1"), A("QS", 3, 60, 4), ADD)
-        ts(lv, S15("fw"), A("pb4", 0, 1), MUL, C("TH", 1), OP.is_le)
         if t == 0:
-            ts(S15("hh"), S15("t2"), 2, SHR, 1023, AND)
-            cp(S15("L1"), S15("hh"))
-        else:
-            ts(S15("hh"), S15("t2"), 4095, AND)
+            au(S15("L1"), S15("a12"), S15("t2"), 2, SHR, 1023, AND)
+        ts(S15("hh"), S15("t2"), 4095, AND)
+        if t:
             ts(S15("a12"), S15("t2"), 12, AND)
             ts(S15("x1"), S15("hh"), TT / 4096.0, MUL, -255.0 / 512, ADD)
             ts(S15("x2"), S15("a12"), TM / 4.0, MUL)
-            tt(S15("ix"), S15("x1"), S15("x2"), ADD)
-            cp(S15("L1"), S15("ix"))
+            tu(S15("L1"), S15("ix"), S15("x1"), S15("x2"), ADD)
         ts(S15("a3"), S15("t2"), 3, AND)
+        win = A("R4", 0, 3 * TM + TT) if t else A("R0")
+        cp(A("RC", 0, min(P, 16 * RCV)), IN(win, A("L1", 0, min(15, RCV))))
+        if RCV < 15: act(A("RC", 16 * RCV, P), IN(win, A("L1", RCV, 15)), AF.Copy)
+        for j in range(4):
+            out = A("pb%d" % j, 0, P)
+            mm(out, A("E0"), A("LN", 0, P), True, False)
+            mm(out, A("SH", 128 * j, 128 * j + 128), A("RC"), False, True)
+            if j in WTV: cp(A("WT", P * j, P * j + P), out)
+            else: act(A("WT", P * j, P * j + P), out, AF.Copy)
+        ts(S15("y2"), S15("a3"), 240.0, MUL)
+        tt(S15("g2"), S15("nf"), S15("SL"), ADD)
+        tt(S15("z2"), S15("y2"), S15("g2"), ADD)
+        tu(S15("L2"), S15("w2"), S15("z2"), S15("NFL"), MIN)
+        ts(A("NEW", 0, 128), IN(A("WT"), A("L2", 0, 8)), C("Kp", 8 + t), ADD)
+        act(A("NEW", 128, P), IN(A("WT"), A("L2", 8, 15)), AF.Identity, bias=C("Kp", 8 + t))
+        part("marks", t)
+        ts(lv, S15("fw"), A("pb4", 0, 1), MUL, C("TH", 1), OP.is_le)
         if not last:
             ts(S15("dead"), S15("fw"), A("pb4", 0, 1), MUL, C("TH", 1), GT)
             cp(C("Bp", 0), A("pb4", 0, 1))
             scan(S15("cum"), A("ONEs", 0, 15), lv, MUL, ADD)
             tt(S15("e1"), S15("dead"), S15("IDX"), MUL)
             mm(A("pb4", 0, 1), A("UPI"), C("cum", 14), True, True)
-            mm(A("pb4", 1, 2), A("BLK"), C("cum", 14), True, True)
-            if t == 0: mm(A("pb4", 2, 3), A("GE8"), C("cum", 14), True, True)
+            mm(A("pb4", 1, 2), A("BLK"), C("cum", 14), True, True, True)
+            if t == 0: mm(A("pb4", 2, 3), A("GE8"), C("cum", 14), True, True, True)
             tt(S15("e3"), S15("cum"), S15("e1"), SUB)
             for c in range(3): ts(A("LP", 5 * c, 5 * c + 5), A("e3", c, 15, 3), A("pb4", 0, 1), SUB, P - 1.0, ADD)
             ts(A("pf1"), A("msk"), A("pb4", 1, 2), MUL)
             if t == 0: cp(C("CN", 10), A("pb4", 2, 3))
-            tt(A("pf2"), A("bas"), A("pf1"), SUB)
-            cp(A("LR"), A("pf2"))
-        cp(A("RC"), IN(A("R4", 0, 3 * TM + TT) if t else A("R0"), S15("L1")))
-        for j in range(4):
-            out = A("pb%d" % j, 0, P)
-            mm(out, A("E0"), A("LN", 0, P), True, False)
-            mm(out, A("SH", 128 * j, 128 * j + 128), A("RC"), False, True)
-            if j % 2: cp(A("WT", P * j, P * j + P), out)
-            else: act(A("WT", P * j, P * j + P), out, AF.Copy)
-        ts(S15("y3"), S15("mi"), 80.0, MUL)
-        tt(S15("g3"), S15("nf"), S15("LOC"), ADD)
-        ts(S15("y2"), S15("a3"), 240.0, MUL)
-        tt(S15("g2"), S15("nf"), S15("SL"), ADD)
-        tt(S15("z3"), S15("y3"), S15("g3"), ADD)
-        tt(S15("z2"), S15("y2"), S15("g2"), ADD)
-        ts(S15("L3"), S15("z3"), 3840.0, MIN)
-        tt(S15("w2"), S15("z2"), S15("NFL"), MIN)
-        act(A("EE"), IN(A("D5"), S15("L3")), AF.Identity, bias=191.75, scale=0.5)
-        cp(S15("L2"), S15("w2"))
-        ts(A("NEW"), IN(A("WT"), S15("L2")), C("Kp", 8 + t), ADD)
-        if not last: cp(IN(A("BIG", R1 * t, R1 * t + P), S15("LP")), A("NEW"))
-        act(A("YT", P * t, P * t + P), IN(A("NEW"), S15("NBu")), AF.Copy)
-        for c in range(15):
-            out = A("pb5", 3 * (c % 5) + c // 5, P, 15); y = 640 * (c // 5) + 16 * (c % 5)
-            mm(out, A("ID"), A(YB(t), y, y + 16), True, False, c % 3 > 0)
-            mm(out, A("ID"), A("EE", 16 * c, 16 * c + 16), False, True, True)
-        act(A("X", NB + P * t, NB + P * t + P), A("pb5", 0, P), AF.Identity, bias=-192.0)
+            tu(A("LR"), A("pf2"), A("bas"), A("pf1"), SUB)
+            cp(IN(A("BIG", R1 * t, R1 * t + P), S15("LP")), A("NEW"))
+            part("yt", t)
+            act(A("YT", P * t, P * t + P), IN(A("NEW"), S15("NBu")), AF.Copy)
+        else:
+            cp(A("YT", P * t, P * t + 128), IN(A("NEW"), A("NBu", 0, 8)))
+            act(A("YT", P * t + 128, P * t + P), IN(A("NEW"), A("NBu", 8, 15)), AF.Copy)
+        part("board", t)
+        tt(S15("z3"), S15("hh"), S15("nf"), ADD)
+        tu(S15("L3"), S15("g3"), S15("z3"), S15("LOC"), MIN)
+        act(A("EE"), IN(A(XH(t)), S15("L3")), AF.Copy)
+        mm(A("pb5", 0, P), A("ID"), A(XH(t), 4096, 4096 + P), True, False)
+        mm(A("pb5", 0, P), A("ID"), A("EE"), False, True)
+        act(A("EF"), A("pb5", 0, P), AF.Identity, bias=191.75, scale=0.5)
+        act(A("X", NB + P * t, NB + P * t + P), IN(A("EF"), S15("NBu")), AF.Identity, bias=-192.0)
+        part("store", t)
         store("Y", T.ya[:, P * t:P * t + P], lv)
         store("Y", T.yx[:, P * t:P * t + P], A("X", NB + P * t, NB + P * t + P))
         store("Y", T.yt[:, P * t:P * t + P], A("YT", P * t, P * t + P))
@@ -572,21 +647,24 @@ def rank_program(g, core, T, topo):
     for t in range(RO):
         TT = T0 + P * t; nx = t + 1 < RO
         if t:
-            ts(A("Rh", TT - P, TT), A("YT", P * t - P, P * t), -1024.0, ADD)
+            part("rh", TT)
+            act(A("Rh", TT - P, TT), A("YT", P * t - P, P * t), AF.Identity, bias=-1024.0)
             bh(t, OLD[t], 256 // PLANS[t][0])
             xh(t, OLD[t] * PLANS[t][0], 256, NB + P * t)
-        for c in ORD2: step2(t, c)
+        for c in range(3): step2(t, c)
         if nx:
             prep(t)
             bh(t + 1, 0, OLD[t + 1])
             xh(t + 1, 0, OLD[t + 1] * PLANS[t + 1][0], NB + P * t)
         if t == 1:
-            for j in range(8): r4(j // 2, A("R4", TM * (j // 2) + 512 * (j % 2), TM * (j // 2) + 512 * (j % 2) + 512), 512 * (j % 2), 512 * (j % 2) + 512, 1, "pb7" if j % 2 else "pb3")
+            for j in range(4):
+                for v in (0, 512): r4(j, A("R4", TM * j + v, TM * j + v + 512), v, v + 512, 1)
         if t:
-            for j in range(4): r4(j, A("R4", TM * j + TT - P, TM * j + TT), TT - P, TT, 1, "pb7" if j % 2 else "pb3")
+            for j in range(4): r4(j, A("R4", TM * j + TT - P, TM * j + TT), TT - P, TT, 1)
         keep(t)
-        for c in ORD5: step4(t, c)
-        for c in ORD5: step5(t, c, c == ORD5[0], c == ORD5[2])
+        for c in range(3): spread(t, c)
+        for cs in GR4: step4(t, cs)
+        for c in range(3): step5(t, c)
         close(t)
 
     seen = {}; bank = {}
@@ -611,7 +689,10 @@ def rank_program(g, core, T, topo):
         if o["kind"] == "arr": deps = set(); soft = {n - 1}
         if o["kind"] == "d" and o["w"]:
             soft.update(m for m in range(n) if ops[m]["kind"] == "d" and ops[m]["q"] == o["q"])
-        if "wide" in o: soft.update([m for m in range(n) if "wide" in ops[m]][-1:])
+        if o["q"] == "G" and o["tag"][:3] == "set": soft.update([m for m in range(n) if ops[m]["q"] == "G"][-1:])
+        if "wide" in o: soft.update([m for m in range(n) if ops[m].get("wide") == o["wide"]][-1:])
+        if "opens" in o: soft.update(m for m in range(n) if ops[m].get("ahead") == o["opens"])
+        soft.discard(n)
         o["deps"] = sorted(deps); o["soft"] = sorted(soft)
     if not ORDER: ORDER.extend(_schedule(ops))
     pos = {m: n for n, m in enumerate(ORDER)}

@@ -34,16 +34,16 @@ _S = dict(
     XHa=(4336, B), XHb=(4336, B), BHa=(256, U), BHb=(256, U), RES=(240, U), RESh=(240, H), WT=(1200, F), RC=(240, H), NEW=(240, F), YT=(720, F),
     YS=(480, B), YB0=(1920, B), YB1=(1920, B), YB2=(1920, B), EE=(240, B), EF=(240, B), LN=(480, B), E0=(128, B), LV=(48, F),
     ONE=(128, B), TWO=(128, B), ONEf=(128, F), BLK=(128, B), BLKt=(128, B), BLKf=(128, F), EW=(144, B), TRI=(128, B), UP=(128, B), UPI=(128, B), GE8=(128, B),
-    S7=(128, F), S15=(128, F), S15b=(128, B), ID=(128, B), NID=(128, B), IDf=(128, F), G8=(128, F), G8t=(128, F), BK1=(128, B), SH=(512, B),
+    S7=(128, F), S15=(128, F), S15b=(128, B), ID=(128, B), NID=(128, B), G8=(128, F), G8t=(128, F), BK1=(128, B), SH=(512, B),
     RS=(384, B), RK=(384, B), RT=(384, B), MK=(128 * len(SPANS), B), W16=(128, H),
-    Ki0=(2, I), Kp=(16, F), T17=(18, F), GE=(18, F), LTt=(18, F), C16=(80, F), BGM=(80, B), RST=(160, F), PK1=(80, F), PK2=(80, F),
-    MT=(80, F), PBS=(80, F), RK2=(80, F), PAY=(80, F), KT=(16, F), WK=(4, I), WKf=(4, F),
+    Ki0=(4, I), M16=(128, B), Kp=(16, F), T17=(20, F), GE=(16, F), LTt=(20, F), SPN=(64, F), C16=(80, F), BGM=(80, B), RST=(160, F), RSU=(160, F), SV=(240, I), FM0=(30, F), FM1=(30, I), FM2=(30, I), PK1=(80, F), PK2=(80, F),
+    MT=(80, F), PBS=(80, F), RK2=(80, F), PAY=(80, H), PL=(128, B), AC=(160, F), NEG=(16, F), dB=(2, F), KT=(16, F), WK=(4, I), WKf=(4, F),
     TC=(4, I), TCf=(4, F), TH=(8, F), CN=(16, F), SL=(16, F), IDX=(16, F), NFL=(16, F), LOC=(16, F), LAN=(18, F),
     s0=(18, F), s1=(18, F), s2=(18, F), s3=(18, F), s4=(16, F), i0=(16, I), NBu=(16, U), LR=(18, U),
     SC1=(240, F), SC2=(240, F), SU=(240, F), kf=(16, F), LY=(18, U), ri=(16, I), QD0=(60, F), QD1=(60, F), QS=(60, F), uf=(16, F),
-    Hi=(240, I), Hj=(240, I), Hu=(240, U), K=(16, F), Ki=(16, I), nf=(16, F), fw=(16, B), kp=(16, I),
+    Hi=(240, I), Hj=(240, I), Hu=(240, U), K=(16, F), Ki=(16, I), nf=(16, F), fw=(48, B), kp=(16, I),
     t1=(16, F), t2=(16, I), hh=(16, I), a12=(16, I), a3=(16, I), x1=(16, F), x2=(16, F), ix=(16, F), L1=(16, U), L2=(16, U), L3=(16, U),
-    g2=(16, F), g3=(16, F), y2=(16, F), y3=(16, F), z2=(16, F), z3=(16, F), w2=(16, F), Bp=(2, F), cum=(16, B), dead=(16, F), e1=(16, F), e3=(16, F),
+    g2=(16, F), g3=(16, F), y2=(16, F), y3=(16, F), z2=(16, F), z3=(16, F), w2=(16, F), cum=(16, B), e1=(16, F), e3=(16, F),
     LP=(16, U), msk=(18, F), bas=(18, F), pf1=(18, F), pf2=(18, F), ONEs=(64, F),
 )
 HOME = {}
@@ -59,19 +59,27 @@ SEMAPHORES = ["qV", "qS", "qP", "qG", "sent"] + ["arr%d%d" % (t, c) for t in ran
 
 
 ORDER = []
-PACE = [dict(cy=0.83, pe=0.42, ga=1.56, sc=3.8, lat=170, dma=1500, bw=200.0, rem=2500),
-        dict(cy=1.15, pe=0.6, ga=1.8, sc=5.0, lat=200, dma=2200, bw=160.0, rem=3500)]
-WEIGHT = (1.0, 1.45)
-SHIFTS, MOVES, MIX, HEAT, SIDE, SEED = 200, (22000, 22000, 22000, 8000), 0.0, 300.0, 0.3, 12345
+PACE = [dict(cy=0.83, pe=0.46, ga=1.56, sc=3.8, lat=210, wake=50, fix=0, dma=1500, bw=200.0, rem=2400),
+        dict(cy=1.15, pe=0.62, ga=1.85, sc=5.0, lat=220, wake=200, fix=5, dma=2000, bw=170.0, rem=3200)]
+WEIGHT = (1.0, 1.8)
+SHIFTS, MOVES, MIX, HEAT, SIDE, SEED = 100, (40000, 40000, 30000, 25000), 0.0, 500.0, 1.0, 41
 TT16, AND16, GCAST = True, False, True
-XC = 24
-CH2 = (((8, 4, 4), (8, 4, 4), (8, 4, 4)),) * 3
-CH5 = (((4, 4, 4, 4), (8, 8), (8, 6, 2)),) * 3
-GR5 = ((16,), (16,), (8, 8))
+RED32, SCAN32, SCANIN = True, True, True
+ORD5 = (0, 2, 1)
+MARKS = ("LY", "Hu", "SU", "YS", "QS")
+TREE, HIS = True, (tuple((c, k) for c in (1, 2) for k in range(5)),) * 3
+HOP, ZRA = 16, 12
+XCV, EARLY = 8, 1
+RV2 = (tuple((2, j) for j in range(4)),) * 3
+MKS = range(4, 22)
+XC = 32
+CH2 = (((8, 6, 2), (8, 2, 4, 2), (8, 2, 4, 2)),) * 3
+CH5 = (((4, 4, 4, 4), (8, 6, 2), (8, 8)),) * 3
+GR5 = ((16,), (8, 8), (16,))
 GR4 = ((0,), (1,), (2,))
-SP5 = (((1, 1),), ((1, 1),), ((1, 0), (1, 1)))
-REPG = 320
-XV = ((192, 256), (0, 0), (0, 0))
+SP5 = (((2, 1),), ((2, 1),), ((2, 0), (2, 1)))
+REPG = 160
+XV = ((256, 256), (0, 0), (0, 0))
 DONE = (0, 0, 0)
 RCV, WTV = 8, (1, 3)
 
@@ -85,12 +93,13 @@ def _times(ops, p):
         elif kind == "arr": out.append((0.0, p["rem"] - 300.0))
         else:
             d = {"e": max(64, n * r), "ga": r * 1.2 + n * p["ga"], "sc": r * 1.2 + n * p["sc"], "pe": n * p["pe"] / p["cy"], "g": r * 1.2 + 2 * n}[kind] * p["cy"]
+            if kind == "e": d += p["fix"] * (1.0 if o["q"] == "V" else 0.5)
             out.append((d, d))
     return out
 
 
 def _replay(G, order, p, lo, hi, old):
-    qs, deps = G; d0, d1 = p["d0"], p["d1"]
+    qs, deps = G; d0, d1 = p["d0"], p["d1"]; wake = p["wake"]
     fin, end, by = (old[0][:], old[1][:], old[2][:]) if lo else ([0.0] * len(qs), [0.0] * len(qs), [-1] * len(qs))
     last = [-1] * 12; free = [0.0] * 12; j = lo; left = 5
     while j and left:
@@ -99,8 +108,12 @@ def _replay(G, order, p, lo, hi, old):
             last[q] = n; free[q] = fin[n]; left -= q < 5
     for n in order[lo:hi]:
         q = qs[n]; t = free[q]; w = last[q]
-        for m in deps[n]:
-            if end[m] > t: t = end[m]; w = m
+        if q == 3:
+            for m in deps[n]:
+                if end[m] + wake > t: t = end[m] + wake; w = m
+        else:
+            for m in deps[n]:
+                if end[m] > t: t = end[m]; w = m
         free[q] = fin[n] = t + d0[n]; end[n] = t + d1[n]; by[n] = w; last[q] = n
     return fin, end, by
 
@@ -133,10 +146,10 @@ def _schedule(ops):
         tm = _times(ops, q); q["d0"] = [a for a, b in tm]; q["d1"] = [b + q["lat"] * (o["kind"] != "r") for (a, b), o in zip(tm, ops)]
     p = PACE[0]; tm = _times(ops, p); d0 = p["d0"]; fw = [[] for _ in ops]; on = [[] for _ in ops]
     for i, o in enumerate(ops):
-        for m, lat in [(m, p["lat"]) for m in deps[i]] + [(m, tm[m][0] - tm[m][1]) for m in o["soft"]]:
+        for m, lat in [(m, p["lat"] + p["wake"] * (qs[i] == 3)) for m in deps[i]] + [(m, tm[m][0] - tm[m][1]) for m in o["soft"]]:
             fw[i].append((m, tm[m][1] + lat)); on[m].append((i, tm[m][1] + lat))
     pre = [set(m for m, _ in fw[i]) for i in range(n)]
-    wide = [i for i, o in enumerate(ops) if "wide" in o]; gates = [i for i, o in enumerate(ops) if o.get("gate")]
+    wide = [i for i, o in enumerate(ops) if "wide" in o or (o["w"] and o["w"][0][0] in MARKS)]; gates = [i for i, o in enumerate(ops) if o.get("gate")]
     names = sorted(set(o["tag"] for o in ops)); tag = [names.index(o["tag"]) for o in ops]
 
     def draw(k):
@@ -173,7 +186,7 @@ def _schedule(ops):
         goal = gates[stage] if stage < len(gates) else -1; first = gates[stage - 1] if 0 < stage <= len(gates) else 0
         marks = [i for i in wide if first <= i and (goal < 0 or i < goal)]
         st = [_replay(G, best[1], q, 0, n, None) for q in PACE]
-        cur = best = (value(st, goal, marks), best[1], st); pos = None
+        cur = best = (value(st, goal, marks), best[1], st); pos = None; taken = 0
         for k in range(moves):
             u = draw(6); order = cur[1]; heat = HEAT * u[3] ** 2 * (1.0 - k / moves)
             if pos is None:
@@ -193,7 +206,7 @@ def _schedule(ops):
                     j = by[j]
             pairs = ways[w]
             if not pairs: continue
-            a, b = pairs[int(u[0] * (len(pairs) if w[1] == goal else min(len(pairs), 30)))]; lo, hi = pos[a], pos[b]; hop = int(1 + 12 * u[2] ** 3)
+            a, b = pairs[int(u[0] * (len(pairs) if w[1] == goal else min(len(pairs), 30)))]; lo, hi = pos[a], pos[b]; hop = int(1 + HOP * u[2] ** 4)
             if u[1] < 0.5:
                 while hop > 1 and lo > 0:
                     lo -= 1; hop -= qs[order[lo]] == qs[b]
@@ -212,9 +225,11 @@ def _schedule(ops):
             order = order[:lo] + new + order[hi + 1:]; stop = max(cut, hi + 1)
             st = [_replay(G, order, q, lo, stop, s) for q, s in zip(PACE, cur[2])]; v = value(st, goal, marks)
             if v < cur[0] + heat:
-                fin = st[0][0]; at = {m: j for j, m in enumerate(order)}
-                order[:stop] = sorted(order[:stop], key=lambda j: (fin[j] - d0[j], at[j]))
-                cur = (v, order, st); pos = None
+                for j, m in enumerate(new): pos[m] = lo + j
+                ways = {}; cut = pos[goal] + 1 if goal >= 0 else n; taken += 1
+                if taken % 40 == 0:
+                    fin = st[0][0]; order[:stop] = sorted(order[:stop], key=lambda j: (fin[j] - d0[j], pos[j])); pos = None
+                cur = (v, order, st)
                 if v < best[0]: best = cur
     return best[1]
 
@@ -265,7 +280,7 @@ def rank_program(g, core, T, topo):
         elif len(aps) > 1 and len(aps[1]) > 3: cost = ("ga", size(aps[0]), 50 if q == "V" else 65)
         elif fn == "tensor_tensor": cost = ("e", size(aps[0]), 1 if any(a[2][0][0].startswith("pb") for a in aps[1:]) else 2)
         else: cost = ("e", size(aps[min(1, len(aps) - 1)]), 0.5 if q == "V" and all(wide(a) == 2 for a in aps[:2]) else 1)
-        ops.append(dict(tag=piece[0] + (fn[:3] + q) * (piece[0] == "set"), cost=cost, q=q, fn=fn, a=[x[1] if isap(x) else x for x in args],
+        ops.append(dict(tag=piece[0] + (fn[:3] + q + str(len(ops) * (q == "G"))) * (piece[0] == "set"), cost=cost, q=q, fn=fn, a=[x[1] if isap(x) else x for x in args],
                         k={n: (x[1] if isap(x) else x) for n, x in (kw or {}).items()}, w=w, r=r, kind=kind))
 
     def part(name, *k):
@@ -307,8 +322,9 @@ def rank_program(g, core, T, topo):
         emit(q, "dma_start", [o, src], kind="d")
         loaded[0] += ops[-1]["cost"][1] + 48000; ops[-1]["cost"] = ("dma", loaded[0], 0)
 
-    def store(q, dst, i):
+    def store(q, dst, i, size):
         emit(q, "dma_start", [dst, i[1]], kind="d", extra=([], i[2]))
+        ops[-1]["cost"] = ("dma", size, 0)
 
     Kp, P5, R0c, P3, P15, PKc = [C("Kp", j) for j in range(6)]
     EQ, GEQ, GT, NE = OP.is_equal, OP.is_ge, OP.is_gt, OP.not_equal
@@ -329,13 +345,18 @@ def rank_program(g, core, T, topo):
 
     ms(A("ONE"), 1.0); ms(A("TWO"), 2.0); ms(A("ONEf"), 1.0); ms(A("Lz", 0, 8), 0.0); ms(A("EW"), 0.0); ms(A("ONEs"), 1.0)
     iota(C("Ki0", 0), [[0, 1]], 0, 1)
-    sel(A("ID"), A("ONE"), [[-1, 128]], EQ, 0, 1)
-    iota(A("T17"), [[1, 18]])
+    iota(A("T17"), [[1, 20]])
+    iota(A("BLKt"), [[1, 128]])
+    iota(A("M16"), [[1, 8], [0, 16]])
     iota(A("A1"), [[16, 64]])
-    sel(A("BLKt"), A("ONE"), [[-16, 8], [0, 16]], GEQ, 0, 1)
-    sel(A("BLK"), A("BLKt"), [[16, 8], [0, 16]], GEQ, 15, -1)
+    cp(C("Kp", 13), C("Ki0", 0)); ts(C("Ki0", 2), C("Ki0", 0), 4, SHR); cp(C("Kp", 14), C("Ki0", 2))
+    ts(A("ID"), A("BLKt"), C("Kp", 13), EQ); ts(A("BLK"), A("M16"), C("Kp", 14), EQ)
+    sel(A("S7"), A("ONEf"), [[-16, 8], [0, 16]], EQ, -7, 1)
     sel(A("TRI"), A("BLK"), [[1, 128]], GEQ, 0, -1)
     sel(A("UP"), A("BLK"), [[-1, 128]], GT, 0, 1)
+    sel(A("S15"), A("ONEf"), [[-16, 8], [0, 16]], EQ, -15, 1)
+    iota(A("LAN"), [[1, 3], [48, 6]])
+    for o in ops: o["head"] = o["q"] == "G"
     ts(C("Ki0", 1), C("Ki0", 0), 15, AND)
     cp(Kp, C("Ki0", 1))
     ts(A("SL"), A("A1", 0, 16), Kp, ADD); ts(A("IDu"), A("A1", 0, 32), Kp, ADD)
@@ -345,23 +366,19 @@ def rank_program(g, core, T, topo):
     ts(P5, Kp, 5.0, MUL); ts(R0c, Kp, 0.0, EQ); ts(P3, Kp, 3.0, MUL); ts(P15, Kp, 15.0, MUL)
     ts(PKc, Kp, -80.0, MUL, TOP - 15, ADD)
     for t in range(RO): ts(C("Kp", 8 + t), R0c, float(NB + P * t - 1024), MUL, 1024.0, ADD)
-    sel(A("S7"), A("ONEf"), [[-16, 8], [0, 16]], EQ, -7, 1)
-    sel(A("S15"), A("ONEf"), [[-16, 8], [0, 16]], EQ, -15, 1)
     ts(A("EW", 15, 143, 16), A("BLK", 0, 128, 16), 32768.0, MUL)
-    iota(A("LAN"), [[1, 3], [48, 6]])
     ts(A("LAN"), A("LAN"), P3, ADD)
-    ms(A("RST"), 0.0); ms(A("RST", 0, 160, 16), TOP)
+    ms(A("RST"), 0.0); ms(A("RST", 15, 160, 16), 1024.0); ms(A("RSU"), 0.0); ms(A("RSU", 15, 160, 16), 1023.5)
     ms(A("PK2"), -1.0); ms(A("PK2", 15, 80, 16), TOP)
     ms(A("PK1"), 0.0); ts(A("PK1", 15, 80, 16), A("T17", 0, 5), -16.0, MUL, PKc, ADD)
     ms(A("QD0"), 1.0); ms(A("QD0", 0, 60, 4), 0.0); ms(A("QD0", 2, 60, 4), 2.0 ** 19)
     ms(A("QD1", 1, 60, 4), -12.0 / 2 ** 24); ms(A("QD1", 2, 60, 4), RND); ms(A("QD1", 3, 60, 4), -RND)
-    part("zr")
-    for c in range(3): act(A("Zp", 80 * c, 80 * c + 80), A("Z", c, P, 3), AF.Copy)
-    for k in range(16): act(A("ZR", k, 3840, 16), A("Zp"), AF.Copy)
 
     def mask(j):
-        lo, hi = SPANS[j]; part("mask", j < 4)
-        ts(A("MK", 128 * j, 128 * j + 128), A("ID"), C("GE", lo), MUL, C("LTt", hi), MUL)
+        lo, hi = SPANS[j]; part("mask", j < 4, j in MKS)
+        if j in MKS: act(A("MK", 128 * j, 128 * j + 128), A("ID"), AF.Copy, scale=C("SPN", 16 * (hi - lo - 1) + lo))
+        else: ts(A("MK", 128 * j, 128 * j + 128), A("ID"), C("SPN", 16 * (hi - lo - 1) + lo), MUL)
+        ops[-1]["idle"] = True
 
     def bh(t, n0, n1):
         per, stp, plan = PLANS[t]; part("bh", t, n0)
@@ -370,10 +387,12 @@ def rank_program(g, core, T, topo):
             mm(A("pb6", rho + per * n0, rho + per * (n1 - 1) + 1, per), A("MK", 128 * k, 128 * k + 128),
                A("Rh", v + stp * n0, v + stp * (n1 - 1) + 1, stp), lo == 0, hi == 16, lo > 0)
         ts(A(BH(t), n0 * per, n1 * per), A("pb6", n0 * per, n1 * per), 1024.0, ADD)
+        if n0 == 0: ops[-1]["early"] = t - 1
 
     def xh(t, c0, c1, nb):
-        for c in range(c0, c1, XC):
-            d = min(c + XC, c1); part("xh", t, c0, c // 64)
+        cuts = [c for c in range(c0, c1) if (c % XCV == 0 if XV[t][0] <= c <= XV[t][1] else (c - c0) % XC == 0) or c == c0] + [c1]
+        for c, d in zip(cuts, cuts[1:]):
+            part("xh", t, c0, c // 64)
             o, i = A(XH(t), 16 * c, 16 * d), IN(A("X", 0, nb), A(BH(t), c, d))
             if XV[t][0] <= c < XV[t][1]: cp(o, i)
             else:
@@ -397,8 +416,13 @@ def rank_program(g, core, T, topo):
     tu(A("p0u"), A("A2"), A("e0"), A("rho"), ADD)
     mm(A("pb4", 0, 2), A("S7"), A("rho", 41, 57, 15), True, True)
     mm(A("pb4", 2, 3), A("S15"), C("rho", 63), True, True)
-    ts(A("GE"), A("T17"), Kp, OP.is_le); ts(A("LTt"), A("T17"), Kp, GT)
+    part("spans")
+    ts(A("GE"), A("T17", 0, 16), Kp, OP.is_le); ts(A("LTt"), A("T17"), Kp, GT)
+    for w in range(4): tt(A("SPN", 16 * w, 16 * w + 16), A("GE"), A("LTt", w + 1, w + 17), MUL)
     for j in range(len(SPANS)): mask(j)
+    part("zr")
+    for c in range(3): act(A("Zp", 80 * c, 80 * c + 80), A("Z", c, P, 3), AF.Copy); ops[-1]["busy"] = True
+    for k in range(ZRA): act(A("ZR", k, 3840, 16), A("Zp"), AF.Copy)
     part("lr")
     cp(A("CN", 0, 3), A("pb4", 0, 3))
     ts(A("s0"), A("LAN"), C("CN", 0), ADD)
@@ -406,9 +430,11 @@ def rank_program(g, core, T, topo):
     tu(A("LR"), A("s2"), A("s0"), A("s1"), SUB)
     for b in range(2):
         part("rh", b)
-        act(A("Rh", 512 * b, 512 * b + 512), IN(A("Ri", 512 * b, 512 * b + 512), A("IDu")), AF.Identity, bias=-1024.0)
+        act(A("Rh", 512 * b, 512 * b + 512), IN(A("Ri", 512 * b, 512 * b + 512), A("IDu")), AF.Identity, bias=-1024.0); ops[-1]["early"] = -2
         part("sc", b)
-        cp(IN(A("BIG", CI, R1), A("p0u", 32 * b, 32 * b + 32)), A("Ri", 512 * b, 512 * b + 512))
+        cp(IN(A("BIG", CI, R1), A("p0u", 32 * b, 32 * b + 32)), A("Ri", 512 * b, 512 * b + 512)); ops[-1]["busy"] = True
+    part("zr", 1)
+    for k in range(ZRA, 16): act(A("ZR", k, 3840, 16), A("Zp"), AF.Copy); ops[-1]["after"] = -2
     bh(0, 0, 256)
     xh(0, 0, 256, NB)
     piece[0] = "set"
@@ -421,10 +447,8 @@ def rank_program(g, core, T, topo):
         mm(A("pb7", 0, 128), A("ID"), A("RK", 128 * j - 128, 128 * j), False, True)
         act(A("RT", 128 * j - 128, 128 * j), A("pb7", 0, 128), AF.Copy)
     iota(A("MT"), [[1, 16], [0, 5]])
-    iota(A("PBS"), [[2048, 16], [0, 5]], KOFF)
     sel(A("G8t", p=(0, 8)), A("ONEf", p=(0, 8)), [[1, 128]], GEQ, 0, -16)
     sel(A("G8", p=(0, 8)), A("G8t", p=(0, 8)), [[-1, 128]], GEQ, 15, 16)
-    sel(A("IDf"), A("ONEf"), [[-1, 128]], EQ, 0, 1)
     iota(S15("NFL"), [[80, 3], [1, 5]], 960)
     act(A("BLKf"), A("BLK"), AF.Copy)
     sel(A("BK1"), A("BLK"), [[0, 8], [1, 16]], GT, 0, 0)
@@ -443,7 +467,7 @@ def rank_program(g, core, T, topo):
     gcp(A("BIG", CJ, CJ + P), A("BIG", CI, CI + P), P)
     part("tables")
     ts(A("E0"), A("ID"), R0c, MUL)
-    ts(A("BGM"), A("C16"), Kp, NE, 2048.0, MUL)
+    ts(A("BGM"), A("C16"), Kp, NE, 1024.0, MUL)
     ts(C("WKf", 0), C("WK", 0), 2048.0, GEQ); ts(C("WKf", 1), C("WK", 0), 2.0 ** -12, MUL)
     cp(C("WKf", 2), C("WK", 1))
     ts(C("WKf", 3), C("WKf", 1), C("WKf", 0), SUB)
@@ -453,10 +477,15 @@ def rank_program(g, core, T, topo):
     mm(A("pb5", 0, 80), A("BLKf"), A("RK2"), True, True)
     mm(A("pb5", 80, 82), A("G8", p=(0, 8)), A("TCf", 0, 2, p=(0, 8)), True, True)
     ts(A("KT"), A("pb5", 0, 80, 5), 4096.0, MUL)
-    tt(A("PAY"), A("pb5", 0, 80), A("PBS"), ADD)
+    ts(C("Kp", 6), Kp, 1.0, EQ, 2048.0, MUL); ts(C("Kp", 7), Kp, 2.0, EQ, -63.0, MUL)
+    ts(A("PBS"), A("MT"), C("Kp", 6), MUL, C("Kp", 7), ADD)
+    ts(A("RK2"), A("pb5", 0, 80), R0c, MUL)
+    tt(A("PAY"), A("RK2"), A("PBS"), ADD)
+    ts(C("Kp", 11), Kp, 2.0, EQ, 2.0 ** 18, MUL); ts(C("Kp", 12), Kp, 2.0, OP.is_lt, C("Kp", 11), ADD)
+    ts(A("PL"), A("BLK"), C("Kp", 12), MUL)
     ts(C("TH", 0), A("pb5", 80, 81), 32768.0, MUL, float(KOFF), ADD)
     cp(C("TH", 1), A("pb5", 81, 82))
-    ts(C("TH", 4), C("TH", 0), -1.0, MUL, 1.0, ADD); ts(C("TH", 3), C("TH", 4), 8192.0, MUL)
+    ms(A("FM0", 0, 30, 2), 0.0); ms(A("NEG"), -1.0)
     act(S15("NFL"), S15("NFL"), AF.Identity, bias=P5)
     act(S15("LOC"), S15("SL"), AF.Identity, bias=4096.0)
     act(A("NID"), A("ID"), AF.Copy, scale=-1.0)
@@ -478,12 +507,13 @@ def rank_program(g, core, T, topo):
         if t == 0:
             tt(C("CN", 3), C("CN", 2), C("CN", 1), SUB)
             ts(A("msk"), A("LAN"), C("CN", 3), GEQ)
-            ts(A("s3"), A("LAN"), C("CN", 3), GEQ, C("CN", 2), MUL)
+            ts(C("CN", 4), C("CN", 2), float(P), ADD)
+            ts(A("s3"), A("LAN"), C("CN", 3), GEQ, C("CN", 4), MUL)
             ts(A("s0"), A("LAN"), C("CN", 1), ADD, float(CI), ADD)
             tt(A("bas"), A("s0"), A("s3"), SUB)
         else:
             ts(A("msk"), A("LAN"), C("CN", 10), GEQ)
-            ts(A("s3"), A("LAN"), C("CN", 10), GEQ, float(CJ - CI), MUL)
+            ts(A("s3"), A("LAN"), C("CN", 10), GEQ, float(CJ - CI - P), MUL)
             ts(A("s0"), A("LAN"), C("CN", 10), SUB, float(CI), ADD)
             tt(A("bas"), A("s0"), A("s3"), ADD)
 
@@ -497,11 +527,13 @@ def rank_program(g, core, T, topo):
     def step2(t, c):
         bank = "pb%d" % c; o = 1280 * c; p = 0; n0 = 80 * c; part("s2", t, c)
         cp(A("RES", n0, n0 + 80), IN(A("BIG", CI if t == 0 else 0, (R1, R1, CJ + P)[t]), A("LR", 6 * c, 6 * c + 5)))
-        for n in CH2[t][c]:
+        if t + c == 0: ops[-1]["after"] = -1
+        for j, n in enumerate(CH2[t][c]):
             a, b = o + 80 * p, o + 80 * (p + n)
             tt(A("D2", a, b), IN(A("X", 0, NB + P * t), A("RES", a // 16, b // 16)), A("ZR", a, b), SUB)
             ops[-1]["wide"] = "V"; ops[-1]["gate"] = t and a == 0
-            act(A("A2w", a, b), A("D2", a, b), AF.Relu, scale=-1.0 / 1024)
+            if (c, j) in RV2[t]: ts(A("A2w", a, b), A("D2", a, b), -1.0 / 1024, MUL, 0.0, OP.max)
+            else: act(A("A2w", a, b), A("D2", a, b), AF.Relu, scale=-1.0 / 1024)
             if a == 0: ops[-1]["opens"] = t
             for r in range(p, p + n):
                 mm(A(bank, 0, 80), A("EW", 15 - r, 143 - r), A("A2w", o + 80 * r, o + 80 * r + 80), r == 0, r == 15, r > p)
@@ -539,13 +571,17 @@ def rank_program(g, core, T, topo):
         for j in range(w):
             mm(A(bank, 80 * j, 80 * j + 80), A("ID"), A("BGM"), True, False)
             mm(A(bank, 80 * j, 80 * j + 80), A("W16"), A(YB(t), 640 * (c + j), 640 * (c + j) + 80), False, True)
-        scan(A("SU", n0, n1), A("RST", 0, 80 * w), A(bank, 0, 80 * w), ADD, MIN)
-        raw = A("SU", n0 + 15, n1, 16); ri = A("ri", 5 * c, 5 * (c + w))
-        ts(ri, raw, -0.5, ADD)
+        raw = A("SU", n0 + 15, n1, 16); ri = A("SV", n0 + 15, n1, 16)
+        scan(A("SU", n0, n1), A(bank, 0, 80 * w), A("RST", 0, 80 * w), MIN, ADD, 4096.0)
+        if SCAN32: scan(A("SV", n0, n1), A(bank, 0, 80 * w), A("RSU", 0, 80 * w), MIN, ADD, 4096.0)
+        else: ts(ri, raw, -0.5, ADD)
         tt(A("QD1", s0, s1, 4), raw, ri, SUB); tt(A("QD0", s0 + 1, s1, 4), raw, ri, SUB)
         scan(A("QS", s0, s1), A("QD0", s0, s1), A("QD1", s0, s1), MUL, ADD)
         for c in cs:
-            for k in range(5): ts(A("Hi", 80 * c + k, 80 * c + 80, 5), A("KT"), C("QD1", 20 * c + 4 * k), MUL, C("QS", 20 * c + 4 * k + 3), ADD)
+            for k in range(5):
+                o, u, q = A("Hi", 80 * c + k, 80 * c + 80, 5), C("QD1", 20 * c + 4 * k), C("QS", 20 * c + 4 * k + 3)
+                if (c, k) in HIS[t]: act(o, A("KT"), AF.Identity, scale=u, bias=q)
+                else: ts(o, A("KT"), u, MUL, q, ADD)
         au(A("Hu", n0, n1), A("Hj", n0, n1), A("Hi", n0, n1), 4095, AND)
 
     def step5(t, c):
@@ -563,37 +599,61 @@ def rank_program(g, core, T, topo):
             else:
                 tt(A("D5", a, b), x, A(YB(t), 640 * c, 640 * c + 80 * n), SUB)
                 ops[-1]["wide"] = "V"
+                if j == 0 and EARLY < 3 and c == ORD5[EARLY]: ops[-1]["after"] = t
                 act(A("A5", a, b), A("D5", a, b), AF.Abs)
             m += n
         m = 0
         for n in GR5[c]:
-            out = A(bank, 5 * m, 5 * (m + n))
-            mm(out, A("IDf"), A("PAY", 5 * m, 5 * (m + n)), True, False)
+            out = A(bank, 5 * m, 5 * (m + n)) if c == ORD5[2] or not TREE else A("pb%d" % ORD5[0], ORD5.index(c), 160, 2)
+            mm(out, A("PL"), A("PAY", 5 * m, 5 * (m + n)), True, False)
             for r in range(16): mm(out, A("EW", 15 - r, 143 - r), A("A5", o + 80 * m + r, o + 80 * (m + n), 16), False, r == 15, r > 0)
             m += n
         part("least", t, c)
-        for k in range(5): emit("V", "tensor_reduce", [C("K", 5 * c + k), A(bank, k, 80, 5), AxisListType.X, MIN])
-        ts(A("fw", c, 15, 3), A("K", 5 * c, 5 * c + 5), C("TH", 0), OP.is_lt, -1.0 if c == 2 else 1.0, MUL)
-        if c == 0 and t: mm(A("pb4", 0, 1), A("IDf"), C("Bp", 0), True, False)
-        for k in range(5): mm(A("pb4", 0, 1), A("TWO" if c == 2 else "ONE"), C("fw", 3 * k + c), c + k + t == 0, c == 2 and k == 4, k > 0)
+        if TREE and c == ORD5[0]: return
+        if TREE and c == ORD5[1]:
+            bank = "pb%d" % ORD5[0]
+            act(A("AC", 0, 80), A(bank, 80, 160), AF.Copy)
+            tt(A("AC", 80, 160), A(bank, 0, 80), A("AC", 0, 80), MIN)
+            tt(A("AC", 0, 40), A("AC", 80, 120), A("AC", 120, 160), MIN)
+            tt(A("AC", 40, 60), A("AC", 0, 20), A("AC", 20, 40), MIN)
+            for i in range(2):
+                tt(A("Ki", 5 * ORD5[i], 5 * ORD5[i] + 5), A("AC", 40 + i, 50, 2), A("AC", 50 + i, 60, 2), MIN)
+                forks(t, ORD5[i])
+            return
+        for k in range(5): emit("V", "tensor_reduce", [C("Ki" if RED32 else "K", 5 * c + k), A(bank, k, 80, 5), AxisListType.X, MIN])
+        forks(t, c)
+
+    def forks(t, c):
+        ts(A("fw", 16 * t + c, 16 * t + 15, 3), A("Ki" if RED32 else "K", 5 * c, 5 * c + 5), C("TH", 0), OP.is_lt, -1.0 if c == 2 else 1.0, MUL)
+        for u in range(t + 1) if c == ORD5[0] else (t,):
+            for e in (range(3) if u < t else (c,)):
+                mm(A("pb4", 0, 5), A("TWO" if e == 2 else "ONE"), A("fw", 16 * u + e, 16 * u + 15, 3), c == ORD5[0] and u == 0 and (e == 0 or t == 0), c == ORD5[2], 0 < u + e and u < t)
 
     def close(t):
         last = t == RO - 1; TT = T0 + P * t; lv = A("LV", 16 * t, 16 * t + 15); part("ring", t)
-        act(S15("uf"), A("QD1", 0, 60, 4), AF.Copy, scale=4096.0)
-        cp(S15("Ki"), S15("K"))
-        ts(S15("kp"), S15("Ki"), 2047, AND)
-        act(S15("nf"), S15("K"), AF.Relu, bias=C("TH", 3), scale=8192.0)
-        tt(S15("t1"), S15("kp"), S15("uf"), MUL)
-        tt(S15("t2"), S15("t1"), A("QS", 3, 60, 4), ADD)
+        if not RED32: cp(S15("Ki"), S15("K"))
+        ts(S15("nf"), S15("Ki"), C("TH", 0), GEQ, 8192.0, MUL)
+        if SCANIN:
+            act(A("FM0", 1, 30, 2), A("QD1", 0, 60, 4), AF.Copy, scale=4096.0)
+            cp(A("FM1", 1, 30, 2), A("QS", 3, 60, 4))
+            ts(A("FM1", 0, 30, 2), S15("Ki"), 2047, AND)
+            scan(A("FM2"), A("FM0"), A("FM1"), MUL, ADD)
+            t2 = A("FM2", 1, 30, 2)
+        else:
+            act(S15("uf"), A("QD1", 0, 60, 4), AF.Copy, scale=4096.0)
+            ts(S15("kp"), S15("Ki"), 2047, AND)
+            tt(S15("t1"), S15("kp"), S15("uf"), MUL)
+            tt(S15("t2"), S15("t1"), A("QS", 3, 60, 4), ADD)
+            t2 = S15("t2")
         if t == 0:
-            au(S15("L1"), S15("a12"), S15("t2"), 2, SHR, 1023, AND)
-        ts(S15("hh"), S15("t2"), 4095, AND)
+            au(S15("L1"), S15("a12"), t2, 2, SHR, 1023, AND)
+        ts(S15("hh"), t2, 4095, AND)
         if t:
-            ts(S15("a12"), S15("t2"), 12, AND)
+            ts(S15("a12"), t2, 12, AND)
             ts(S15("x1"), S15("hh"), TT / 4096.0, MUL, -255.0 / 512, ADD)
             ts(S15("x2"), S15("a12"), TM / 4.0, MUL)
             tu(S15("L1"), S15("ix"), S15("x1"), S15("x2"), ADD)
-        ts(S15("a3"), S15("t2"), 3, AND)
+        ts(S15("a3"), t2, 3, AND)
         win = A("R4", 0, 3 * TM + TT) if t else A("R0")
         cp(A("RC", 0, min(P, 16 * RCV)), IN(win, A("L1", 0, min(15, RCV))))
         if RCV < 15: act(A("RC", 16 * RCV, P), IN(win, A("L1", RCV, 15)), AF.Copy)
@@ -610,19 +670,19 @@ def rank_program(g, core, T, topo):
         ts(A("NEW", 0, 128), IN(A("WT"), A("L2", 0, 8)), C("Kp", 8 + t), ADD)
         act(A("NEW", 128, P), IN(A("WT"), A("L2", 8, 15)), AF.Identity, bias=C("Kp", 8 + t))
         part("marks", t)
-        ts(lv, S15("fw"), A("pb4", 0, 1), MUL, C("TH", 1), OP.is_le)
+        fw = A("fw", 16 * t, 16 * t + 15)
+        emit("V", "tensor_reduce", [C("dB", 0), A("pb4", 0, 5), AxisListType.X, ADD])
+        ts(lv, fw, C("dB", 0), MUL, C("TH", 1), OP.is_le)
         if not last:
-            ts(S15("dead"), S15("fw"), A("pb4", 0, 1), MUL, C("TH", 1), GT)
-            cp(C("Bp", 0), A("pb4", 0, 1))
-            scan(S15("cum"), A("ONEs", 0, 15), lv, MUL, ADD)
-            tt(S15("e1"), S15("dead"), S15("IDX"), MUL)
+            scan(S15("cum"), S15("NEG"), lv, ADD, ADD)
+            tt(S15("e1"), lv, S15("IDX"), MUL)
             mm(A("pb4", 0, 1), A("UPI"), C("cum", 14), True, True)
             mm(A("pb4", 1, 2), A("BLK"), C("cum", 14), True, True, True)
             if t == 0: mm(A("pb4", 2, 3), A("GE8"), C("cum", 14), True, True, True)
-            tt(S15("e3"), S15("cum"), S15("e1"), SUB)
-            for c in range(3): ts(A("LP", 5 * c, 5 * c + 5), A("e3", c, 15, 3), A("pb4", 0, 1), SUB, P - 1.0, ADD)
+            tt(S15("e3"), S15("cum"), S15("e1"), ADD)
+            for c in range(3): ts(A("LP", 5 * c, 5 * c + 5), A("e3", c, 15, 3), A("pb4", 0, 1), SUB)
             ts(A("pf1"), A("msk"), A("pb4", 1, 2), MUL)
-            if t == 0: cp(C("CN", 10), A("pb4", 2, 3))
+            if t == 0: ts(C("CN", 10), A("pb4", 2, 3), P / 2.0, ADD)
             tu(A("LR"), A("pf2"), A("bas"), A("pf1"), SUB)
             cp(IN(A("BIG", R1 * t, R1 * t + P), S15("LP")), A("NEW"))
             part("yt", t)
@@ -639,9 +699,9 @@ def rank_program(g, core, T, topo):
         act(A("EF"), A("pb5", 0, P), AF.Identity, bias=191.75, scale=0.5)
         act(A("X", NB + P * t, NB + P * t + P), IN(A("EF"), S15("NBu")), AF.Identity, bias=-192.0)
         part("store", t)
-        store("Y", T.ya[:, P * t:P * t + P], lv)
-        store("Y", T.yx[:, P * t:P * t + P], A("X", NB + P * t, NB + P * t + P))
-        store("Y", T.yt[:, P * t:P * t + P], A("YT", P * t, P * t + P))
+        store("Y", T.ya[:, P * t:P * t + P], lv, 500000)
+        store("Y", T.yx[:, P * t:P * t + P], A("X", NB + P * t, NB + P * t + P), 200000)
+        store("Y", T.yt[:, P * t:P * t + P], A("YT", P * t, P * t + P), 170000)
 
     OLD = (None, 12, 26)
     for t in range(RO):
@@ -664,7 +724,7 @@ def rank_program(g, core, T, topo):
         keep(t)
         for c in range(3): spread(t, c)
         for cs in GR4: step4(t, cs)
-        for c in range(3): step5(t, c)
+        for c in ORD5: step5(t, c)
         close(t)
 
     seen = {}; bank = {}
@@ -689,9 +749,11 @@ def rank_program(g, core, T, topo):
         if o["kind"] == "arr": deps = set(); soft = {n - 1}
         if o["kind"] == "d" and o["w"]:
             soft.update(m for m in range(n) if ops[m]["kind"] == "d" and ops[m]["q"] == o["q"])
-        if o["q"] == "G" and o["tag"][:3] == "set": soft.update([m for m in range(n) if ops[m]["q"] == "G"][-1:])
+        if o.get("head"): soft.update([m for m in range(n) if ops[m]["q"] == "G"][-1:])
+        if "busy" in o: soft.update(m for m in range(n) if "idle" in ops[m] and ops[m]["q"] == o["q"])
         if "wide" in o: soft.update([m for m in range(n) if ops[m].get("wide") == o["wide"]][-1:])
         if "opens" in o: soft.update(m for m in range(n) if ops[m].get("ahead") == o["opens"])
+        if "after" in o: soft.update(m for m in range(n) if ops[m].get("early") == o["after"])
         soft.discard(n)
         o["deps"] = sorted(deps); o["soft"] = sorted(soft)
     if not ORDER: ORDER.extend(_schedule(ops))
@@ -704,11 +766,13 @@ def rank_program(g, core, T, topo):
         for m in o["deps"]:
             key = ops[m]["q"] if ops[m]["kind"] == "c" else m
             if key not in best or pos[best[key]] < pos[m]: best[key] = m
-        need = []
-        for key, m in best.items():
-            if got[o["q"]].get(key, -1) < pos[m]:
-                got[o["q"]][key] = pos[m]; need.append(m); ops[m]["sig"] = True
-        o["need"] = need
+        need = []; know = got[o["q"]]
+        for key, m in sorted(best.items(), key=lambda x: -pos[x[1]]):
+            if know.get(key, -1) < pos[m]:
+                know[key] = pos[m]; need.append(m); ops[m]["sig"] = True
+                for k2, at in ops[m].get("know", {}).items():
+                    if know.get(k2, -1) < at: know[k2] = at
+        o["need"] = need; o["know"] = dict(know)
     cnt = {q: 0 for q in Q}; nd = 0; sent = 0; tail = []
     for n in ORDER:
         o = ops[n]

from concourse.bass import DstId, RemoteDMATransfer
from concourse.mybir import AluOpType as OP, AxisListType, ActivationFunctionType as AF

NB, T0, P, RO = 2048, 1024, 240, 3
TM = T0 + P * (RO - 1)
CI, R1, CJ = 240, 1264, 1504
KOFF = -63 * 2 ** 18
TOP = 65536.0
RND = 1.5 * 2 ** 23
F, H, I, U, B = "float32", "float16", "int32", "uint16", "bfloat16"


def _plan(T):
    per = 1
    while (per * 16 * T) % 4096: per *= 2
    out = []
    for rho in range(per):
        vs = [((16 * rho + a) * T) >> 12 for a in range(16)]
        for v in sorted(set(vs)):
            a = [i for i in range(16) if vs[i] == v]
            out.append((rho, v, a[0], a[-1] + 1))
    return per, per * 16 * T // 4096, out


PLANS = [_plan(T0 + P * t) for t in range(RO)]
SPANS = []
for _p in PLANS:
    for _x in _p[2]:
        if _x[2:] not in SPANS: SPANS.append(_x[2:])

_S = dict(
    X=(2768, B), Ri=(1024, I), Z=(240, B), Zp=(240, B), Lt=(64, I), Lb=(64, B), Lz=(72, B), rho=(64, F), A1=(64, F), A2=(64, F), e0=(64, F), p0u=(64, U), IDu=(32, U),
    BIG=(1744, F), Rh=(TM, H), R0=(1024, F), R4=(4 * TM, F), ZR=(3840, B), D2=(3840, B), A2w=(3840, B), D5=(3840, B), A5=(3840, B),
    XHa=(4336, B), XHb=(4336, B), BHa=(256, U), BHb=(256, U), RES=(240, U), RESh=(240, H), WT=(1200, F), RC=(240, H), NEW=(240, F), YT=(720, F),
    YS=(480, B), YB0=(1920, B), YB1=(1920, B), YB2=(1920, B), EE=(240, B), EF=(240, B), LN=(480, B), E0=(128, B), LV=(48, F),
    ONE=(128, B), TWO=(128, B), ONEf=(128, F), BLK=(128, B), BLKt=(128, B), BLKf=(128, F), EW=(144, B), TRI=(128, B), UP=(128, B), UPI=(128, B), GE8=(128, B),
    S7=(128, F), S15=(128, F), S15b=(128, B), ID=(128, B), NID=(128, B), G8=(128, F), G8t=(128, F), BK1=(128, B), SH=(512, B),
    RS=(384, B), RK=(384, B), RT=(384, B), MK=(128 * len(SPANS), B), W16=(128, H),
    Ki0=(4, I), M16=(128, B), Kp=(16, F), T17=(20, F), GE=(16, F), LTt=(20, F), SPN=(64, F), C16=(80, F), BGM=(80, B), RST=(160, F), RSU=(160, F), SV=(240, I), FM0=(30, F), FM1=(30, I), FM2=(30, I), PK1=(80, F), PK2=(80, F),
    MT=(80, F), PBS=(80, F), RK2=(80, F), PAY=(80, H), PL=(128, B), AC=(160, F), NEG=(16, F), dB=(2, F), KT=(16, F), WK=(4, I), WKf=(4, F),
    TC=(4, I), TCf=(4, F), TH=(8, F), CN=(16, F), SL=(16, F), IDX=(16, F), NFL=(16, F), LOC=(16, F), LAN=(18, F),
    s0=(18, F), s1=(18, F), s2=(18, F), s3=(18, F), s4=(16, F), i0=(16, I), NBu=(16, U), LR=(18, U),
    SC1=(240, F), SC2=(240, F), SU=(240, F), kf=(16, F), LY=(18, U), ri=(16, I), QD0=(60, F), QD1=(60, F), QS=(60, F), uf=(16, F),
    Hi=(240, I), Hj=(240, I), Hu=(240, U), K=(16, F), Ki=(16, I), nf=(16, F), fw=(48, B), kp=(16, I),
    t1=(16, F), t2=(16, I), hh=(16, I), a12=(16, I), a3=(16, I), x1=(16, F), x2=(16, F), ix=(16, F), L1=(16, U), L2=(16, U), L3=(16, U),
    g2=(16, F), g3=(16, F), y2=(16, F), y3=(16, F), z2=(16, F), z3=(16, F), w2=(16, F), cum=(16, B), e1=(16, F), e3=(16, F),
    LP=(16, U), msk=(18, F), bas=(18, F), pf1=(18, F), pf2=(18, F), ONEs=(64, F),
)
HOME = {}
_W = {}
for _k, _v in _S.items():
    if _v[0] <= 18 and _k not in ("WK", "TC"):
        HOME[_k] = ("pool_" + _v[1], _W.get(_v[1], 0)); _W[_v[1]] = _W.get(_v[1], 0) + (_v[0] + 15) // 16 * 16
SCRATCH = {k: ("sbuf", [128, v[0]], v[1]) for k, v in _S.items() if k not in HOME}
for _k, _v in _W.items(): SCRATCH["pool_" + _k] = ("sbuf", [128, _v], _k)
for _i in range(8): SCRATCH["pb%d" % _i] = ("psum", [128, 512], F)
DMAS = ["d%d" % i for i in range(24)]
SEMAPHORES = ["qV", "qS", "qP", "qG", "sent"] + ["arr%d%d" % (t, c) for t in range(RO) for c in range(2)] + DMAS


ORDER = []
PACE = [dict(cy=0.83, pe=0.46, ga=1.56, sc=3.8, lat=210, wake=50, fix=0, dma=1500, bw=200.0, rem=2400),
        dict(cy=1.15, pe=0.62, ga=1.85, sc=5.0, lat=220, wake=200, fix=5, dma=2000, bw=170.0, rem=3200)]
WEIGHT = (1.0, 1.8)
SHIFTS, MOVES, MIX, HEAT, SIDE, SEED = 100, (40000, 40000, 30000, 25000), 0.0, 500.0, 1.0, 41
TT16, AND16, GCAST = True, False, True
RED32, SCAN32, SCANIN = True, True, True
ORD5 = (0, 2, 1)
MARKS = ("LY", "Hu", "SU", "YS", "QS")
TREE, HIS = True, (tuple((c, k) for c in (1, 2) for k in range(5)),) * 3
HOP, ZRA = 16, 12
XCV, EARLY = 8, 1
RV2 = (tuple((2, j) for j in range(4)),) * 3
MKS = range(4, 22)
XC = 32
CH2 = (((8, 6, 2), (8, 2, 4, 2), (8, 2, 4, 2)),) * 3
CH5 = (((4, 4, 4, 4), (8, 6, 2), (8, 8)),) * 3
GR5 = ((16,), (8, 8), (16,))
GR4 = ((0,), (1,), (2,))
SP5 = (((2, 1),), ((2, 1),), ((2, 0), (2, 1)))
REPG = 160
XV = ((256, 256), (0, 0), (0, 0))
DONE = (0, 0, 0)
RCV, WTV = 8, (1, 3)


def _times(ops, p):
    out = []
    for o in ops:
        kind, n, r = o["cost"]
        if kind == "dma": out.append((60.0, p["dma"] + n / p["bw"]))
        elif kind == "rem": out.append((300.0 + n, 300.0 + n))
        elif kind == "arr": out.append((0.0, p["rem"] - 300.0))
        else:
            d = {"e": max(64, n * r), "ga": r * 1.2 + n * p["ga"], "sc": r * 1.2 + n * p["sc"], "pe": n * p["pe"] / p["cy"], "g": r * 1.2 + 2 * n}[kind] * p["cy"]
            if kind == "e": d += p["fix"] * (1.0 if o["q"] == "V" else 0.5)
            out.append((d, d))
    return out


def _replay(G, order, p, lo, hi, old):
    qs, deps = G; d0, d1 = p["d0"], p["d1"]; wake = p["wake"]
    fin, end, by = (old[0][:], old[1][:], old[2][:]) if lo else ([0.0] * len(qs), [0.0] * len(qs), [-1] * len(qs))
    last = [-1] * 12; free = [0.0] * 12; j = lo; left = 5
    while j and left:
        j -= 1; n = order[j]; q = qs[n]
        if last[q] < 0:
            last[q] = n; free[q] = fin[n]; left -= q < 5
    for n in order[lo:hi]:
        q = qs[n]; t = free[q]; w = last[q]
        if q == 3:
            for m in deps[n]:
                if end[m] + wake > t: t = end[m] + wake; w = m
        else:
            for m in deps[n]:
                if end[m] > t: t = end[m]; w = m
        free[q] = fin[n] = t + d0[n]; end[n] = t + d1[n]; by[n] = w; last[q] = n
    return fin, end, by


def _place(ops, tm, edges, key):
    start = [0.0] * len(ops); busy = {}
    for i in sorted(range(len(ops)), key=key):
        t = 0.0
        for m, lag in edges[i]:
            if start[m] + lag > t: t = start[m] + lag
        d = max(tm[i][0], 1.0); row = busy.setdefault(ops[i]["q"], []); k = len(row)
        while k and row[k - 1][1] > t: k -= 1
        while k < len(row) and row[k][0] < t + d:
            t = max(t, row[k][1]); k += 1
        row.insert(k, (t, t + d)); start[i] = t
    return start


def _schedule(ops):
    n = len(ops); x = [SEED]; names = ["V", "S", "P", "G", "Y"]; anc = [0] * n; deps = []
    for i, o in enumerate(ops):
        if o["q"] not in names: names.append(o["q"])
        d = o["deps"] + ([i - 1] if o["kind"] == "arr" else []); up = 0
        for m in d: up |= anc[m]
        deps.append([m for m in d if not up >> m & 1])
        for m in d: up |= 1 << m
        anc[i] = up
    qs = [names.index(o["q"]) for o in ops]; G = (qs, deps)
    for q in PACE:
        tm = _times(ops, q); q["d0"] = [a for a, b in tm]; q["d1"] = [b + q["lat"] * (o["kind"] != "r") for (a, b), o in zip(tm, ops)]
    p = PACE[0]; tm = _times(ops, p); d0 = p["d0"]; fw = [[] for _ in ops]; on = [[] for _ in ops]
    for i, o in enumerate(ops):
        for m, lat in [(m, p["lat"] + p["wake"] * (qs[i] == 3)) for m in deps[i]] + [(m, tm[m][0] - tm[m][1]) for m in o["soft"]]:
            fw[i].append((m, tm[m][1] + lat)); on[m].append((i, tm[m][1] + lat))
    pre = [set(m for m, _ in fw[i]) for i in range(n)]
    wide = [i for i, o in enumerate(ops) if "wide" in o or (o["w"] and o["w"][0][0] in MARKS)]; gates = [i for i, o in enumerate(ops) if o.get("gate")]
    names = sorted(set(o["tag"] for o in ops)); tag = [names.index(o["tag"]) for o in ops]

    def draw(k):
        u = []
        for _ in range(k):
            x[0] = (x[0] * 1103515245 + 12345) % 2 ** 31; u.append(x[0] / 2 ** 31)
        return u

    def value(st, goal, marks):
        return sum(((max(s[1]) if goal < 0 else s[1][goal]) + SIDE * sum(s[1][i] for i in marks) / len(marks)) / w for s, w in zip(st, WEIGHT))

    def fill(key, up):
        if up:
            for i in range(n - 1, -1, -1):
                for m, _ in fw[i]:
                    if key[m] >= key[i]: key[m] = key[i] - 1e-3
        else:
            for i in range(n):
                for m, _ in fw[i]:
                    if key[m] >= key[i]: key[i] = key[m] + 1e-3
        s = _place(ops, tm, fw, lambda i: (key[i], i))
        order = sorted(range(n), key=lambda i: (s[i], key[i], i))
        return order, [_replay(G, order, q, 0, n, None) for q in PACE]

    late = [0.0] * n; best = cur = None
    for i in range(n - 1, -1, -1): late[i] = max([tm[i][1]] + [late[j] + lag for j, lag in on[i]]) + 1e-3
    for k in range(SHIFTS):
        u = draw(4); off = list(cur[1]) if cur else [0.0] * len(names)
        if cur: off[int(u[0] * len(names))] += (u[1] - 0.5) * 8000 * u[2] ** 2
        order, st = fill([-late[i] - off[tag[i]] for i in range(n)], True); v = value(st, -1, wide)
        if cur is None or v < cur[0] + HEAT * u[3] ** 2 * (1.0 - k / SHIFTS): cur = (v, off)
        if best is None or v < best[0]: best = (v, order, st)
    for stage, moves in enumerate(MOVES):
        goal = gates[stage] if stage < len(gates) else -1; first = gates[stage - 1] if 0 < stage <= len(gates) else 0
        marks = [i for i in wide if first <= i and (goal < 0 or i < goal)]
        st = [_replay(G, best[1], q, 0, n, None) for q in PACE]
        cur = best = (value(st, goal, marks), best[1], st); pos = None; taken = 0
        for k in range(moves):
            u = draw(6); order = cur[1]; heat = HEAT * u[3] ** 2 * (1.0 - k / moves)
            if pos is None:
                pos = {m: j for j, m in enumerate(order)}; ways = {}; cut = pos[goal] + 1 if goal >= 0 else n
            if u[3] < MIX and first == 0 and goal < 0:
                g = int(u[0] * len(names)); d = (u[1] - 0.5) * 8000 * u[2] ** 2; fin = cur[2][0][0]
                order, st = fill([fin[i] - d0[i] + d * (tag[i] == g) for i in range(n)], d < 0); v = value(st, goal, marks)
                if v < cur[0] + heat:
                    cur = (v, order, st); pos = None
                    if v < best[0]: best = cur
                continue
            w = (int(u[4] * len(PACE)), marks[int(u[5] * 2 * len(marks))] if u[5] < 0.5 else goal)
            if w not in ways:
                fin, end, by = cur[2][w[0]]; j = w[1] if w[1] >= 0 else end.index(max(end)); ways[w] = []
                while by[j] >= 0 and pos[j] > pos[first] - 40:
                    if by[j] not in pre[j]: ways[w].append((by[j], j))
                    j = by[j]
            pairs = ways[w]
            if not pairs: continue
            a, b = pairs[int(u[0] * (len(pairs) if w[1] == goal else min(len(pairs), 30)))]; lo, hi = pos[a], pos[b]; hop = int(1 + HOP * u[2] ** 4)
            if u[1] < 0.5:
                while hop > 1 and lo > 0:
                    lo -= 1; hop -= qs[order[lo]] == qs[b]
                part = order[lo:hi + 1]; move = {b}; need = set(pre[b])
                for j in reversed(part):
                    if j in need: move.add(j); need |= pre[j]
                new = [j for j in part if j in move] + [j for j in part if j not in move]
            else:
                while hop > 1 and hi < n - 1:
                    hi += 1; hop -= qs[order[hi]] == qs[a]
                part = order[lo:hi + 1]; move = {a}
                for j in part:
                    if pre[j] & move: move.add(j)
                new = [j for j in part if j not in move] + [j for j in part if j in move]
            if new == part: continue
            order = order[:lo] + new + order[hi + 1:]; stop = max(cut, hi + 1)
            st = [_replay(G, order, q, lo, stop, s) for q, s in zip(PACE, cur[2])]; v = value(st, goal, marks)
            if v < cur[0] + heat:
                for j, m in enumerate(new): pos[m] = lo + j
                ways = {}; cut = pos[goal] + 1 if goal >= 0 else n; taken += 1
                if taken % 40 == 0:
                    fin = st[0][0]; order[:stop] = sorted(order[:stop], key=lambda j: (fin[j] - d0[j], pos[j])); pos = None
                cur = (v, order, st)
                if v < best[0]: best = cur
    return best[1]


def rank_program(g, core, T, topo):
    rank = T.rank_of(core)
    if rank is None:
        return
    N = len(T.cores)
    Q = {"V": g.vector, "S": g.scalar, "P": g.tensor, "G": g, "Y": g.sync}
    ops = []; piece = ["set"]; loaded = [0]; flip = [0]

    def reg(name, lo, hi, st=1):
        return (name, (1 << hi) - (1 << lo) if st == 1 else sum(1 << c for c in range(lo, hi, st)))

    def A(name, lo=0, hi=None, st=1, p=None):
        psum = name.startswith("pb")
        if hi is None: hi = lo + 1 if (lo or psum) else _S[name][0]
        rows = slice(0, 128) if p is None else slice(p[0], p[1])
        buf, o = HOME.get(name, (name, 0))
        ap = T[buf][rows, o + lo:o + hi] if st == 1 else T[buf][rows, o + lo:o + hi:st]
        return ("AP", ap, [reg(name, lo, hi, st)])

    def C(name, c):
        return A(name, c, c + 1)

    def IN(win, off):
        return ("AP", win[1].indirect(off[1]), win[2], off[2])

    def isap(x):
        return isinstance(x, tuple) and len(x) > 2 and x[0] == "AP"

    def emit(q, fn, args, kw=None, kind="c", extra=None):
        w, r = [], []
        for n, a in enumerate(list(args) + list((kw or {}).values())):
            if isap(a):
                (w if n == 0 else r).extend(a[2])
                if len(a) > 3: r.extend(a[3])
        if extra: w, r = extra
        aps = [a for a in args if isap(a)]
        size = lambda a: bin(a[2][0][1]).count("1")
        wide = lambda a: 4 if a[2][0][0].startswith("pb") or _S[a[2][0][0]][1] in (F, I) else 2
        if kind == "r": cost = ("rem", 0, 0)
        elif kind == "d": cost = ("dma", 128 * size(aps[0]) * wide(aps[0]) if aps else 60000, 0)
        elif q == "P": cost = ("pe", max(64, size(aps[0])) * (4 if wide(aps[1]) == 4 else 1), 0)
        elif q == "G": cost = ("g", size(aps[0]), 130 if fn == "iota" else 170)
        elif len(aps[0]) > 3: cost = ("sc", size(aps[1]), 50)
        elif len(aps) > 1 and len(aps[1]) > 3: cost = ("ga", size(aps[0]), 50 if q == "V" else 65)
        elif fn == "tensor_tensor": cost = ("e", size(aps[0]), 1 if any(a[2][0][0].startswith("pb") for a in aps[1:]) else 2)
        else: cost = ("e", size(aps[min(1, len(aps) - 1)]), 0.5 if q == "V" and all(wide(a) == 2 for a in aps[:2]) else 1)
        ops.append(dict(tag=piece[0] + (fn[:3] + q + str(len(ops) * (q == "G"))) * (piece[0] == "set"), cost=cost, q=q, fn=fn, a=[x[1] if isap(x) else x for x in args],
                        k={n: (x[1] if isap(x) else x) for n, x in (kw or {}).items()}, w=w, r=r, kind=kind))

    def part(name, *k):
        piece[0] = name + repr(k)

    cp = lambda o, i: emit("V", "tensor_copy", [o, i])
    tt = lambda o, a, b, op: emit("V", "tensor_tensor", [o, a, b, op])
    ms = lambda o, c: emit("V", "memset", [o, c])

    def tu(o, mid, a, b, op):
        if TT16: tt(o, a, b, op)
        else: tt(mid, a, b, op); cp(o, mid)

    def au(o, mid, a, *k):
        if AND16: ts(o, a, *k)
        else: ts(mid, a, *k); cp(o, mid)

    def ts(o, a, s1, op0, s2=None, op1=None):
        emit("V", "tensor_scalar", [o, a, s1, s2, op0] + ([] if s2 is None else [op1]))

    def act(o, i, f, **k):
        emit("S", "activation", [o, i, f], k)

    def mm(o, l, r, s, e, join=False):
        emit("P", "matmul", [o, l, r, s, e])
        if join:
            b = ops.pop(); a = ops[-1]
            a["more"] = a.get("more", []) + [b["a"]]; a["w"] = a["w"] + b["w"]; a["r"] = a["r"] + b["r"]; a["cost"] = ("pe", a["cost"][1] + b["cost"][1], 0)

    scan = lambda o, d0, d1, o0, o1, first=0.0: emit("V", "tensor_tensor_scan", [o, d0, d1, first, o0, o1])

    def iota(o, pat, base=0, cm=0):
        emit("G", "iota", [o, pat, base, cm], None if _S[o[2][0][0]][1] == I else {"allow_small_or_imprecise_dtypes": True})

    sel = lambda o, i, pat, op, base, cm, fill=0.0: emit("G", "affine_select", [o, i, pat, op, fill, base, cm])
    gcp = lambda o, i, n: sel(o, i, [[0, n]], OP.is_ge, 0, 0)

    def load(q, o, src):
        emit(q, "dma_start", [o, src], kind="d")
        loaded[0] += ops[-1]["cost"][1] + 48000; ops[-1]["cost"] = ("dma", loaded[0], 0)

    def store(q, dst, i, size):
        emit(q, "dma_start", [dst, i[1]], kind="d", extra=([], i[2]))
        ops[-1]["cost"] = ("dma", size, 0)

    Kp, P5, R0c, P3, P15, PKc = [C("Kp", j) for j in range(6)]
    EQ, GEQ, GT, NE = OP.is_equal, OP.is_ge, OP.is_gt, OP.not_equal
    ADD, SUB, MUL, MIN, AND, SHR = OP.add, OP.subtract, OP.mult, OP.min, OP.bitwise_and, OP.arith_shift_right
    YB = lambda t: "YB%d" % t
    XH = lambda t: "XHb" if t % 2 else "XHa"
    BH = lambda t: "BHb" if t % 2 else "BHa"
    S15 = lambda n: A(n, 0, 15)

    for x in range(2):
        for b in range(2):
            load("Y" if b else "S", A("Lt", 32 * b + 16 * x, 32 * b + 16 * x + 16), T.live[x::2, 512 * b:512 * b + 512])
    load("S", A("Z"), T.z[:])
    for b in range(2): load("Y", A("Ri", 512 * b, 512 * b + 512), T.rings[:, 512 * b:512 * b + 512])
    load("Y", A("X", 0, NB), T.x0[:])
    load("Y", C("WK", 0), T.w[:]); load("Y", C("WK", 1), T.kap[:])
    load("Y", A("TC", 0, 1, p=(0, 8)), T.th[:]); load("Y", A("TC", 1, 2, p=(0, 8)), T.cap[:])

    ms(A("ONE"), 1.0); ms(A("TWO"), 2.0); ms(A("ONEf"), 1.0); ms(A("Lz", 0, 8), 0.0); ms(A("EW"), 0.0); ms(A("ONEs"), 1.0)
    iota(C("Ki0", 0), [[0, 1]], 0, 1)
    iota(A("T17"), [[1, 20]])
    iota(A("BLKt"), [[1, 128]])
    iota(A("M16"), [[1, 8], [0, 16]])
    iota(A("A1"), [[16, 64]])
    cp(C("Kp", 13), C("Ki0", 0)); ts(C("Ki0", 2), C("Ki0", 0), 4, SHR); cp(C("Kp", 14), C("Ki0", 2))
    ts(A("ID"), A("BLKt"), C("Kp", 13), EQ); ts(A("BLK"), A("M16"), C("Kp", 14), EQ)
    sel(A("S7"), A("ONEf"), [[-16, 8], [0, 16]], EQ, -7, 1)
    sel(A("TRI"), A("BLK"), [[1, 128]], GEQ, 0, -1)
    sel(A("UP"), A("BLK"), [[-1, 128]], GT, 0, 1)
    sel(A("S15"), A("ONEf"), [[-16, 8], [0, 16]], EQ, -15, 1)
    iota(A("LAN"), [[1, 3], [48, 6]])
    for o in ops: o["head"] = o["q"] == "G"
    ts(C("Ki0", 1), C("Ki0", 0), 15, AND)
    cp(Kp, C("Ki0", 1))
    ts(A("SL"), A("A1", 0, 16), Kp, ADD); ts(A("IDu"), A("A1", 0, 32), Kp, ADD)
    ts(A("A2"), A("A1"), Kp, ADD, -1.0, MUL)
    ts(A("A1"), A("A1"), Kp, ADD, -1024.0, ADD)
    ts(A("A2"), A("A2"), 1023.0, ADD)
    ts(P5, Kp, 5.0, MUL); ts(R0c, Kp, 0.0, EQ); ts(P3, Kp, 3.0, MUL); ts(P15, Kp, 15.0, MUL)
    ts(PKc, Kp, -80.0, MUL, TOP - 15, ADD)
    for t in range(RO): ts(C("Kp", 8 + t), R0c, float(NB + P * t - 1024), MUL, 1024.0, ADD)
    ts(A("EW", 15, 143, 16), A("BLK", 0, 128, 16), 32768.0, MUL)
    ts(A("LAN"), A("LAN"), P3, ADD)
    ms(A("RST"), 0.0); ms(A("RST", 15, 160, 16), 1024.0); ms(A("RSU"), 0.0); ms(A("RSU", 15, 160, 16), 1023.5)
    ms(A("PK2"), -1.0); ms(A("PK2", 15, 80, 16), TOP)
    ms(A("PK1"), 0.0); ts(A("PK1", 15, 80, 16), A("T17", 0, 5), -16.0, MUL, PKc, ADD)
    ms(A("QD0"), 1.0); ms(A("QD0", 0, 60, 4), 0.0); ms(A("QD0", 2, 60, 4), 2.0 ** 19)
    ms(A("QD1", 1, 60, 4), -12.0 / 2 ** 24); ms(A("QD1", 2, 60, 4), RND); ms(A("QD1", 3, 60, 4), -RND)

    def mask(j):
        lo, hi = SPANS[j]; part("mask", j < 4, j in MKS)
        if j in MKS: act(A("MK", 128 * j, 128 * j + 128), A("ID"), AF.Copy, scale=C("SPN", 16 * (hi - lo - 1) + lo))
        else: ts(A("MK", 128 * j, 128 * j + 128), A("ID"), C("SPN", 16 * (hi - lo - 1) + lo), MUL)
        ops[-1]["idle"] = True

    def bh(t, n0, n1):
        per, stp, plan = PLANS[t]; part("bh", t, n0)
        for j, (rho, v, lo, hi) in enumerate(plan):
            k = SPANS.index((lo, hi))
            mm(A("pb6", rho + per * n0, rho + per * (n1 - 1) + 1, per), A("MK", 128 * k, 128 * k + 128),
               A("Rh", v + stp * n0, v + stp * (n1 - 1) + 1, stp), lo == 0, hi == 16, lo > 0)
        ts(A(BH(t), n0 * per, n1 * per), A("pb6", n0 * per, n1 * per), 1024.0, ADD)
        if n0 == 0: ops[-1]["early"] = t - 1

    def xh(t, c0, c1, nb):
        cuts = [c for c in range(c0, c1) if (c % XCV == 0 if XV[t][0] <= c <= XV[t][1] else (c - c0) % XC == 0) or c == c0] + [c1]
        for c, d in zip(cuts, cuts[1:]):
            part("xh", t, c0, c // 64)
            o, i = A(XH(t), 16 * c, 16 * d), IN(A("X", 0, nb), A(BH(t), c, d))
            if XV[t][0] <= c < XV[t][1]: cp(o, i)
            else:
                act(o, i, AF.Copy)
                if t and c0 == 0 and d <= DONE[t]: ops[-1]["ahead"] = t

    def r4(j, out, v0, v1, st):
        n = len(range(v0, v1, st)); part("r4", v0 // 512, st, j // 2)
        if GCAST and j == 0: return gcp(out, A("Rh", v0, v1, st), n)
        mm(A("pb7", 0, n), A("RT", 128 * j - 128, 128 * j) if j else A("ID"), A("Rh", v0, v1, st), True, True)
        act(out, A("pb7", 0, n), AF.Copy)

    part("live")
    cp(A("Lb"), A("Lt"))
    emit("V", "transpose", [A("Lz", 8, 72), A("Lb")])
    mm(A("pb4", 0, 64), A("TRI"), A("Lz", 8, 72), True, False)
    mm(A("pb4", 0, 64), A("UP"), A("Lz", 7, 71), False, True)
    tt(A("e0"), A("A1"), A("Lz", 8, 72), MUL)
    tt(A("e0"), A("e0"), A("A2"), ADD)
    scan(A("rho"), A("ONEs"), A("pb4", 0, 64), MUL, ADD)
    tu(A("p0u"), A("A2"), A("e0"), A("rho"), ADD)
    mm(A("pb4", 0, 2), A("S7"), A("rho", 41, 57, 15), True, True)
    mm(A("pb4", 2, 3), A("S15"), C("rho", 63), True, True)
    part("spans")
    ts(A("GE"), A("T17", 0, 16), Kp, OP.is_le); ts(A("LTt"), A("T17"), Kp, GT)
    for w in range(4): tt(A("SPN", 16 * w, 16 * w + 16), A("GE"), A("LTt", w + 1, w + 17), MUL)
    for j in range(len(SPANS)): mask(j)
    part("zr")
    for c in range(3): act(A("Zp", 80 * c, 80 * c + 80), A("Z", c, P, 3), AF.Copy); ops[-1]["busy"] = True
    for k in range(ZRA): act(A("ZR", k, 3840, 16), A("Zp"), AF.Copy)
    part("lr")
    cp(A("CN", 0, 3), A("pb4", 0, 3))
    ts(A("s0"), A("LAN"), C("CN", 0), ADD)
    ts(A("s1"), A("s0"), C("CN", 2), GEQ, C("CN", 2), MUL)
    tu(A("LR"), A("s2"), A("s0"), A("s1"), SUB)
    for b in range(2):
        part("rh", b)
        act(A("Rh", 512 * b, 512 * b + 512), IN(A("Ri", 512 * b, 512 * b + 512), A("IDu")), AF.Identity, bias=-1024.0); ops[-1]["early"] = -2
        part("sc", b)
        cp(IN(A("BIG", CI, R1), A("p0u", 32 * b, 32 * b + 32)), A("Ri", 512 * b, 512 * b + 512)); ops[-1]["busy"] = True
    part("zr", 1)
    for k in range(ZRA, 16): act(A("ZR", k, 3840, 16), A("Zp"), AF.Copy); ops[-1]["after"] = -2
    bh(0, 0, 256)
    xh(0, 0, 256, NB)
    piece[0] = "set"
    iota(A("C16"), [[0, 5], [1, 16]])
    sel(A("S15b"), A("ONE"), [[-16, 8], [0, 16]], EQ, -15, 1)
    for j in (1, 2, 3):
        sel(A("RS", 128 * j - 128, 128 * j), A("BLK"), [[-1, 128]], EQ, -4 * j, 1)
        sel(A("RK", 128 * j - 128, 128 * j), A("S15b"), [[0, 8], [1, 16]], GEQ, 4 * j - 16, 0)
        mm(A("pb7", 0, 128), A("ID"), A("RS", 128 * j - 128, 128 * j), True, False)
        mm(A("pb7", 0, 128), A("ID"), A("RK", 128 * j - 128, 128 * j), False, True)
        act(A("RT", 128 * j - 128, 128 * j), A("pb7", 0, 128), AF.Copy)
    iota(A("MT"), [[1, 16], [0, 5]])
    sel(A("G8t", p=(0, 8)), A("ONEf", p=(0, 8)), [[1, 128]], GEQ, 0, -16)
    sel(A("G8", p=(0, 8)), A("G8t", p=(0, 8)), [[-1, 128]], GEQ, 15, 16)
    iota(S15("NFL"), [[80, 3], [1, 5]], 960)
    act(A("BLKf"), A("BLK"), AF.Copy)
    sel(A("BK1"), A("BLK"), [[0, 8], [1, 16]], GT, 0, 0)
    iota(A("LN", P, 2 * P), [[1, 3], [3, 80]])
    for j in range(4): sel(A("SH", 128 * j, 128 * j + 128), A("BK1"), [[-1, 128]], EQ, 1 - j, 1)
    part("late")
    for j in range(4):
        for k in range(17 - j, 16):
            col = A("SH", 128 * j + k, 128 * j + 128, 16)
            sel(col, col, [[-16, 8]], NE, -15, 1, 1.0)
    iota(A("LN", 0, P), [[1, 3], [3, 5], [15, 16]])
    sel(A("UPI"), A("BLK"), [[-1, 128]], GEQ, 0, 1)
    sel(A("GE8"), A("BLK"), [[-16, 8], [0, 16]], GEQ, -8, 1)
    part("later")
    for j in range(3): iota(A("R4", TM * j + T0 + P, TM * j + TM), [[0, P]])
    gcp(A("BIG", CJ, CJ + P), A("BIG", CI, CI + P), P)
    part("tables")
    ts(A("E0"), A("ID"), R0c, MUL)
    ts(A("BGM"), A("C16"), Kp, NE, 1024.0, MUL)
    ts(C("WKf", 0), C("WK", 0), 2048.0, GEQ); ts(C("WKf", 1), C("WK", 0), 2.0 ** -12, MUL)
    cp(C("WKf", 2), C("WK", 1))
    ts(C("WKf", 3), C("WKf", 1), C("WKf", 0), SUB)
    ts(A("W16"), A("BLK"), C("WKf", 3), MUL)
    ts(A("RK2"), A("MT"), Kp, EQ, C("WKf", 2), MUL)
    cp(A("TCf", 0, 2, p=(0, 8)), A("TC", 0, 2, p=(0, 8)))
    mm(A("pb5", 0, 80), A("BLKf"), A("RK2"), True, True)
    mm(A("pb5", 80, 82), A("G8", p=(0, 8)), A("TCf", 0, 2, p=(0, 8)), True, True)
    ts(A("KT"), A("pb5", 0, 80, 5), 4096.0, MUL)
    ts(C("Kp", 6), Kp, 1.0, EQ, 2048.0, MUL); ts(C("Kp", 7), Kp, 2.0, EQ, -63.0, MUL)
    ts(A("PBS"), A("MT"), C("Kp", 6), MUL, C("Kp", 7), ADD)
    ts(A("RK2"), A("pb5", 0, 80), R0c, MUL)
    tt(A("PAY"), A("RK2"), A("PBS"), ADD)
    ts(C("Kp", 11), Kp, 2.0, EQ, 2.0 ** 18, MUL); ts(C("Kp", 12), Kp, 2.0, OP.is_lt, C("Kp", 11), ADD)
    ts(A("PL"), A("BLK"), C("Kp", 12), MUL)
    ts(C("TH", 0), A("pb5", 80, 81), 32768.0, MUL, float(KOFF), ADD)
    cp(C("TH", 1), A("pb5", 81, 82))
    ms(A("FM0", 0, 30, 2), 0.0); ms(A("NEG"), -1.0)
    act(S15("NFL"), S15("NFL"), AF.Identity, bias=P5)
    act(S15("LOC"), S15("SL"), AF.Identity, bias=4096.0)
    act(A("NID"), A("ID"), AF.Copy, scale=-1.0)
    act(S15("IDX"), S15("T17"), AF.Identity, bias=P15)
    part("nbu")
    ts(S15("i0"), S15("SL"), 1.0 / 15, MUL, -0.47, ADD)
    ts(S15("y2"), S15("i0"), -15.0, MUL); cp(S15("s4"), S15("i0"))
    tt(S15("y2"), S15("y2"), S15("SL"), ADD)
    ts(S15("i0"), S15("y2"), 1.0 / 3, MUL, -0.34, ADD)
    ts(S15("y2"), S15("y2"), 80.0, MUL)
    ts(S15("y3"), S15("i0"), -224.0, MUL)
    tt(S15("y2"), S15("y2"), S15("s4"), ADD)
    tt(S15("y2"), S15("y2"), S15("y3"), ADD)
    cp(S15("NBu"), S15("y2"))
    for j in range(4): r4(j, A("R0", j, T0, 4), j, T0, 4)

    def prep(t):
        part("prep", t)
        if t == 0:
            tt(C("CN", 3), C("CN", 2), C("CN", 1), SUB)
            ts(A("msk"), A("LAN"), C("CN", 3), GEQ)
            ts(C("CN", 4), C("CN", 2), float(P), ADD)
            ts(A("s3"), A("LAN"), C("CN", 3), GEQ, C("CN", 4), MUL)
            ts(A("s0"), A("LAN"), C("CN", 1), ADD, float(CI), ADD)
            tt(A("bas"), A("s0"), A("s3"), SUB)
        else:
            ts(A("msk"), A("LAN"), C("CN", 10), GEQ)
            ts(A("s3"), A("LAN"), C("CN", 10), GEQ, float(CJ - CI - P), MUL)
            ts(A("s0"), A("LAN"), C("CN", 10), SUB, float(CI), ADD)
            tt(A("bas"), A("s0"), A("s3"), ADD)

    def keep(t):
        part("keep", t)
        ts(A("RESh"), A("RES"), -1024.0, ADD)
        mm(A("pb3", 0, P), A("E0"), A("LN", P, 2 * P), True, False)
        mm(A("pb3", 0, P), A("SH", 0, 128), A("RESh"), False, True)
        act(A("WT", 960, 1200), A("pb3", 0, P), AF.Copy)

    def step2(t, c):
        bank = "pb%d" % c; o = 1280 * c; p = 0; n0 = 80 * c; part("s2", t, c)
        cp(A("RES", n0, n0 + 80), IN(A("BIG", CI if t == 0 else 0, (R1, R1, CJ + P)[t]), A("LR", 6 * c, 6 * c + 5)))
        if t + c == 0: ops[-1]["after"] = -1
        for j, n in enumerate(CH2[t][c]):
            a, b = o + 80 * p, o + 80 * (p + n)
            tt(A("D2", a, b), IN(A("X", 0, NB + P * t), A("RES", a // 16, b // 16)), A("ZR", a, b), SUB)
            ops[-1]["wide"] = "V"; ops[-1]["gate"] = t and a == 0
            if (c, j) in RV2[t]: ts(A("A2w", a, b), A("D2", a, b), -1.0 / 1024, MUL, 0.0, OP.max)
            else: act(A("A2w", a, b), A("D2", a, b), AF.Relu, scale=-1.0 / 1024)
            if a == 0: ops[-1]["opens"] = t
            for r in range(p, p + n):
                mm(A(bank, 0, 80), A("EW", 15 - r, 143 - r), A("A2w", o + 80 * r, o + 80 * r + 80), r == 0, r == 15, r > p)
            p += n
        part("pick", t, c)
        scan(A("SC1", n0, n0 + 80), A(bank, 0, 80), A("PK1"), MIN, ADD, TOP)
        scan(A("SC2", n0, n0 + 80), A(bank, 0, 80), A("PK2"), MIN, ADD, TOP)
        tu(A("LY", 6 * c, 6 * c + 5), A("kf", 5 * c, 5 * c + 5), A("SC2", n0 + 15, n0 + 80, 16), A("SC1", n0 + 15, n0 + 80, 16), SUB)
        y = A(YB(t), 1280, 1360) if c == 2 else A("YS", 160 * t + n0, 160 * t + n0 + 80)
        act(y, IN(A("D2", o, o + 1280), A("LY", 6 * c, 6 * c + 5)), AF.Abs)
        if c < 2: send(t, c)

    def send(t, c):
        dst = T.cores[(rank + 1 + (t + c) % (N - 1)) % N]
        far = [e for e in topo.engines(core, dst) if all(e in topo.engines(core, d) for d in T.cores if d != core)]
        rid, pid = topo.addr(dst, core); y = 160 * t + 80 * c
        tr = RemoteDMATransfer(dst_ids=[DstId(rid=rid, pnc=pid)], dma_engine_mask=sum(1 << e for e in far), remote_sem=T.sem["arr%d%d" % (t, c)],
                               src=T["YS"][:, y:y + 80], dst=T[YB(t)][:, 640 * c:640 * c + 80])
        emit("G", "remote_dma_fused", [[tr]], {"local_sem": T.sem.sent}, kind="r", extra=([], [reg("YS", y, y + 80)]))
        if t + c == 0: ops[-1]["cost"] = ("rem", 1800.0, 0)
        ops.append(dict(tag=piece[0], cost=("arr", 0, 0), kind="arr", q="R%d%d" % (t, c), w=[reg(YB(t), 640 * c, 640 * c + 80)], r=[], n=len(far)))

    def spread(t, c):
        o = 640 * c; n = 80; part("spread", t, c)
        while n < 80 * max([4] + [w for j, w in enumerate(CH5[t][c]) if (c, j) not in SP5[t]]):
            a, b = A(YB(t), o + n, o + 2 * n), A(YB(t), o, o + n)
            if n >= REPG: gcp(a, b, n)
            else: act(a, b, AF.Copy)
            n *= 2
        part("beside", t)
        gcp(A(XH(t), 4096 + 80 * c, 4176 + 80 * c), A(YB(t), o, o + 80), 80)

    def step4(t, cs):
        c = cs[0]; w = len(cs); bank = "pb%d" % c; n0, n1 = 80 * c, 80 * (c + w); s0, s1 = 20 * c, 20 * (c + w); part("s4", t, c)
        for j in range(w):
            mm(A(bank, 80 * j, 80 * j + 80), A("ID"), A("BGM"), True, False)
            mm(A(bank, 80 * j, 80 * j + 80), A("W16"), A(YB(t), 640 * (c + j), 640 * (c + j) + 80), False, True)
        raw = A("SU", n0 + 15, n1, 16); ri = A("SV", n0 + 15, n1, 16)
        scan(A("SU", n0, n1), A(bank, 0, 80 * w), A("RST", 0, 80 * w), MIN, ADD, 4096.0)
        if SCAN32: scan(A("SV", n0, n1), A(bank, 0, 80 * w), A("RSU", 0, 80 * w), MIN, ADD, 4096.0)
        else: ts(ri, raw, -0.5, ADD)
        tt(A("QD1", s0, s1, 4), raw, ri, SUB); tt(A("QD0", s0 + 1, s1, 4), raw, ri, SUB)
        scan(A("QS", s0, s1), A("QD0", s0, s1), A("QD1", s0, s1), MUL, ADD)
        for c in cs:
            for k in range(5):
                o, u, q = A("Hi", 80 * c + k, 80 * c + 80, 5), C("QD1", 20 * c + 4 * k), C("QS", 20 * c + 4 * k + 3)
                if (c, k) in HIS[t]: act(o, A("KT"), AF.Identity, scale=u, bias=q)
                else: ts(o, A("KT"), u, MUL, q, ADD)
        au(A("Hu", n0, n1), A("Hj", n0, n1), A("Hi", n0, n1), 4095, AND)

    def step5(t, c):
        bank = "pb%d" % c; o = 1280 * c; m = 0; part("s5", t, c)
        for j, n in enumerate(CH5[t][c]):
            a, b = o + 80 * m, o + 80 * (m + n); x = IN(A(XH(t), 0, 4096), A("Hu", a // 16, b // 16))
            if (c, j) in SP5[t]:
                act(A("D5", a, b), x, AF.Copy)
                ops[-1]["wide"] = "S"
                for e in range(a, b, 320):
                    f = min(e + 320, b); flip[0] ^= 1; out = A("pb5" if flip[0] else "pb3", 0, f - e)
                    mm(out, A("NID"), A(YB(t), 640 * c, 640 * c + f - e), True, False)
                    mm(out, A("ID"), A("D5", e, f), False, True)
                    act(A("A5", e, f), out, AF.Abs)
            else:
                tt(A("D5", a, b), x, A(YB(t), 640 * c, 640 * c + 80 * n), SUB)
                ops[-1]["wide"] = "V"
                if j == 0 and EARLY < 3 and c == ORD5[EARLY]: ops[-1]["after"] = t
                act(A("A5", a, b), A("D5", a, b), AF.Abs)
            m += n
        m = 0
        for n in GR5[c]:
            out = A(bank, 5 * m, 5 * (m + n)) if c == ORD5[2] or not TREE else A("pb%d" % ORD5[0], ORD5.index(c), 160, 2)
            mm(out, A("PL"), A("PAY", 5 * m, 5 * (m + n)), True, False)
            for r in range(16): mm(out, A("EW", 15 - r, 143 - r), A("A5", o + 80 * m + r, o + 80 * (m + n), 16), False, r == 15, r > 0)
            m += n
        part("least", t, c)
        if TREE and c == ORD5[0]: return
        if TREE and c == ORD5[1]:
            bank = "pb%d" % ORD5[0]
            act(A("AC", 0, 80), A(bank, 80, 160), AF.Copy)
            tt(A("AC", 80, 160), A(bank, 0, 80), A("AC", 0, 80), MIN)
            tt(A("AC", 0, 40), A("AC", 80, 120), A("AC", 120, 160), MIN)
            tt(A("AC", 40, 60), A("AC", 0, 20), A("AC", 20, 40), MIN)
            for i in range(2):
                tt(A("Ki", 5 * ORD5[i], 5 * ORD5[i] + 5), A("AC", 40 + i, 50, 2), A("AC", 50 + i, 60, 2), MIN)
                forks(t, ORD5[i])
            return
        for k in range(5): emit("V", "tensor_reduce", [C("Ki" if RED32 else "K", 5 * c + k), A(bank, k, 80, 5), AxisListType.X, MIN])
        forks(t, c)

    def forks(t, c):
        ts(A("fw", 16 * t + c, 16 * t + 15, 3), A("Ki" if RED32 else "K", 5 * c, 5 * c + 5), C("TH", 0), OP.is_lt, -1.0 if c == 2 else 1.0, MUL)
        for u in range(t + 1) if c == ORD5[0] else (t,):
            for e in (range(3) if u < t else (c,)):
                mm(A("pb4", 0, 5), A("TWO" if e == 2 else "ONE"), A("fw", 16 * u + e, 16 * u + 15, 3), c == ORD5[0] and u == 0 and (e == 0 or t == 0), c == ORD5[2], 0 < u + e and u < t)

    def close(t):
        last = t == RO - 1; TT = T0 + P * t; lv = A("LV", 16 * t, 16 * t + 15); part("ring", t)
        if not RED32: cp(S15("Ki"), S15("K"))
        ts(S15("nf"), S15("Ki"), C("TH", 0), GEQ, 8192.0, MUL)
        if SCANIN:
            act(A("FM0", 1, 30, 2), A("QD1", 0, 60, 4), AF.Copy, scale=4096.0)
            cp(A("FM1", 1, 30, 2), A("QS", 3, 60, 4))
            ts(A("FM1", 0, 30, 2), S15("Ki"), 2047, AND)
            scan(A("FM2"), A("FM0"), A("FM1"), MUL, ADD)
            t2 = A("FM2", 1, 30, 2)
        else:
            act(S15("uf"), A("QD1", 0, 60, 4), AF.Copy, scale=4096.0)
            ts(S15("kp"), S15("Ki"), 2047, AND)
            tt(S15("t1"), S15("kp"), S15("uf"), MUL)
            tt(S15("t2"), S15("t1"), A("QS", 3, 60, 4), ADD)
            t2 = S15("t2")
        if t == 0:
            au(S15("L1"), S15("a12"), t2, 2, SHR, 1023, AND)
        ts(S15("hh"), t2, 4095, AND)
        if t:
            ts(S15("a12"), t2, 12, AND)
            ts(S15("x1"), S15("hh"), TT / 4096.0, MUL, -255.0 / 512, ADD)
            ts(S15("x2"), S15("a12"), TM / 4.0, MUL)
            tu(S15("L1"), S15("ix"), S15("x1"), S15("x2"), ADD)
        ts(S15("a3"), t2, 3, AND)
        win = A("R4", 0, 3 * TM + TT) if t else A("R0")
        cp(A("RC", 0, min(P, 16 * RCV)), IN(win, A("L1", 0, min(15, RCV))))
        if RCV < 15: act(A("RC", 16 * RCV, P), IN(win, A("L1", RCV, 15)), AF.Copy)
        for j in range(4):
            out = A("pb%d" % j, 0, P)
            mm(out, A("E0"), A("LN", 0, P), True, False)
            mm(out, A("SH", 128 * j, 128 * j + 128), A("RC"), False, True)
            if j in WTV: cp(A("WT", P * j, P * j + P), out)
            else: act(A("WT", P * j, P * j + P), out, AF.Copy)
        ts(S15("y2"), S15("a3"), 240.0, MUL)
        tt(S15("g2"), S15("nf"), S15("SL"), ADD)
        tt(S15("z2"), S15("y2"), S15("g2"), ADD)
        tu(S15("L2"), S15("w2"), S15("z2"), S15("NFL"), MIN)
        ts(A("NEW", 0, 128), IN(A("WT"), A("L2", 0, 8)), C("Kp", 8 + t), ADD)
        act(A("NEW", 128, P), IN(A("WT"), A("L2", 8, 15)), AF.Identity, bias=C("Kp", 8 + t))
        part("marks", t)
        fw = A("fw", 16 * t, 16 * t + 15)
        emit("V", "tensor_reduce", [C("dB", 0), A("pb4", 0, 5), AxisListType.X, ADD])
        ts(lv, fw, C("dB", 0), MUL, C("TH", 1), OP.is_le)
        if not last:
            scan(S15("cum"), S15("NEG"), lv, ADD, ADD)
            tt(S15("e1"), lv, S15("IDX"), MUL)
            mm(A("pb4", 0, 1), A("UPI"), C("cum", 14), True, True)
            mm(A("pb4", 1, 2), A("BLK"), C("cum", 14), True, True, True)
            if t == 0: mm(A("pb4", 2, 3), A("GE8"), C("cum", 14), True, True, True)
            tt(S15("e3"), S15("cum"), S15("e1"), ADD)
            for c in range(3): ts(A("LP", 5 * c, 5 * c + 5), A("e3", c, 15, 3), A("pb4", 0, 1), SUB)
            ts(A("pf1"), A("msk"), A("pb4", 1, 2), MUL)
            if t == 0: ts(C("CN", 10), A("pb4", 2, 3), P / 2.0, ADD)
            tu(A("LR"), A("pf2"), A("bas"), A("pf1"), SUB)
            cp(IN(A("BIG", R1 * t, R1 * t + P), S15("LP")), A("NEW"))
            part("yt", t)
            act(A("YT", P * t, P * t + P), IN(A("NEW"), S15("NBu")), AF.Copy)
        else:
            cp(A("YT", P * t, P * t + 128), IN(A("NEW"), A("NBu", 0, 8)))
            act(A("YT", P * t + 128, P * t + P), IN(A("NEW"), A("NBu", 8, 15)), AF.Copy)
        part("board", t)
        tt(S15("z3"), S15("hh"), S15("nf"), ADD)
        tu(S15("L3"), S15("g3"), S15("z3"), S15("LOC"), MIN)
        act(A("EE"), IN(A(XH(t)), S15("L3")), AF.Copy)
        mm(A("pb5", 0, P), A("ID"), A(XH(t), 4096, 4096 + P), True, False)
        mm(A("pb5", 0, P), A("ID"), A("EE"), False, True)
        act(A("EF"), A("pb5", 0, P), AF.Identity, bias=191.75, scale=0.5)
        act(A("X", NB + P * t, NB + P * t + P), IN(A("EF"), S15("NBu")), AF.Identity, bias=-192.0)
        part("store", t)
        store("Y", T.ya[:, P * t:P * t + P], lv, 500000)
        store("Y", T.yx[:, P * t:P * t + P], A("X", NB + P * t, NB + P * t + P), 200000)
        store("Y", T.yt[:, P * t:P * t + P], A("YT", P * t, P * t + P), 170000)

    OLD = (None, 12, 26)
    for t in range(RO):
        TT = T0 + P * t; nx = t + 1 < RO
        if t:
            part("rh", TT)
            act(A("Rh", TT - P, TT), A("YT", P * t - P, P * t), AF.Identity, bias=-1024.0)
            bh(t, OLD[t], 256 // PLANS[t][0])
            xh(t, OLD[t] * PLANS[t][0], 256, NB + P * t)
        for c in range(3): step2(t, c)
        if nx:
            prep(t)
            bh(t + 1, 0, OLD[t + 1])
            xh(t + 1, 0, OLD[t + 1] * PLANS[t + 1][0], NB + P * t)
        if t == 1:
            for j in range(4):
                for v in (0, 512): r4(j, A("R4", TM * j + v, TM * j + v + 512), v, v + 512, 1)
        if t:
            for j in range(4): r4(j, A("R4", TM * j + TT - P, TM * j + TT), TT - P, TT, 1)
        keep(t)
        for c in range(3): spread(t, c)
        for cs in GR4: step4(t, cs)
        for c in ORD5: step5(t, c)
        close(t)

    seen = {}; bank = {}
    for n, o in enumerate(ops):
        deps = set(); soft = set()
        for regs, wr in ((o["r"], False), (o["w"], True)):
            for (name, cols) in regs:
                if name.startswith("pb"):
                    e, before, now = bank.get(name, (None, [], []))
                    if e != o["q"]: e, before, now = o["q"], (now[-1:] if e == "P" else now), []
                    deps.update(before)
                    if e == "P": soft.update(now[-1:])
                    if n not in now: now = now + [n]
                    bank[name] = (e, before, now)
                    continue
                deps.update(m for (c2, w2, m) in seen.get(name, []) if m != n and (wr or w2) and cols & c2)
        for regs, wr in ((o["r"], False), (o["w"], True)):
            for (name, cols) in regs:
                old = seen.get(name, [])
                if wr: old = [x for x in old if x[0] & ~cols]
                seen[name] = old + [(cols, wr, n)]
        if o["kind"] == "arr": deps = set(); soft = {n - 1}
        if o["kind"] == "d" and o["w"]:
            soft.update(m for m in range(n) if ops[m]["kind"] == "d" and ops[m]["q"] == o["q"])
        if o.get("head"): soft.update([m for m in range(n) if ops[m]["q"] == "G"][-1:])
        if "busy" in o: soft.update(m for m in range(n) if "idle" in ops[m] and ops[m]["q"] == o["q"])
        if "wide" in o: soft.update([m for m in range(n) if ops[m].get("wide") == o["wide"]][-1:])
        if "opens" in o: soft.update(m for m in range(n) if ops[m].get("ahead") == o["opens"])
        if "after" in o: soft.update(m for m in range(n) if ops[m].get("early") == o["after"])
        soft.discard(n)
        o["deps"] = sorted(deps); o["soft"] = sorted(soft)
    if not ORDER: ORDER.extend(_schedule(ops))
    pos = {m: n for n, m in enumerate(ORDER)}
    got = {q: {} for q in Q}
    for n in ORDER:
        o = ops[n]
        if o["kind"] == "arr": continue
        best = {}
        for m in o["deps"]:
            key = ops[m]["q"] if ops[m]["kind"] == "c" else m
            if key not in best or pos[best[key]] < pos[m]: best[key] = m
        need = []; know = got[o["q"]]
        for key, m in sorted(best.items(), key=lambda x: -pos[x[1]]):
            if know.get(key, -1) < pos[m]:
                know[key] = pos[m]; need.append(m); ops[m]["sig"] = True
                for k2, at in ops[m].get("know", {}).items():
                    if know.get(k2, -1) < at: know[k2] = at
        o["need"] = need; o["know"] = dict(know)
    cnt = {q: 0 for q in Q}; nd = 0; sent = 0; tail = []
    for n in ORDER:
        o = ops[n]
        if o["kind"] == "arr":
            o["at"] = (T.sem["arr" + o["q"][1:]], o["n"]); sent += o["n"]; continue
        q = Q[o["q"]]
        for m in o["need"]: q.wait_ge(*ops[m]["at"])
        call = {"tensor_copy": lambda: q.tensor_copy, "tensor_tensor": lambda: q.tensor_tensor, "tensor_scalar": lambda: q.tensor_scalar,
                "memset": lambda: q.memset, "tensor_reduce": lambda: q.tensor_reduce, "tensor_tensor_scan": lambda: q.tensor_tensor_scan,
                "transpose": lambda: q.transpose, "activation": lambda: q.activation, "matmul": lambda: q.matmul, "iota": lambda: q.iota,
                "affine_select": lambda: q.affine_select, "dma_start": lambda: q.dma_start, "remote_dma_fused": lambda: q.remote_dma_fused}[o["fn"]]()
        ins = call(*o["a"], **o["k"])
        for a in o.get("more", []): ins = call(*a)
        if o["kind"] == "d":
            s = T.sem[DMAS[nd]]; nd += 1; ins.then_inc(s, 16); o["at"] = (s, 16)
            if not o.get("sig"): tail.append(o["at"])
        elif o["kind"] == "c" and o.get("sig"):
            cnt[o["q"]] += 1; s = T.sem["q" + o["q"]]; ins.then_inc(s, 1); o["at"] = (s, cnt[o["q"]])
    g.wait_ge(T.sem.sent, sent)
    for at in tail: g.sync.wait_ge(*at)
